import numpy as np, ml_dtypes
CORES = [3,11,19,27,35,43,51,59]
N = 8
BF = ml_dtypes.bfloat16
def gentries(a):
    return np.ascontiguousarray(a.reshape(8, 16, -1).transpose(0, 2, 1)).reshape(8, -1)
def gtable(e):
    e = np.asarray(e); return np.ascontiguousarray(e.reshape(8, -1, 16).transpose(0, 2, 1)).reshape(128, -1).astype(np.int32)
W, D, L, B, K, RO, Q = 4096, 8, 512, 8, 4096, 4, 3
def join(p, c):
    return (((p * c) >> 5) + p + 37 * c) & (W - 1)
def parts(rng):
    x = rng.integers(0, 256, (N, 8, 16, W)); p = rng.integers(0, W, (N, 8, D, L)); c = rng.integers(0, W, (N, 8, D, L))
    c = np.where(rng.random(c.shape) < 0.0625, p, c); s = rng.integers(1, 65, (N, 8, 1, L))
    n = (rng.integers(0, 256, (N, 8, 16, L)) * s * s) >> 12
    return x, p, c, n, rng.integers(0, 64, (N, 8, 16)), rng.integers(1100, 1800, (N, 8))
def pack(x, p, c, n, w, t):
    return {"lit": np.ascontiguousarray(x.reshape(N, 128, W)).astype(np.float32).astype(BF), "pn": np.stack([gtable(a) for a in p.reshape(N, 8, K)]), "cn": np.stack([gtable(a) for a in c.reshape(N, 8, K)]),
            "neg": np.ascontiguousarray(n.reshape(N, 128, L)).astype(np.float32).astype(BF), "wt": w.reshape(N, 128, 1).astype(np.int32), "th": t.reshape(N, 8, 1).astype(np.int32)}
def pat(rng, m):
    return ((np.arange(16)[:, None] * (2 * rng.integers(0, 8, m.shape) + 1) + rng.integers(0, 16, m.shape)) & 15) < m
def setup_inputs(rng):
    return pack(*parts(rng))
def setup_inputs_spread(rng):
    x, p, c, n, w, t = parts(rng)
    x = rng.integers(0, 256, x.shape) >> rng.integers(0, 8, (N, 8, 1, W)); n = rng.integers(0, 256, n.shape) >> rng.integers(0, 8, (N, 8, 1, L))
    p = np.minimum((W * rng.random(p.shape) ** 3).astype(np.int64), W - 1); c = np.minimum((W * rng.random(c.shape) ** 2).astype(np.int64), W - 1)
    w = w >> rng.integers(0, 6, w.shape); t = np.minimum(np.exp2(12 * rng.random((N, 8))).astype(np.int64), 4080)
    return pack(x, p, c, n, w, t)
def setup_inputs_ends(rng):
    cho = np.array([0, 1, 7, 8, 9, 10, 15, 16])
    x = 255 * pat(rng, rng.choice(cho, (N, 8, 1, W))); n = 255 * pat(rng, rng.choice(cho, (N, 8, 1, L)))
    p = (W - 1) * rng.integers(0, 2, (N, 8, D, L)); c = (W - 1) * rng.integers(0, 2, (N, 8, D, L))
    w = 63 * rng.integers(0, 2, (N, 8, 16)); w[:, 0] = 0; w[:, 7] = 63
    t = 4080 * ((np.arange(8)[None, :] + np.arange(N)[:, None] + N + 1) & 1)
    x[:, 1::2, :, 0] = 0; x[:, 1::2, :, W - 1] = 255; x[:, 2, :, 0] = 255; x[:, 2, :, W - 1] = 0
    x[:, 7, :, int(join(W - 1, W - 1))] = 255
    for i in (0, 1, L - 1): p[:, 7, :, i] = W - 1; c[:, 7, :, i] = W - 1; n[:, 7, :, i] = 255
    for i in (2, L - 2): p[:, 7, :, i] = W - 1; c[:, 7, :, i] = 0; n[:, 7, :, i] = 255
    return pack(x, p, c, n, w, t)
def setup_inputs_corners(rng):
    x, p, c, n, w, t = parts(rng)
    a = np.arange(W // 2); a = a[join(a, a) >= W // 2]; m = len(a) // 6; F = np.ascontiguousarray(a[:6 * m].reshape(m, 6).T)
    o = np.argsort(rng.random((N, 8, 16)), axis=-1)[..., None]; sh = (N, 8, 16, m); u = rng.random(sh)
    low = [u < 0, (o < 7) & (u < 2), (o < 7) & (u < 0.3), (o == rng.integers(7, 16, (N, 8, 1, m))), (o < 8) | (u < 0.3), u < 0.25]
    for f in range(6):
        hi = 100 + rng.integers(0, 156, sh) * rng.integers(0, 2, sh); lo = 99 - rng.integers(0, 100, sh) * rng.integers(0, 2, sh)
        x[..., F[f]] = np.where(low[f], lo, hi)
    x[..., W // 2:] = rng.integers(100, 256, (N, 8, 16, W - W // 2))
    ty = rng.integers(0, 6, (N, 8, 1, L)); j = np.arange(D)[None, None, :, None]; pl = rng.integers(0, D - 1, (N, 8, 1, L))
    fam = 2 * rng.integers(0, 2, (N, 8, D, L))
    fam = np.where((ty == 0) & (j == 0), 4, fam); fam = np.where(ty == 1, 0, fam)
    fam = np.where(((ty == 2) | (ty == 3)) & (j == pl), 1, fam); fam = np.where((ty == 2) & (j == D - 1), 3, fam)
    fam = np.where(ty == 4, 5, fam); fam = np.where(ty == 5, rng.integers(0, 4, fam.shape), fam)
    free = rng.random((N, 8, 1, L)) < 0.125
    p = F[fam, rng.integers(0, m, fam.shape)]; c = np.where(free, c, p); n = np.where(free, n, 100)
    w[:, 0] = 0; w[:, 1] = 63; w[:, 2::2] = 63 * rng.integers(0, 2, (N, 3, 16))
    t = rng.choice(np.array([0, 63, 1365, 4080]), (N, 8)); t[:, 3] = 0; t[:, 5] = 4080
    return pack(x, p, c, n, w, t)
def setup_inputs_ties(rng):
    x, p, c, n, w, t = parts(rng); h = W // 2
    t = rng.integers(200, 1600, (N, 8)); t[:, 3] = rng.choice(np.array([2048, 2051, 3000, 3001, 3003, 4016, 4063, 4064]), N); t[:, 5] = rng.integers(2048, 4079, N); t[:, 7] = 4079
    tot = t[..., None, None] + rng.integers(-1, 2, (N, 8, 1, h))
    d = (tot >> 4) + (np.arange(16)[:, None] < (tot & 15))
    u = np.minimum(rng.integers(0, 12, (N, 8, 8, h)), np.minimum(255 - d[:, :, 0::2], d[:, :, 1::2]))
    d[:, :, 0::2] += u; d[:, :, 1::2] -= u
    lo = (np.minimum(144, 256 - d) * rng.random(d.shape)).astype(np.int64); hi = lo + d; sg = rng.random(lo.shape) < 0.5
    x[..., 0::2] = np.where(sg, hi, lo); x[..., 1::2] = np.where(sg, lo, hi)
    free = rng.random((N, 8, 1, L)) < 0.125; a = 2 * rng.integers(0, h, (N, 8, D, L)); b = rng.integers(0, 2, (N, 8, D, L))
    p = np.where(free, p, a + b); c = np.where(free, c, a + 1 - b)
    v = np.full((N, 8, 16, L), 255)
    for k in range(2):
        e = [np.take_along_axis(x, i[:, :, None, :], 3) for i in (p[:, :, k], c[:, :, k], join(p[:, :, k], c[:, :, k]))]
        v = np.minimum(v, np.minimum(np.maximum(e[0], e[1]), e[2]))
    n = np.where(free, n, np.minimum(v + (rng.random(v.shape) < 0.3), 255))
    return pack(x, p, c, n, w, t)
def setup_inputs_crowd(rng):
    x, p, c, n, w, t = parts(rng); x = np.minimum(x, 254); top = np.array([7, 7, 7, 7, 3, 3, 3, 3])
    calm = np.where(pat(rng, np.full((N, 8, 1, L), 9)), 0, rng.integers(1, 256, n.shape))
    for q in range(N):
        for g in range(8):
            i = int(rng.integers(0, L)); col = rng.integers(0, W, 4)
            if g % 4 == 0: p[q, g] = col[0]; c[q, g] = col[1]
            if g % 4 == 1:
                own = p[q, g, :, i].copy(); p[q, g] = col[0]; p[q, g, :, i] = own
            if g % 4 == 2: p[q, g] = col[rng.integers(0, 4, (D, L))]; c[q, g] = col[rng.integers(0, 4, (D, L))]
        k = (3 - q) % 4; n[q] = calm[q] if k < 2 else 255
        g, i = int(rng.integers(0, 8)), int(rng.integers(0, L))
        if k == 1:
            x[q] = x[q] & top[:, None, None]; n[q] = np.minimum(n[q], top[:, None, None]); t[q] = np.maximum(16 * top - 63, 0)
            n[q, g, :, i] = top[g] + 1
        if k == 2: x[q] = 127 + (x[q] >> 1)
        if k == 3: n[q, g, :, i] = calm[q, g, :, i]
    c[:, :, 0] = p[:, :, 0]
    return pack(x, p, c, n, w, t)
def check_inputs(d):
    bad = []
    for k, lo, hi in (("lit", 0, 255), ("pn", 0, W - 1), ("cn", 0, W - 1), ("neg", 0, 255), ("wt", 0, 63), ("th", 0, 4080)):
        v = np.asarray(d[k]).astype(np.float64)
        if not np.all((v >= lo) & (v <= hi)): bad.append("range of " + k)
        elif np.any(v != np.floor(v)): bad.append("whole numbers in " + k)
    return bad
def pick(v, ix):
    return np.stack([v[g][:, ix[g]] for g in range(8)])
def reference(lit, pn, cn, neg, wt, th):
    X = lit.astype(np.float32).astype(np.int16).reshape(N, 8, 16, W); n = neg.astype(np.float32).astype(np.int16).reshape(N, 8, 16, L)
    P = np.stack([gentries(a) for a in pn]).astype(np.int64); C = np.stack([gentries(a) for a in cn]).astype(np.int64)
    w = wt.astype(np.int64).reshape(N, 8, 16, 1); lim = th.astype(np.int64).reshape(N, 8, 1); A = [0] * N
    j = np.arange(D)[None, :, None]
    for t in range(RO):
        newp, names, mins = [], [], []
        for r in range(N):
            h = join(P[r], C[r]); x, y, z = pick(X[r], P[r]), pick(X[r], C[r]), pick(X[r], h)
            ok = np.add.reduce(np.abs(x - y), axis=1, dtype=np.int64) <= lim[r] + (A[r] & 63)
            l = np.where(ok[:, None, :], np.minimum(np.maximum(x, y), z), np.int16(255)).reshape(8, 16, D, L)
            nm = np.where(ok, h, P[r]).reshape(8, D, L); fell = np.zeros((8, D, L), bool); esc = np.zeros((8, L), bool)
            for s in range(Q):
                M = np.minimum.accumulate(l, axis=2)
                blk = np.add.reduce(M >= n[r][:, :, None, :], axis=1, dtype=np.int64) < 9
                has = np.any(blk, axis=1)[:, None, :]; ks = np.argmax(blk, axis=1)[:, None, :]
                if s == 0: esc = ~has[:, 0]
                turn = has & (j <= ks); cut = has & (j > ks)
                nm = np.where(turn, np.concatenate([np.take_along_axis(nm, ks, 1), nm[:, :-1]], axis=1), nm)
                l = np.where(turn[:, None], np.concatenate([np.take_along_axis(l, ks[:, None], 2), l[:, :, :-1]], axis=2), l)
                l = np.where(cut[:, None], np.int16(255), l); fell = fell | cut
            m = np.minimum.reduce(l, axis=2)
            place = B * np.arange(L)[None, :] + (np.add.reduce(w[r] * m, axis=1) & (B - 1))
            val = (m + n[r]) >> 1
            for g in range(8): X[r, g][:, place[g]] = val[g]
            A[r] = int(np.count_nonzero(esc))
            newp.append(np.where(fell, C[r].reshape(8, D, L), nm).reshape(8, K))
            names.append(nm.reshape(8, K)); mins.append(np.where(esc[:, None, :], n[r], m))
        d = 1 + t % 3
        P = np.stack(newp); C = np.stack([names[(r - d) % N] for r in range(N)]); n = np.stack([mins[(r - d) % N] for r in range(N)])
    yx = X.reshape(N, 128, W).astype(np.float32).astype(BF)
    return {"yp": np.stack([gtable(a) for a in P]).astype(np.float32), "yc": np.stack([gtable(a) for a in C]).astype(np.float32), "yn": n.reshape(N, 128, L).astype(np.float32).astype(BF), "yx": yx}

@@ -1,0 +1,483 @@
+from concourse.mybir import dt, AluOpType as A, ActivationFunctionType as F, AxisListType as AX
+
+NH = 1
+NB = 32 // NH
+NL = 16 * NB
+RO = 4
+ROUTE = ()
+LATE = (3,)
+ORDER = "d0 m0 x1 y1 l0 d1 m1 e0 x2 y2 l1 d2 m2 x3 y3 z0 v0 e1 v1 l2 d3 m3 e2 h0 v2 l3 e3 s0 s1 s2 v3 n0 s3"
+SC = 2.0 ** 40
+BIG = 2.0 ** 60
+MAGIC = 12582912.0
+bf, f32, i32, u16 = "bfloat16", "float32", "int32", "uint16"
+SCRATCH = {
+    "X": ("sbuf", [128, 4096], bf), "xg": ("sbuf", [128, 4096], bf), "yg": ("sbuf", [128, 4096], bf),
+    "mx": ("sbuf", [128, 4096], bf), "lr": ("sbuf", [128, 4096], bf),
+    "es": ("sbuf", [128, 4624], bf), "E": ("sbuf", [128, 4608], bf), "V": ("sbuf", [128, 4608], bf),
+    "cR": ("sbuf", [128, 1152], bf), "cC": ("sbuf", [128, 1152], bf),
+    "pin": ("sbuf", [128, 256], i32), "cin": ("sbuf", [128, 256], i32), "nin": ("sbuf", [128, 512], bf),
+    "win": ("sbuf", [128, 1], i32), "tin": ("sbuf", [128, 8], i32), "tbc": ("sbuf", [128, 8], i32),
+    "Pn": ("sbuf", [128, 32, 8], f32), "Nn": ("sbuf", [128, 32, 8], f32), "rp": ("sbuf", [128, 32, 8], f32),
+    "hs": ("sbuf", [128, 32, 8], i32), "hi": ("sbuf", [128, 32, 8], i32), "dr": ("sbuf", [128, 32, 8], f32),
+    "acc": ("sbuf", [128, 32, 8], f32), "sm": ("sbuf", [128, 256], f32), "keep": ("sbuf", [128, 256], f32),
+    "poff": ("sbuf", [128, 256], u16), "coff": ("sbuf", [128, 256], u16), "hoff": ("sbuf", [128, 256], u16),
+    "hp": ("sbuf", [128, 256], f32), "LH": ("sbuf", [128, 32, 2, 16], bf), "Ti": ("sbuf", [128, 64], i32),
+    "v2": ("sbuf", [128, 512], bf), "v2c": ("sbuf", [128, 512], bf), "v3": ("sbuf", [128, 512], bf), "v3c": ("sbuf", [128, 512], bf),
+    "g1": ("sbuf", [128, 512], bf), "g2": ("sbuf", [128, 512], bf), "g3": ("sbuf", [128, 512], bf),
+    "val": ("sbuf", [128, 512], bf), "vf": ("sbuf", [128, 512], f32), "N4": ("sbuf", [128, 512], bf),
+    "ne": ("sbuf", [128, 32], bf), "o2f": ("sbuf", [128, 32], f32), "o2g": ("sbuf", [128, 32], f32),
+    "si": ("sbuf", [128, 32], i32), "sj": ("sbuf", [128, 32], i32), "sk": ("sbuf", [128, 32], f32),
+    "base": ("sbuf", [128, 32], f32), "lane8": ("sbuf", [128, 32], f32), "lb": ("sbuf", [128, 32], bf), "junk": ("sbuf", [128, 32], f32),
+    "col": ("sbuf", [128, 16], f32), "coli": ("sbuf", [128, 4], i32), "wb": ("sbuf", [128, 2], bf), "cnt": ("sbuf", [128, 2], f32),
+    "thr": ("sbuf", [128, 1], f32), "G": ("sbuf", [128, 8], f32), "G0": ("sbuf", [128, 8], f32), "b16": ("sbuf", [128, 32], f32),
+    "Ip": ("sbuf", [128, 128], bf), "ad": ("sbuf", [128, 4096], bf),
+    "ones": ("sbuf", [128, 128], bf), "BO": ("sbuf", [128, 128], bf), "BO0": ("sbuf", [128, 128], bf), "I": ("sbuf", [128, 128], bf),
+    "Isc": ("sbuf", [128, 128], bf), "In": ("sbuf", [128, 128], bf), "Ih": ("sbuf", [128, 128], bf), "Im": ("sbuf", [128, 128], bf),
+    "Fm": ("sbuf", [128, 1024], bf), "ok2": ("sbuf", [128, 256, 2], bf), "Z": ("sbuf", [128, 144], bf), "Zh": ("sbuf", [128, 144], bf), "Zw": ("sbuf", [128, 144], bf),
+    "Zs": ("sbuf", [128, 144], bf), "oan": ("sbuf", [128, 32], f32), "c25": ("sbuf", [128, 512], bf), "Yp": ("sbuf", [128, 256], f32), "Yc": ("sbuf", [128, 256], f32),
+    "pe0": ("psum", [128, 8, 8, 16], f32), "pe1": ("psum", [128, 8, 8, 16], f32),
+    "pD0": ("psum", [128, 64, 8], f32), "pD1": ("psum", [128, 64, 8], f32),
+    "pn1": ("psum", [128, 512], f32), "pn2": ("psum", [128, 32, 16], f32),
+}
+for _s in (1, 2, 3):
+    SCRATCH["t%d" % _s] = ("sbuf", [128, 256], i32)
+    SCRATCH["q%d" % _s] = ("sbuf", [128, 256], f32)
+    SCRATCH["d%d" % _s] = ("sbuf", [128, 256], f32)
+for _n in ("oa", "ob", "o2", "o3", "eo", "po"):
+    SCRATCH[_n] = ("sbuf", [128, 32], u16)
+for _t in range(RO + 1):
+    SCRATCH["C%d" % _t] = ("sbuf", [128, 32, 8], f32)
+for _t in range(RO):
+    SCRATCH["MN%d" % _t] = ("sbuf", [128, 1024], bf)
+    SCRATCH["Fin%d" % _t] = ("sbuf", [128, 32, 8], f32)
+    SCRATCH["ms%d" % _t] = ("sbuf", [128, 512], bf)
+DMAS = ["lp", "lc", "ln", "lw", "lt", "lx0", "lx1", "sp", "sc", "sn"] + ["sx%d" % h for h in range(2 if NH == 2 else 4)]
+SEMAPHORES = ["v", "a", "t", "p", "sent"] + DMAS + ["r%s%d%d" % (k, t, h) for k in "cn" for t in range(RO) for h in range(NH)]
+
+
+def rank_program(g, core, T, topo):
+    rank = T.rank_of(core)
+    if rank is None:
+        return
+    N = len(T.cores)
+    Q = {"v": g.vector, "a": g.scalar, "t": g.tensor, "p": g, "s": g.sync}
+    V, S, PE = g.vector, g.scalar, g.tensor
+    cnt = {"v": 0, "a": 0, "t": 0, "p": 0}
+    seen = {q: {} for q in Q}
+    lastw, readers, total = {}, {}, {}
+
+    def need(q, sem, n):
+        if seen[q].get(sem, 0) < n:
+            Q[q].wait_ge(T.sem[sem], n)
+            seen[q][sem] = n
+
+    def deps(q, rd, wr):
+        want = {}
+        for k in rd:
+            if k in lastw and not (q == "t" and lastw[k][0] == "t"):
+                s, n = lastw[k]; want[s] = max(want.get(s, 0), n)
+        for k in list(wr) + [k for k in rd if k[0] == "@"]:
+            for s, n in list(readers.get(k, {}).items()) + ([lastw[k]] if k in lastw else []):
+                if s != q:
+                    want[s] = max(want.get(s, 0), n)
+        for k in wr:
+            if q != "t" and q in readers.get(k, {}):
+                want[q] = max(want.get(q, 0), readers[k][q])
+        for s, n in want.items():
+            need(q, s, n)
+
+    def done(sem, n, rd, wr):
+        for k in rd:
+            readers.setdefault(k, {})[sem] = n
+        for k in wr:
+            lastw[k] = (sem, n); readers[k] = {}
+        total[sem] = n
+
+    def op(q, fn, rd, wr):
+        deps(q, rd, wr)
+        cnt[q] += 1
+        fn().then_inc(T.sem[q], 1)
+        done(q, cnt[q], rd, wr)
+
+    def mm(calls, rd, wr):
+        deps("t", rd, wr)
+        for a in calls[:-1]:
+            PE.matmul(*a)
+        cnt["t"] += 1
+        PE.matmul(*calls[-1]).then_inc(T.sem.t, 1)
+        done("t", cnt["t"], rd, wr)
+
+    def dma(q, sem, out, in_, rd, wr):
+        deps(q, rd, wr)
+        Q[q].dma_start(out, in_).then_inc(T.sem[sem], 16)
+        done(sem, 16, rd, wr)
+
+    def ts(o, i, s1, s2, o0, o1, rd, wr):
+        if o1 is None:
+            op("v", lambda: V.tensor_scalar(o, i, s1, None, o0), rd, wr)
+        else:
+            op("v", lambda: V.tensor_scalar(o, i, s1, s2, o0, o1), rd, wr)
+
+    def tt(o, a, b, f, rd, wr):
+        op("v", lambda: V.tensor_tensor(o, a, b, f), rd, wr)
+
+    def cp(o, i, rd, wr):
+        op("v", lambda: V.tensor_copy(o, i), rd, wr)
+
+    def fill(o, c, wr, rd=()):
+        op("v", lambda: V.memset(o, c), rd, wr)
+
+    def act(o, i, rd, wr, f=F.Identity, **k):
+        op("a", lambda: S.activation(o, i, f, **k), rd, wr)
+
+    def send(dst_ap, src_ap, sem, t, rd):
+        to = T.cores[(rank + 1 + t % 3) % N]
+        rid, pid, _ = topo.addr(to)
+        deps("p", rd, [])
+        g.remote_dma(dst_ap, src_ap, T.sem[sem], T.sem.sent, pid, rid, topo.mask(core, to))
+        total["sent"] = total.get("sent", 0) + len(topo.engines(core, to))
+
+    def arrival(sem, t, key):
+        fr = T.cores[(rank - 1 - t % 3) % N]
+        lastw[key] = (sem, len(topo.engines(fr, core))); total[sem] = lastw[key][1]
+
+    H = range(NH)
+    PNK = ["Pn%d" % h for h in H]
+    dma("s", "lp", T.pin[:], T.pn[:], [], ["pin"])
+    dma("a", "lx0", T.X[:, 0:2048], T.lit[:, 0:2048], [], ["Xa"])
+    dma("s", "lx1", T.X[:, 2048:4096], T.lit[:, 2048:4096], [], ["Xb"])
+    dma("a", "lc", T.cin[:], T.cn[:], [], ["cin"])
+    dma("s", "ln", T.nin[:], T.neg[:], [], ["nin"])
+    dma("a", "lw", T.win[:], T.wt[:], [], ["win"])
+    dma("s", "lt", T.tin[0:1, :], T.th[:], [], ["tin"])
+    XK = ["Xa", "Xb"]
+    fill(T.ones[:], 1.0, ["ones"])
+    fill(T.G0[:], 1.0, ["G0"])
+    fill(T.Fm[:], -1024.0, ["Fm"])
+    op("p", lambda: g.iota(T.coli[:, 0:1], [[0, 1]], 0, 1), [], ["coli"])
+    op("p", lambda: g.iota(T.b16[:], [[16, 32]], 0, 0, allow_small_or_imprecise_dtypes=True), [], ["b16"])
+    op("p", lambda: g.affine_select(T.I[:], T.ones[:], [[-1, 128]], A.is_equal, 0.0, 0, 1), ["ones"], ["I"])
+    op("p", lambda: g.affine_select(T.G[:], T.G0[:], [[-16, 8]], A.is_ge, 0.0, 0, 1), ["G0"], ["G"])
+    op("p", lambda: g.affine_select(T.G[:], T.G[:], [[16, 8]], A.is_ge, 0.0, 15, -1), ["G"], ["G"])
+    op("p", lambda: g.partition_broadcast(T.tbc[:], T.tin[0:1, :], 128), ["tin"], ["tbc"])
+    op("p", lambda: g.affine_select(T.Fm[:], T.Fm[:], [[-2, 8], [-16, 8], [0, 16]], A.is_ge, 0.0, 0, 1), ["Fm"], ["Fm"])
+    op("p", lambda: g.affine_select(T.Fm[:], T.Fm[:], [[2, 8], [16, 8], [0, 16]], A.is_ge, 0.0, 1, -1), ["Fm"], ["Fm"])
+    op("p", lambda: g.affine_select(T.BO0[:], T.ones[:], [[-16, 8], [0, 16]], A.is_ge, 0.0, 0, 1), ["ones"], ["BO0"])
+    op("p", lambda: g.affine_select(T.BO[:], T.BO0[:], [[16, 8], [0, 16]], A.is_ge, 0.0, 15, -1), ["BO0"], ["BO"])
+    for z in ("Z", "Zh", "Zw", "Zs"):
+        fill(T[z][:], 0.0, [z])
+    fill(T.cR[:], -BIG, ["cR"])
+    fill(T.c25[:], 0.25, ["c25"])
+    for k in range(8):
+        ts(T.Pn[:, :, k], T.pin[:, 32 * k:32 * k + 32], -2048.0, None, A.add, None, ["pin"], PNK)
+    for h in H:
+        ts(T.poff[:, 8 * NB * h:8 * NB * (h + 1)], T.Pn[:, NB * h:NB * (h + 1), :], 2048.0, None, A.add, None, PNK, ["poff%d" % h])
+    for k in range(8):
+        ts(T.C0[:, :, k], T.cin[:, 32 * k:32 * k + 32], -2048.0, None, A.add, None, ["cin"], ["C0%d" % h for h in H])
+    for nm, sc in (("Isc", 1.0 / SC), ("In", -1.0), ("Ih", 0.5 / SC), ("Ip", 0.5), ("Im", -1.0 * NL)):
+        act(T[nm][:], T.I[:], ["I"], [nm], scale=sc)
+    for h in H:
+        act(T.MN0[:, 2 * NL * h + NL:2 * NL * (h + 1)], T.nin[:, NL * h:NL * (h + 1)], ["nin"], ["n0%d" % h], scale=-1.0, bias=255.0)
+
+    def consts_head():
+        ts(T.coli[:, 3:4], T.coli[:, 0:1], 1, None, A.bitwise_and, None, ["coli"], ["aj"])
+        ts(T.col[:, 4:5], T.coli[:, 3:4], -1.0, 1.0, A.mult, A.add, ["aj"], ["par"])
+        cp(T.col[:, 5:6], T.coli[:, 3:4], ["aj"], ["par"])
+        cp(T.Z[:, 15:143:16], T.G[:], ["G", "Z"], ["Z"])
+        ts(T.Zh[:, 15:143:16], T.G[:], -0.5, None, A.mult, None, ["G", "Zh"], ["Zh"])
+        tt(T.G0[:], T.tbc[:], T.G[:], A.mult, ["tbc", "G"], ["G0"])
+        fill(T.es[:, 4608:4624], BIG, ["ez"])
+        op("v", lambda: V.tensor_reduce(T.col[:, 3:4], T.G0[:], AX.X, A.add), ["G0"], ["th"])
+        fill(T.cR[:, 0::9], BIG, ["cR"], ["cR"])
+        ts(T.thr[:], T.col[:, 3:4], 0.5, None, A.mult, None, ["th"], ["thr"])
+        for k in range(9):
+            fill(T.cC[:, k::9], 32.0 ** k, ["cC"])
+
+    def consts_tail():
+        ts(T.coli[:, 1:2], T.coli[:, 0:1], 15, None, A.bitwise_and, None, ["coli"], ["coli"])
+        fill(T.keep[:], 1.0, ["keep"])
+        cp(T.col[:, 0:1], T.coli[:, 1:2], ["coli"], ["r"])
+        for s in (1, 2, 3):
+            fill(T["d%d" % s][:], -100.0, ["d%d" % s])
+        fill(T.keep[:, 1::8], 0.0, ["keep"], ["keep"])
+        fill(T.pn2[:, :, 10], 0.0, ["@pn2"])
+        ts(T.lb[:], T.b16[:], 1.0 * NL, None, A.add, None, ["b16"], ["lb"])
+        ts(T.lane8[:], T.b16[:], T.col[:, 0:1], 8.0, A.add, A.mult, ["b16", "r"], ["lane8"])
+        ts(T.base[:], T.b16[:], T.col[:, 0:1], 9.0, A.add, A.mult, ["b16", "r"], ["base"])
+        ts(T.col[:, 1:2], T.win[:], -1.0, None, A.mult, None, ["win"], ["nw"])
+        cp(T.wb[:, 0:1], T.win[:], ["win"], ["wb"])
+        ts(T.d1[:, 0::8], T.base[:, 0:NB], 1.0, None, A.add, None, ["base", "d1"], ["d1"])
+        mm([(T.pn2[:, 0, 15:16], T.BO[:], T.wb[:, 0:1], True, True)], ["BO", "wb"], ["@pn2"])
+        cp(T.d2[:, 0::8], T.base[:, 0:NB], ["base", "d2"], ["d2"])
+        cp(T.d3[:, 1::8], T.base[:, 0:NB], ["base", "d3"], ["d3"])
+        ts(T.Zw[:, 15:143:16], T.G[:], T.col[:, 1:2], None, A.mult, None, ["G", "nw", "Zw"], ["Zw"])
+        ts(T.Zs[:, 15:143:16], T.G[:], T.col[:, 1:2], -1.0 / SC, A.mult, A.mult, ["G", "nw", "Zs"], ["Zs"])
+        ts(T.col[:, 2:3], T.pn2[:, 0, 15:16], 254.0, None, A.mult, None, ["@pn2"], ["c0"])
+
+    def pside(h):
+        b = slice(NB * h, NB * (h + 1)); k = "Pn%d" % h
+        act(T.pn1[:, 0:256], T.Pn[:, b, :], [k], ["@pn1"], bias=3232.0)
+        act(T.pn1[:, 256:512], T.Pn[:, b, :], [k], ["@pn1"], bias=2048.0)
+        act(T.rp[:, b, :], T.Pn[:, b, :], [k], ["rp%d" % h], scale=2080.0, bias=-3801088.0)
+
+    def coffs(t, h):
+        ts(T.coff[:, 8 * NB * h:8 * NB * (h + 1)], T["C%d" % t][:, NB * h:NB * (h + 1), :], 2048.0, None, A.add, None, ["C%d%d" % (t, h)], ["coff%d" % h])
+
+    def joined(t, h):
+        b = slice(NB * h, NB * (h + 1)); b2 = slice(32 + NB * h, 32 + NB * (h + 1)); s = str(h)
+        tt(T.pn1[:, 0:256], T.pn1[:, 0:256], T["C%d" % t][:, b, :], A.mult, ["@pn1", "C%d%d" % (t, h)], ["@pn1"])
+        tt(T.hs[:, b, :], T.pn1[:, 0:256], T.rp[:, b, :], A.add, ["@pn1", "rp" + s], ["hs" + s])
+        ts(T.hi[:, b, :], T.hs[:, b, :], 5, 4095, A.arith_shift_right, A.bitwise_and, ["hs" + s], ["hi" + s])
+        cp(T.hoff[:, 8 * NB * h:8 * NB * (h + 1)], T.hi[:, b, :], ["hi" + s], ["hoff" + s])
+
+    def apart(c):
+        tt(T.hp[:], T.hi[:], T.pn1[:, 256:512], A.subtract, ["hi0", "@pn1"], ["hp"])
+
+    def limit(t):
+        if t > 0:
+            ts(T.coli[:, 2:3], T.cnt[:, 0:1], 4096.0, None, A.add, None, ["cnt0"], ["ai"])
+            ts(T.coli[:, 3:4], T.coli[:, 2:3], 63, None, A.bitwise_and, None, ["ai"], ["aj"])
+            ts(T.thr[:], T.coli[:, 3:4], T.col[:, 3:4], 0.5, A.add, A.mult, ["aj", "th"], ["thr"])
+
+    def nap(t, l0, n):
+        h = l0 // NL; o = 2 * NL * h + NL + l0 - NL * h
+        return T["MN%d" % t][:, o:o + n]
+
+    def gx(c):
+        e = slice(1024 * c, 1024 * c + 1024); o = slice(64 * c, 64 * c + 64); h = str(8 * c // NB); s = str(c)
+        act(T.xg[:, e], T.X[:].indirect(T.poff[:, o]), XK + ["poff" + h], ["x" + s])
+
+    def gy(c):
+        e = slice(1024 * c, 1024 * c + 1024); o = slice(64 * c, 64 * c + 64); h = str(8 * c // NB); s = str(c)
+        act(T.yg[:, e], T.X[:].indirect(T.coff[:, o]), XK + ["coff" + h], ["y" + s])
+
+    def gmx(c, early=False):
+        if early and c in ROUTE:
+            return
+        e = slice(1024 * c, 1024 * c + 1024); o = slice(64 * c, 64 * c + 64); h = str(8 * c // NB); s = str(c)
+        pD = T["pD%d" % (c % 2)]; k = "@pD%d" % (c % 2)
+        part = lambda z, src, first, last: [(pD[:, 0:8, :], T[z][:, 15 - r:143 - r], src[:, 1024 * c + r:1024 * c + 1024:16], first and r == 0, last and r == 15) for r in range(16)]
+        if c in ROUTE:
+            pe = T["pe%d" % (c % 2)]; ks = ["@pe%d0" % (c % 2), "@pe%d1" % (c % 2)]
+            hv = lambda src, u: src[:, 1024 * c + 512 * u:1024 * c + 512 * u + 512]
+            for u in range(2):
+                mm([(pe[:, 4 * u:4 * u + 4], T.I[:], hv(T.xg, u), True, False), (pe[:, 4 * u:4 * u + 4], T.In[:], hv(T.yg, u), False, True)], ["I", "In", "x" + s, "y" + s], [ks[u]])
+                act(hv(T.ad, u), pe[:, 4 * u:4 * u + 4], [ks[u]], ["ad%s%d" % (s, u)], F.Abs, scale=0.5)
+            for u in range(2):
+                mm([(pe[:, 4 * u:4 * u + 4], T.Ip[:], hv(T.xg, u), True, False), (pe[:, 4 * u:4 * u + 4], T.Ip[:], hv(T.yg, u), False, False),
+                    (pe[:, 4 * u:4 * u + 4], T.I[:], hv(T.ad, u), False, True)], ["Ip", "ad%s%d" % (s, u)], [ks[u]])
+                act(hv(T.mx, u), pe[:, 4 * u:4 * u + 4], [ks[u]], ["mx" + s])
+            mm(part("Z", T.ad, True, True), ["Z", "ad%s0" % s, "ad%s1" % s], [k])
+            return
+        ylast = c in LATE
+        if early:
+            mm(part("Zh", T.xg, True, False), ["Zh", "x" + s], [k])
+            if not ylast:
+                mm(part("Zh", T.yg, False, False), ["y" + s], [k])
+            return
+        tt(T.mx[:, e], T.X[:].indirect(T.coff[:, o]), T.xg[:, e], A.max, XK + ["coff" + h, "x" + s], ["mx" + s])
+        if ylast:
+            mm(part("Zh", T.yg, False, False), ["y" + s], [k])
+        mm(part("Z", T.mx, False, True), ["Z", "mx" + s], [k])
+
+    def glr(t, c):
+        e = slice(1024 * c, 1024 * c + 1024); o = slice(64 * c, 64 * c + 64); h = str(8 * c // NB); s = str(c)
+        late = c in LATE
+        pe = T["pe%d" % (c % 2)]
+        gather = lambda: tt(T.lr[:, e], T.X[:].indirect(T.hoff[:, o]), T.mx[:, e], A.min, XK + ["hoff" + h, "mx" + s], ["lr" + s])
+        if not late:
+            gather()
+        for u in range(2):
+            ts(T.ok2[:, o, u], T["pD%d" % (c % 2)][:, 0:8, :], T.thr[:], T.col[:, 4 + u:5 + u], A.is_le, A.mult, ["@pD%d" % (c % 2), "thr", "par"], ["ok2" + s])
+        if late:
+            gather()
+
+    def esum(t, c):
+        h = str(8 * c // NB); s = str(c); late = c in LATE
+        pe = T["pe%d" % (c % 2)]
+        lit = lambda u, first: [(pe[:, 4 * u:4 * u + 4], T.I[:], T.lr[:, 1024 * c + 512 * u:1024 * c + 512 * u + 512], first, not first)]
+        for u in range(2):
+            bk = slice(4 * u, 4 * u + 4); k = "@pe%d%d" % (c % 2, u)
+            mm(([(pe[:, bk], T.I[:], T.c25[:], True, False)] if late else lit(u, True)) +
+               [(pe[:, bk, j, :], T.I[:], nap(t, 128 * c + 64 * u, 64), False, False) for j in range(8)], ["I", "c25" if late else "lr" + s, "n%d%s" % (t, h)], [k])
+        for u in range(2):
+            bk = slice(4 * u, 4 * u + 4); k = "@pe%d%d" % (c % 2, u)
+            mm([(pe[:, bk, :, 2 * r:2 * r + 2], T.Fm[:, 128 * r:128 * r + 128], T.ok2[:, 64 * c + 32 * u:64 * c + 32 * u + 32, :], False, r == 7 and not late) for r in range(8)], ["Fm", "ok2" + s], [k])
+        for u in range(2 if late else 0):
+            mm(lit(u, False), ["lr" + s], ["@pe%d%d" % (c % 2, u)])
+
+    def evac(c):
+        pe = T["pe%d" % (c % 2)]
+        for j in range(8):
+            act(T.es[:, 1152 * c + 1 + j:1152 * c + 1152:9], pe[:, :, j, :], ["@pe%d0" % (c % 2), "@pe%d1" % (c % 2)], ["es%d" % c], scale=SC, bias=(769.75 if c in LATE else 770.0) * SC)
+
+    def scans(c):
+        e = slice(1152 * c, 1152 * c + 1152); s = str(c)
+        op("v", lambda: V.tensor_tensor_scan(T.E[:, e], T.cR[:], T.es[:, e], 0.0, A.max, A.min), ["cR", "ez", "es" + s], ["E" + s])
+        op("v", lambda: V.tensor_tensor_scan(T.V[:, e], T.E[:, e], T.cC[:], 1.0, A.max, A.min), ["cC", "E" + s], ["V" + s])
+
+    def tail(t, h):
+        s = str(h); b = slice(NB * h, NB * (h + 1)); b2 = slice(32 + NB * h, 32 + NB * (h + 1)); L = slice(NL * h, NL * (h + 1))
+        cs = range(4 * h // NH, 4 * (h + 1) // NH)
+        ES, EK, VK, OK = (["%s%d" % (k, c) for c in cs] for k in ("es", "E", "V", "ok2"))
+        ES = ES + ["ez"]
+        esw = T.es[:, 9 * NL * h:9 * NL * (h + 1) + 1]; Ew = T.E[:, 9 * NL * h:9 * NL * (h + 1)]; v1 = T.V[:, 9 * NL * h + 8:9 * NL * (h + 1):9]
+        pD = T["pD%d" % h]; kD = "@pD%d" % h; pe = T["pe%d" % h]; kM, kV = "@pe%d0" % h, "@pe%d1" % h
+        Ti = T.Ti[:, 2 * NB * h:2 * NB * (h + 1)]; w = NB // 8
+        C = T["C%d" % t]; Fin = T["Fin%d" % t]; MN = T["MN%d" % t]; kn = "n%d%d" % (t, h); kC = "C%d%d" % (t, h)
+        Mp = MN[:, 2 * NL * h:2 * NL * h + NL]; npr = nap(t, NL * h, NL)
+
+        def count(n, v, keys):
+            u = 32.0 ** (1 - n)
+            ts(T.LH[:, b, 0, :], v, u, u * 2.0 ** 20, A.max, A.min, keys, ["LHa" + s])
+            act(T.LH[:, b, 1, :], v, keys, ["LHb" + s], F.Relu, scale=2.0 ** -20, bias=-u)
+            mm([(pD[:, 0:2 * w, :], T.Z[:, 15 - r:143 - r], T.LH[:, b, :, r], r == 0, r == 15) for r in range(16)], ["LHa" + s, "LHb" + s, "Z"], [kD])
+
+        def decode(n):
+            tn = T["t%d" % n]; k = "t%d%s" % (n, s)
+            ts(Ti, pD[:, 0:2 * w, :], 32.0 ** (n - 1) / 31, 7 * 33825 - 8.0 / 31, A.mult, A.add, [kD], ["Ti" + s])
+            for j in range(4):
+                if n == 3 and j == 3:
+                    ts(tn[:, 3::8], T.Ti[:, 0:64:2], 19, 1, A.logical_shift_right, A.bitwise_and, ["Ti" + s], [k])
+                else:
+                    ts(tn[:, j::4], Ti, 4 + 5 * j, 1, A.logical_shift_right, A.bitwise_and, ["Ti" + s], [k])
+            op("v", lambda: V.tensor_tensor_scan(T["q%d" % n][:], T["d%d" % n][:], tn[:], -8.0, A.max, A.add), [k, "d%d" % n], ["q%d%s" % (n, s)])
+
+        def turn(n, out, src, ko, ks):
+            tt(T.pn1[:, 1:257], T["t%d" % n][:], T.pn2[:, b, 4 - n:12 - n], A.mult, ["t%d%s" % (n, s), "@pn2", "@pn1"], ["@pn1"])
+            op("v", lambda: V.tensor_tensor_scan(T.sm[:], T.keep[:], T.pn1[:, 0:256], 0.0, A.mult, A.subtract), ["keep", "@pn1"], ["sm" + s])
+            cp(T.pn1[:, 0:256:8], T.sm[:, 7::8], ["sm" + s], ["@pn1"])
+            if n < 3:
+                cp(T.pn2[:, b, 3 - n], T.sm[:, 7::8], ["sm" + s], ["@pn2"])
+            tt(out, src, T.pn1[:, 0:256], A.add, [ks, "@pn1"], [ko])
+
+        mm([(T.pD0[:, 32:64, :], T.I[:], T.ok2[:, :, u], u == 0, u == 1) for u in range(2)], OK, ["@pD0"])
+        tt(T.pn1[:, 256:512], T.pD0[:, 32:64, :], T.hp[:], A.mult, ["@pD0", "hp"], ["@pn1"])
+        tt(T.Nn[:, b, :], T.Pn[:, b, :], T.pn1[:, 256:512], A.add, ["Pn" + s, "@pn1"], ["Nn" + s])
+        yield
+        count(1, v1, VK)
+        ts(T.v3c[:, L], v1, 2.0 ** 30, None, A.min, None, VK, ["v1c" + s])
+        tt(T.dr[:, b, 0:7], T.Nn[:, b, 0:7], T.Nn[:, b, 1:8], A.subtract, ["Nn" + s], ["dr" + s])
+        act(T.pn1[:, 256:512], C[:, b, :], [kC], ["@pn1"])
+        yield
+        decode(1)
+        cp(T.oa[:, b], T.q1[:, 7::8], ["q1" + s], ["oa" + s])
+        ts(T.ne[:, b], T.t1[:, 7::8], -1.0, 1.0, A.mult, A.add, ["t1" + s], ["ne" + s])
+        tt(T.v2[:, L], esw.indirect(T.oa[:, b]), T.v3c[:, L], A.min, ES + ["v1c" + s, "oa" + s], ["v2" + s])
+        pX, kX = (T.pD1, "@pD1") if NH == 1 else (pD, kD)
+        mm([(pX[:, 32:32 + NB, j], T.I[:], T.ne[:, b], True, True) for j in range(7)] +
+           [(pX[:, 8:8 + w, :], T.ones[:], T.ne[:, b], True, True),
+            (pX[:, 12:12 + w, :], T.Im[:], T.ne[:, b], True, False), (pX[:, 12:12 + w, :], T.I[:], T.lb[:, 0:NB], False, True)], ["ne" + s, "I", "Im", "lb", "ones"], [kX])
+        count(2, T.v2[:, L], ["v2" + s])
+        ts(T.v2c[:, L], T.v2[:, L], 2.0 ** -5, None, A.max, None, ["v2" + s], ["v2c" + s])
+        tt(T.oan[:, b], T.q1[:, 7::8], T.ne[:, b], A.mult, ["q1" + s, "ne" + s], ["oan" + s])
+        tt(T.pn2[:, b, 3:10], pX[:, 32:32 + NB, 0:7], T.dr[:, b, 0:7], A.mult, [kX, "dr" + s], ["@pn2"])
+        ts(T.eo[:, b], pX[:, 12:12 + w, :], T.col[:, 0:1], None, A.add, None, [kX, "r"], ["eo" + s])
+        if t < RO - 1:
+            act(T.junk[:, b], pX[:, 8:8 + w, :], [kX], ["cnt" + s], scale=-1.0, accum_out=T.cnt[:, h:h + 1])
+        ts(T.t3[:, 7::8], T.t1[:, 7::8], 2.0, None, A.mult, None, ["t1" + s], ["t3" + s])
+        turn(1, T.acc[:, b, :], T.Nn[:, b, :], "acc" + s, "Nn" + s)
+        yield
+        decode(2)
+        cp(T.ob[:, b], T.q2[:, 7::8], ["q2" + s], ["ob" + s])
+        tt(T.v3[:, L], esw.indirect(T.ob[:, b]), T.v2c[:, L], A.min, ES + ["v2c" + s, "ob" + s], ["v3" + s])
+        act(T.g1[:, L], esw.indirect(T.ob[:, b]), ES + ["ob" + s], ["g1" + s])
+        count(3, T.v3[:, L], ["v3" + s])
+        turn(2, T.acc[:, b, :], T.acc[:, b, :], "acc" + s, "acc" + s)
+        yield
+        decode(3)
+        n0 = 2 * NL * h + NL
+        mm([(pe[:, 4:4 + w], T.I[:], T.c25[:, 0:NL], True, False), (pe[:, 4:4 + w], T.In[:], npr, False, False)], ["In", "c25", kn], [kV])
+        mm([(pe[:, 0:w], T.In[:], npr, True, False)], [kn], [kM])
+        mm([(pD[:, 16:16 + w, :], T.Zw[:, 15 - r:143 - r], MN[:, n0 + r:n0 + NL:16], r == 0, False) for r in range(16)], ["Zw", kn], [kD])
+        tt(T.o2f[:, b], T.oan[:, b], T.t3[:, 0::8], A.mult, ["oan" + s, "t3" + s], ["o2f" + s])
+        tt(T.t3[:, 0::8], T.t3[:, 0::8], T.t2[:, 0::8], A.mult, ["t3" + s, "t2" + s], ["t3" + s])
+        cp(T.o3[:, b], T.q3[:, 7::8], ["q3" + s], ["o3" + s])
+        tt(T.o2g[:, b], T.o2f[:, b], T.base[:, 0:NB], A.max, ["o2f" + s, "base"], ["o2g" + s])
+        turn(3, Fin[:, b, :], T.acc[:, b, :], "Fin" + s, "acc" + s)
+        send(T["C%d" % (t + 1)][:, b, :], Fin[:, b, :], "rc%d%d" % (t, h), t, ["Fin" + s])
+        arrival("rc%d%d" % (t, h), t, "C%d%d" % (t + 1, h))
+        cp(T.o2[:, b], T.o2g[:, b], ["o2g" + s], ["o2" + s])
+        tt(T.g2[:, L], Ew.indirect(T.o3[:, b]), T.g1[:, L], A.min, EK + ["o3" + s, "g1" + s], ["g2" + s])
+        tt(T.g3[:, L], esw.indirect(T.o2[:, b]), T.g2[:, L], A.min, ES + ["o2" + s, "g2" + s], ["g3" + s])
+        mm([(pe[:, 4:4 + w], T.Ih[:], T.g3[:, L], False, True)], ["Ih", "g3" + s], [kV])
+        mm([(pD[:, 16:16 + w, :], T.Zs[:, 15 - r:143 - r], T.g3[:, NL * h + r:NL * (h + 1):16], False, r == 15) for r in range(16)], ["Zs", "g3" + s], [kD])
+        mm([(pe[:, 0:w], T.Isc[:], T.g3[:, L], False, True)], ["Isc", "g3" + s], [kM])
+        def values():
+            act(T.vf[:, L], pe[:, 4:4 + w], [kV], ["vf" + s], bias=MAGIC + 254.0)
+            act(T.val[:, L], T.vf[:, L], ["vf" + s], ["val" + s], bias=-MAGIC)
+        if t < RO - 1:
+            values()
+        act(Mp, pe[:, 0:w], [kM], ["Mp" + s], scale=-1.0, bias=1.0)
+        mw = MN[:, 2 * NL * h:2 * NL * (h + 1)].indirect(T.eo[:, b])
+        if t < RO - 1:
+            act(T["ms%d" % t][:, L], mw, ["Mp" + s, kn, "eo" + s], ["ms" + s])
+            send(nap(t + 1, NL * h, NL), T["ms%d" % t][:, L], "rn%d%d" % (t, h), t, ["ms" + s])
+        else:
+            act(T["ms%d" % t][:, L], mw, ["Mp" + s, kn, "eo" + s], ["ms" + s], scale=-1.0, bias=255.0)
+            send(T.N4[:, L], T["ms%d" % t][:, L], "rn%d%d" % (t, h), t, ["ms" + s])
+            values()
+        arrival("rn%d%d" % (t, h), t, "n%d%d" % (t + 1, h))
+        yield
+        tt(T.pn1[:, 256:512], Fin[:, b, :], T.pn1[:, 256:512], A.subtract, ["Fin" + s, "@pn1"], ["@pn1"])
+        tt(T.pn1[:, 257:512], T.t3[:, 0:255], T.pn1[:, 257:512], A.mult, ["t3" + s, "@pn1"], ["@pn1"])
+        tt(T.Pn[:, b, :], C[:, b, :], T.pn1[:, 256:512], A.add, [kC, "@pn1"], ["Pn" + s])
+        ts(T.si[:, b], pD[:, 16:16 + w, :], T.col[:, 2:3], None, A.add, None, [kD, "c0"], ["si" + s])
+        cp(T.Pn[:, b, 0], Fin[:, b, 0], ["Fin" + s, "Pn" + s], ["Pn" + s])
+        ts(T.sj[:, b], T.si[:, b], 7, None, A.bitwise_and, None, ["si" + s], ["sj" + s])
+        if t < RO - 1:
+            limit(t + 1)
+        tt(T.sk[:, b], T.sj[:, b], T.lane8[:, 0:NB], A.add, ["sj" + s, "lane8"], ["sk" + s])
+        if t < RO - 1 or NH == 2:
+            xk = XK if NH == 1 else [XK[h]]
+            cp(T.po[:, b], T.sk[:, b], ["sk" + s], ["po" + s])
+            if t < RO - 1:
+                ts(T.poff[:, 8 * NB * h:8 * NB * (h + 1)], T.Pn[:, b, :], 2048.0, None, A.add, None, ["Pn" + s], ["poff" + s])
+            cp(T.X[:, 8 * NL * h:8 * NL * (h + 1)].indirect(T.po[:, b]), T.val[:, L], ["po" + s, "val" + s], xk)
+            if t == RO - 1:
+                dma("s", "sx" + s, T.yx[:, 8 * NL * h:8 * NL * (h + 1)], T.X[:, 8 * NL * h:8 * NL * (h + 1)], xk, [])
+        else:
+            for u in range(4):
+                ts(T.po[:, 8 * u:8 * u + 8], T.sk[:, 8 * u:8 * u + 8], -1024.0 * u, None, A.add, None, ["sk0"], ["po%d" % u])
+            for u in range(4):
+                e = slice(1024 * u, 1024 * u + 1024)
+                cp(T.X[:, e].indirect(T.po[:, 8 * u:8 * u + 8]), T.val[:, 128 * u:128 * u + 128], ["po%d" % u, "val0"], ["Xq%d" % u] + (XK if u == 0 else []))
+                dma("s", "sx%d" % u, T.yx[:, e], T.X[:, e], ["Xq%d" % u], [])
+        if t < RO - 1:
+            pside(h)
+        yield
+
+    for h in H:
+        pside(h)
+    for t in range(RO):
+        gx(0)
+        coffs(t, 0)
+        gy(0)
+        joined(t, 0)
+        if t == 0:
+            consts_head()
+        rest = tail(t, 0)
+
+        def slot0(c):
+            act(T.es[:, 0:9 * NL:9], nap(t, 0, NL), ["n%d0" % t, "ez"], ["ez"], scale=SC, bias=SC)
+
+        def names(c):
+            next(rest)
+            if t == 0:
+                consts_tail()
+        step = {"x": gx, "y": gy, "d": lambda c: gmx(c, True), "m": gmx, "l": lambda c: glr(t, c), "e": lambda c: esum(t, c),
+                "v": evac, "s": scans, "z": slot0, "n": names, "h": apart}
+        for w in ORDER.split():
+            step[w[0]](int(w[1]))
+        for _ in rest:
+            pass
+    for k in range(8):
+        act(T.Yp[:, 32 * k:32 * k + 32], T.Pn[:, :, k], PNK, ["Yp"], bias=2048.0)
+    dma("a", "sp", T.yp[:], T.Yp[:], ["Yp"], [])
+    dma("s", "sn", T.yn[:], T.N4[:], ["n%d%d" % (RO, h) for h in H], [])
+    for k in range(8):
+        act(T.Yc[:, 32 * k:32 * k + 32], T["C%d" % RO][:, :, k], ["C%d%d" % (RO, h) for h in H], ["Yc"], bias=2048.0)
+    dma("a", "sc", T.yc[:], T.Yc[:], ["Yc"], [])
+    for sem, n in total.items():
+        need("p", sem, n)

@@ -20,7 +20,8 @@ SCRATCH = {
     "win": ("sbuf", [128, 1], i32), "tin": ("sbuf", [128, 8], i32), "tbc": ("sbuf", [128, 8], i32),
     "Pn": ("sbuf", [128, 32, 8], f32), "Nn": ("sbuf", [128, 32, 8], f32), "rp": ("sbuf", [128, 32, 8], f32),
     "hs": ("sbuf", [128, 32, 8], i32), "hi": ("sbuf", [128, 32, 8], i32), "dr": ("sbuf", [128, 32, 8], f32),
-    "acc": ("sbuf", [128, 32, 8], f32), "sm": ("sbuf", [128, 256], f32), "keep": ("sbuf", [128, 256], f32),
+    "tm1": ("sbuf", [128, 264], f32), "tm2": ("sbuf", [128, 264], f32), "tm3": ("sbuf", [128, 264], f32),
+    "pat": ("sbuf", [128, 64], f32), "Jp": ("sbuf", [128, 128], f32), "Jn": ("sbuf", [128, 128], f32),
     "poff": ("sbuf", [128, 256], u16), "coff": ("sbuf", [128, 256], u16), "hoff": ("sbuf", [128, 256], u16),
     "hp": ("sbuf", [128, 256], f32), "LH": ("sbuf", [128, 32, 2, 16], bf), "Ti": ("sbuf", [128, 64], i32),
     "v2": ("sbuf", [128, 512], bf), "v2c": ("sbuf", [128, 512], bf), "v3": ("sbuf", [128, 512], bf), "v3c": ("sbuf", [128, 512], bf),
@@ -177,6 +178,8 @@ def rank_program(g, core, T, topo):
         ts(T.C0[:, :, k], T.cin[:, 32 * k:32 * k + 32], -2048.0, None, A.add, None, ["cin"], ["C0%d" % h for h in H])
     for nm, sc in (("Isc", 1.0 / SC), ("In", -1.0), ("Ih", 0.5 / SC), ("Ip", 0.5), ("Im", -1.0 * NL)):
         act(T[nm][:], T.I[:], ["I"], [nm], scale=sc)
+    act(T.Jp[:], T.I[:], ["I"], ["J"])
+    act(T.Jn[:], T.I[:], ["I"], ["J"], scale=-1.0)
     for h in H:
         act(T.MN0[:, 2 * NL * h + NL:2 * NL * (h + 1)], T.nin[:, NL * h:NL * (h + 1)], ["nin"], ["n0%d" % h], scale=-1.0, bias=255.0)
 
@@ -196,11 +199,11 @@ def rank_program(g, core, T, topo):
 
     def consts_tail():
         ts(T.coli[:, 1:2], T.coli[:, 0:1], 15, None, A.bitwise_and, None, ["coli"], ["coli"])
-        fill(T.keep[:], 1.0, ["keep"])
         cp(T.col[:, 0:1], T.coli[:, 1:2], ["coli"], ["r"])
         for s in (1, 2, 3):
             fill(T["d%d" % s][:], -100.0, ["d%d" % s])
-        fill(T.keep[:, 1::8], 0.0, ["keep"], ["keep"])
+        for s in (1, 2, 3):
+            fill(T["tm%d" % s][:, 0:1], 0.0, ["tm%d" % s])
         fill(T.pn2[:, :, 10], 0.0, ["@pn2"])
         ts(T.lb[:], T.b16[:], 1.0 * NL, None, A.add, None, ["b16"], ["lb"])
         ts(T.lane8[:], T.b16[:], T.col[:, 0:1], 8.0, A.add, A.mult, ["b16", "r"], ["lane8"])
@@ -342,15 +345,24 @@ def rank_program(g, core, T, topo):
                     ts(tn[:, 3::8], T.Ti[:, 0:64:2], 19, 1, A.logical_shift_right, A.bitwise_and, ["Ti" + s], [k])
                 else:
                     ts(tn[:, j::4], Ti, 4 + 5 * j, 1, A.logical_shift_right, A.bitwise_and, ["Ti" + s], [k])
-            op("v", lambda: V.tensor_tensor_scan(T["q%d" % n][:], T["d%d" % n][:], tn[:], -8.0, A.max, A.add), [k, "d%d" % n], ["q%d%s" % (n, s)])
+            if n < 3:
+                place(n)
+
+        def place(n):
+            op("v", lambda: V.tensor_tensor_scan(T["q%d" % n][:], T["d%d" % n][:], T["t%d" % n][:], -8.0, A.max, A.add), ["t%d%s" % (n, s), "d%d" % n], ["q%d%s" % (n, s)])
 
         def turn(n, out, src, ko, ks):
-            tt(T.pn1[:, 1:257], T["t%d" % n][:], T.pn2[:, b, 4 - n:12 - n], A.mult, ["t%d%s" % (n, s), "@pn2", "@pn1"], ["@pn1"])
-            op("v", lambda: V.tensor_tensor_scan(T.sm[:], T.keep[:], T.pn1[:, 0:256], 0.0, A.mult, A.subtract), ["keep", "@pn1"], ["sm" + s])
-            cp(T.pn1[:, 0:256:8], T.sm[:, 7::8], ["sm" + s], ["@pn1"])
+            tm = T["tm%d" % n]; k = "tm%d" % n
+            tt(tm[:, 1:257], T["t%d" % n][:], T.pn2[:, b, 4 - n:12 - n], A.mult, ["t%d%s" % (n, s), "@pn2", k], [k])
             if n < 3:
-                cp(T.pn2[:, b, 3 - n], T.sm[:, 7::8], ["sm" + s], ["@pn2"])
-            tt(out, src, T.pn1[:, 0:256], A.add, [ks, "@pn1"], [ko])
+                mm([(T.pn2[:, b, 3 - n], T.Jn[:], tm[:, m:256:8], m == 1, m == 7) for m in range(1, 8)], ["J", k], ["@pn2"])
+                act(T.pat[:, 32 * n - 32:32 * n], T.pn2[:, b, 3 - n], ["@pn2"], ["pat%d" % n])
+                mm(([(T.pn1[:, 0:256], T.Jp[:], T.Nn[:], True, False)] if n == 1 else [(T.pn1[:, 0:256:8], T.Jp[:], T.pat[:, 0:32], False, False)]) +
+                   [(T.pn1[:, 0:256], T.Jp[:], tm[:, 0:256], False, False)], [k, "Nn0"] + (["pat1"] if n == 2 else []), ["@pn1"])
+            else:
+                mm([(T.pn1[:, 0:256:8], T.Jp[:], T.pat[:, 32:64], False, False)], ["pat2"], ["@pn1"])
+                mm([(T.pn1[:, 0:256:8], T.Jn[:], tm[:, m:256:8], False, False) for m in range(1, 8)] + [(T.pn1[:, 0:256], T.Jp[:], tm[:, 0:256], False, True)], [k], ["@pn1"])
+                act(out, T.pn1[:, 0:256], ["@pn1"], [ko])
 
         mm([(T.pD0[:, 32:64, :], T.I[:], T.ok2[:, :, u], u == 0, u == 1) for u in range(2)], OK, ["@pD0"])
         tt(T.pn1[:, 256:512], T.pD0[:, 32:64, :], T.hp[:], A.mult, ["@pD0", "hp"], ["@pn1"])
@@ -360,6 +372,8 @@ def rank_program(g, core, T, topo):
         ts(T.v3c[:, L], v1, 2.0 ** 30, None, A.min, None, VK, ["v1c" + s])
         tt(T.dr[:, b, 0:7], T.Nn[:, b, 0:7], T.Nn[:, b, 1:8], A.subtract, ["Nn" + s], ["dr" + s])
         act(T.pn1[:, 256:512], C[:, b, :], [kC], ["@pn1"])
+        mm([(pe[:, 4:4 + w], T.I[:], T.c25[:, 0:NL], True, False), (pe[:, 4:4 + w], T.In[:], npr, False, False)], ["In", "c25", kn], [kV])
+        mm([(pe[:, 0:w], T.In[:], npr, True, False)], [kn], [kM])
         yield
         decode(1)
         cp(T.oa[:, b], T.q1[:, 7::8], ["q1" + s], ["oa" + s])
@@ -369,40 +383,41 @@ def rank_program(g, core, T, topo):
         mm([(pX[:, 32:32 + NB, j], T.I[:], T.ne[:, b], True, True) for j in range(7)] +
            [(pX[:, 8:8 + w, :], T.ones[:], T.ne[:, b], True, True),
             (pX[:, 12:12 + w, :], T.Im[:], T.ne[:, b], True, False), (pX[:, 12:12 + w, :], T.I[:], T.lb[:, 0:NB], False, True)], ["ne" + s, "I", "Im", "lb", "ones"], [kX])
+        n0 = 2 * NL * h + NL
+        mm([(pX[:, 16:16 + w, :], T.Zw[:, 15 - r:143 - r], MN[:, n0 + r:n0 + NL:16], r == 0, False) for r in range(16)], ["Zw", kn], [kX])
         count(2, T.v2[:, L], ["v2" + s])
         ts(T.v2c[:, L], T.v2[:, L], 2.0 ** -5, None, A.max, None, ["v2" + s], ["v2c" + s])
-        tt(T.oan[:, b], T.q1[:, 7::8], T.ne[:, b], A.mult, ["q1" + s, "ne" + s], ["oan" + s])
         tt(T.pn2[:, b, 3:10], pX[:, 32:32 + NB, 0:7], T.dr[:, b, 0:7], A.mult, [kX, "dr" + s], ["@pn2"])
-        ts(T.eo[:, b], pX[:, 12:12 + w, :], T.col[:, 0:1], None, A.add, None, [kX, "r"], ["eo" + s])
         if t < RO - 1:
             act(T.junk[:, b], pX[:, 8:8 + w, :], [kX], ["cnt" + s], scale=-1.0, accum_out=T.cnt[:, h:h + 1])
-        ts(T.t3[:, 7::8], T.t1[:, 7::8], 2.0, None, A.mult, None, ["t1" + s], ["t3" + s])
-        turn(1, T.acc[:, b, :], T.Nn[:, b, :], "acc" + s, "Nn" + s)
+        turn(1, None, None, None, None)
         yield
         decode(2)
         cp(T.ob[:, b], T.q2[:, 7::8], ["q2" + s], ["ob" + s])
         tt(T.v3[:, L], esw.indirect(T.ob[:, b]), T.v2c[:, L], A.min, ES + ["v2c" + s, "ob" + s], ["v3" + s])
         act(T.g1[:, L], esw.indirect(T.ob[:, b]), ES + ["ob" + s], ["g1" + s])
         count(3, T.v3[:, L], ["v3" + s])
-        turn(2, T.acc[:, b, :], T.acc[:, b, :], "acc" + s, "acc" + s)
+        turn(2, None, None, None, None)
+        tt(T.oan[:, b], T.q1[:, 7::8], T.ne[:, b], A.mult, ["q1" + s, "ne" + s], ["oan" + s])
+        ts(T.eo[:, b], pX[:, 12:12 + w, :], T.col[:, 0:1], None, A.add, None, [kX, "r"], ["eo" + s])
+        ts(T.t3[:, 7::8], T.t1[:, 7::8], 2.0, None, A.mult, None, ["t1" + s], ["t3" + s])
+        if t < RO - 1:
+            limit(t + 1)
         yield
         decode(3)
-        n0 = 2 * NL * h + NL
-        mm([(pe[:, 4:4 + w], T.I[:], T.c25[:, 0:NL], True, False), (pe[:, 4:4 + w], T.In[:], npr, False, False)], ["In", "c25", kn], [kV])
-        mm([(pe[:, 0:w], T.In[:], npr, True, False)], [kn], [kM])
-        mm([(pD[:, 16:16 + w, :], T.Zw[:, 15 - r:143 - r], MN[:, n0 + r:n0 + NL:16], r == 0, False) for r in range(16)], ["Zw", kn], [kD])
         tt(T.o2f[:, b], T.oan[:, b], T.t3[:, 0::8], A.mult, ["oan" + s, "t3" + s], ["o2f" + s])
         tt(T.t3[:, 0::8], T.t3[:, 0::8], T.t2[:, 0::8], A.mult, ["t3" + s, "t2" + s], ["t3" + s])
-        cp(T.o3[:, b], T.q3[:, 7::8], ["q3" + s], ["o3" + s])
         tt(T.o2g[:, b], T.o2f[:, b], T.base[:, 0:NB], A.max, ["o2f" + s, "base"], ["o2g" + s])
-        turn(3, Fin[:, b, :], T.acc[:, b, :], "Fin" + s, "acc" + s)
+        turn(3, Fin[:, b, :], None, "Fin" + s, None)
         send(T["C%d" % (t + 1)][:, b, :], Fin[:, b, :], "rc%d%d" % (t, h), t, ["Fin" + s])
         arrival("rc%d%d" % (t, h), t, "C%d%d" % (t + 1, h))
+        place(3)
         cp(T.o2[:, b], T.o2g[:, b], ["o2g" + s], ["o2" + s])
+        cp(T.o3[:, b], T.q3[:, 7::8], ["q3" + s], ["o3" + s])
         tt(T.g2[:, L], Ew.indirect(T.o3[:, b]), T.g1[:, L], A.min, EK + ["o3" + s, "g1" + s], ["g2" + s])
         tt(T.g3[:, L], esw.indirect(T.o2[:, b]), T.g2[:, L], A.min, ES + ["o2" + s, "g2" + s], ["g3" + s])
         mm([(pe[:, 4:4 + w], T.Ih[:], T.g3[:, L], False, True)], ["Ih", "g3" + s], [kV])
-        mm([(pD[:, 16:16 + w, :], T.Zs[:, 15 - r:143 - r], T.g3[:, NL * h + r:NL * (h + 1):16], False, r == 15) for r in range(16)], ["Zs", "g3" + s], [kD])
+        mm([(pX[:, 16:16 + w, :], T.Zs[:, 15 - r:143 - r], T.g3[:, NL * h + r:NL * (h + 1):16], False, r == 15) for r in range(16)], ["Zs", "g3" + s], [kX])
         mm([(pe[:, 0:w], T.Isc[:], T.g3[:, L], False, True)], ["Isc", "g3" + s], [kM])
         def values():
             act(T.vf[:, L], pe[:, 4:4 + w], [kV], ["vf" + s], bias=MAGIC + 254.0)
@@ -423,11 +438,9 @@ def rank_program(g, core, T, topo):
         tt(T.pn1[:, 256:512], Fin[:, b, :], T.pn1[:, 256:512], A.subtract, ["Fin" + s, "@pn1"], ["@pn1"])
         tt(T.pn1[:, 257:512], T.t3[:, 0:255], T.pn1[:, 257:512], A.mult, ["t3" + s, "@pn1"], ["@pn1"])
         tt(T.Pn[:, b, :], C[:, b, :], T.pn1[:, 256:512], A.add, [kC, "@pn1"], ["Pn" + s])
-        ts(T.si[:, b], pD[:, 16:16 + w, :], T.col[:, 2:3], None, A.add, None, [kD, "c0"], ["si" + s])
+        ts(T.si[:, b], pX[:, 16:16 + w, :], T.col[:, 2:3], None, A.add, None, [kX, "c0"], ["si" + s])
         cp(T.Pn[:, b, 0], Fin[:, b, 0], ["Fin" + s, "Pn" + s], ["Pn" + s])
         ts(T.sj[:, b], T.si[:, b], 7, None, A.bitwise_and, None, ["si" + s], ["sj" + s])
-        if t < RO - 1:
-            limit(t + 1)
         tt(T.sk[:, b], T.sj[:, b], T.lane8[:, 0:NB], A.add, ["sj" + s, "lane8"], ["sk" + s])
         if t < RO - 1 or NH == 2:
             xk = XK if NH == 1 else [XK[h]]

@@ -1,60 +1,146 @@
 from concourse.mybir import dt, AluOpType as A, ActivationFunctionType as F, AxisListType as AX
 
-NH = 1
-NB = 32 // NH
-NL = 16 * NB
+NP = 2
+PB = 128 // NP
+L = 512 // NP
+NB = L // 16
+K8 = 8 * NB
 RO = 4
-ROUTE = ()
-LATE = (3,)
-ORDER = "d0 m0 x1 y1 l0 d1 m1 e0 x2 y2 l1 d2 m2 x3 y3 z0 v0 e1 v1 l2 d3 m3 e2 h0 v2 l3 e3 s0 s1 s2 v3 n0 s3"
-SC = 2.0 ** 40
-BIG = 2.0 ** 60
+GC = 512
+VB = 32
+FOLD, FOLD0 = "ss", "--"
+V1, EZ, MERGE = "p", "p", False
+OPT = "1235"
+MW = K8 + L
+TURNS, DELTAS, PASSES, PLANS = (7.0, 8.0, 9.0, 10.0, 11.0, 12.0, 14.0), (0.15, 0.22, 0.3), 3, 3
+CYC, PEC, VFIX, SFIX = 0.83e-3, 0.417e-3, 0.05, 0.065
+CASES = ((1.2, 1.56, 3.8, 0.11, 1.6, 250.0, 5.0, 0.3, 0.8, 1.6), (1.0, 1.56, 3.8, 0.1, 1.5, 220.0, 5.0, 0.05, 0.8, 1.4), (1.0, 1.4, 3.8, 0.1, 1.5, 220.0, 4.0, 0.05, 0.8, 2.0),
+         (1.0, 1.56, 3.8, 0.1, 1.5, 220.0, 2.5, 0.05, 0.8, 1.0), (1.4, 2.0, 3.0, 0.1, 1.5, 220.0, 3.5, 0.3, 0.8, 1.4), (1.25, 1.1, 2.0, 0.1, 1.5, 220.0, 2.5, 0.05, 0.8, 1.6),
+         (1.4, 1.1, 5.5, 0.08, 1.5, 220.0, 4.0, 0.5, 0.8, 1.4), (1.1, 1.56, 3.8, 0.1, 2.0, 180.0, 8.0, 0.05, 1.5, 1.1), (1.2, 1.3, 3.8, 0.1, 1.5, 220.0, 3.0, 0.05, 0.8, 2.2))
+BIG = 1024.0
 MAGIC = 12582912.0
 bf, f32, i32, u16 = "bfloat16", "float32", "int32", "uint16"
-SCRATCH = {
-    "X": ("sbuf", [128, 4096], bf), "xg": ("sbuf", [128, 4096], bf), "yg": ("sbuf", [128, 4096], bf),
-    "mx": ("sbuf", [128, 4096], bf), "lr": ("sbuf", [128, 4096], bf),
-    "es": ("sbuf", [128, 4624], bf), "E": ("sbuf", [128, 4608], bf), "V": ("sbuf", [128, 4608], bf),
-    "cR": ("sbuf", [128, 1152], bf), "cC": ("sbuf", [128, 1152], bf),
-    "pin": ("sbuf", [128, 256], i32), "cin": ("sbuf", [128, 256], i32), "nin": ("sbuf", [128, 512], bf),
-    "win": ("sbuf", [128, 1], i32), "tin": ("sbuf", [128, 8], i32), "tbc": ("sbuf", [128, 8], i32),
-    "Pn": ("sbuf", [128, 32, 8], f32), "Nn": ("sbuf", [128, 32, 8], f32), "rp": ("sbuf", [128, 32, 8], f32),
-    "hs": ("sbuf", [128, 32, 8], i32), "hi": ("sbuf", [128, 32, 8], i32), "dr": ("sbuf", [128, 32, 8], f32),
-    "tm1": ("sbuf", [128, 264], f32), "tm2": ("sbuf", [128, 264], f32), "tm3": ("sbuf", [128, 264], f32),
-    "pat": ("sbuf", [128, 64], f32), "Jp": ("sbuf", [128, 128], f32), "Jn": ("sbuf", [128, 128], f32),
-    "poff": ("sbuf", [128, 256], u16), "coff": ("sbuf", [128, 256], u16), "hoff": ("sbuf", [128, 256], u16),
-    "hp": ("sbuf", [128, 256], f32), "LH": ("sbuf", [128, 32, 2, 16], bf), "Ti": ("sbuf", [128, 64], i32),
-    "v2": ("sbuf", [128, 512], bf), "v2c": ("sbuf", [128, 512], bf), "v3": ("sbuf", [128, 512], bf), "v3c": ("sbuf", [128, 512], bf),
-    "g1": ("sbuf", [128, 512], bf), "g2": ("sbuf", [128, 512], bf), "g3": ("sbuf", [128, 512], bf),
-    "val": ("sbuf", [128, 512], bf), "vf": ("sbuf", [128, 512], f32), "N4": ("sbuf", [128, 512], bf),
-    "ne": ("sbuf", [128, 32], bf), "o2f": ("sbuf", [128, 32], f32), "o2g": ("sbuf", [128, 32], f32),
-    "si": ("sbuf", [128, 32], i32), "sj": ("sbuf", [128, 32], i32), "sk": ("sbuf", [128, 32], f32),
-    "base": ("sbuf", [128, 32], f32), "lane8": ("sbuf", [128, 32], f32), "lb": ("sbuf", [128, 32], bf), "junk": ("sbuf", [128, 32], f32),
-    "col": ("sbuf", [128, 16], f32), "coli": ("sbuf", [128, 4], i32), "wb": ("sbuf", [128, 2], bf), "cnt": ("sbuf", [128, 2], f32),
-    "thr": ("sbuf", [128, 1], f32), "G": ("sbuf", [128, 8], f32), "G0": ("sbuf", [128, 8], f32), "b16": ("sbuf", [128, 32], f32),
-    "Ip": ("sbuf", [128, 128], bf), "ad": ("sbuf", [128, 4096], bf),
-    "ones": ("sbuf", [128, 128], bf), "BO": ("sbuf", [128, 128], bf), "BO0": ("sbuf", [128, 128], bf), "I": ("sbuf", [128, 128], bf),
-    "Isc": ("sbuf", [128, 128], bf), "In": ("sbuf", [128, 128], bf), "Ih": ("sbuf", [128, 128], bf), "Im": ("sbuf", [128, 128], bf),
-    "Fm": ("sbuf", [128, 1024], bf), "ok2": ("sbuf", [128, 256, 2], bf), "Z": ("sbuf", [128, 144], bf), "Zh": ("sbuf", [128, 144], bf), "Zw": ("sbuf", [128, 144], bf),
-    "Zs": ("sbuf", [128, 144], bf), "oan": ("sbuf", [128, 32], f32), "c25": ("sbuf", [128, 512], bf), "Yp": ("sbuf", [128, 256], f32), "Yc": ("sbuf", [128, 256], f32),
-    "pe0": ("psum", [128, 8, 8, 16], f32), "pe1": ("psum", [128, 8, 8, 16], f32),
-    "pD0": ("psum", [128, 64, 8], f32), "pD1": ("psum", [128, 64, 8], f32),
-    "pn1": ("psum", [128, 512], f32), "pn2": ("psum", [128, 32, 16], f32),
+PIPE = {
+    "X": ([4096], bf), "xg": ([8 * L], bf), "yg": ([8 * L], bf), "mx": ([8 * L], bf), "lr": ([8 * L], bf), "xy": ([16 * L], bf), "xm": ([16 * L], bf),
+    "es": ([L * 9], bf), "E": ([L * 9], bf), "V": ([L // VB, 9 * VB], bf), "v1": ([L], bf), "v2c": ([L], bf),
+    "wcol": ([8], f32), "Zw": ([144], bf),
+    "Pn": ([NB, 8], f32), "Nn": ([NB, 8], f32), "rp": ([K8], f32), "hs": ([K8], i32), "hi": ([K8], i32), "hp": ([K8], f32),
+    "dr": ([NB, 7], f32), "tm": ([3, K8 + 8], f32), "fr": ([3, K8], f32),
+    "poff": ([K8], u16), "coff": ([K8], u16), "hoff": ([K8], u16), "ok2": ([K8, 2], bf),
+    "s1": ([NB, 8], bf), "t1": ([K8], bf), "t2": ([K8], i32), "t3": ([K8 + 8], i32), "Ti": ([2 * NB], i32),
+    "LH": ([NB, 2, 16], bf), "v2": ([L], bf), "v3": ([L], bf), "g1": ([L], bf), "g2": ([L], bf), "g3": ([L], bf),
+    "val": ([L], bf), "vf": ([L], f32), "N4": ([L], bf), "ne": ([NB], bf), "o2f": ([NB], f32),
+    "q2": ([K8], f32), "Q3": ([2 * K8], f32), "d3": ([K8], f32), "pre": ([NB], f32), "kw": ([NB, 8], f32), "kx": ([NB, 8], f32), "q1": ([K8], f32),
+    "si": ([NB], i32), "sj": ([NB], i32), "sk": ([NB], f32), "junk": ([NB], f32),
+    "oa": ([NB], u16), "ob": ([NB], u16), "oo": ([2 * NB], u16), "eo": ([NB], u16), "po": ([NB], u16),
+    "C": ([(RO + 1) * MW], f32), "Fin": ([RO * MW], f32), "MN": ([RO * 2 * L], bf), "ms": ([RO * L], bf),
+    "Yk": ([16, NB], f32), "Yo": ([512], f32),
 }
-for _s in (1, 2, 3):
-    SCRATCH["t%d" % _s] = ("sbuf", [128, 256], i32)
-    SCRATCH["q%d" % _s] = ("sbuf", [128, 256], f32)
-    SCRATCH["d%d" % _s] = ("sbuf", [128, 256], f32)
-for _n in ("oa", "ob", "o2", "o3", "eo", "po"):
-    SCRATCH[_n] = ("sbuf", [128, 32], u16)
-for _t in range(RO + 1):
-    SCRATCH["C%d" % _t] = ("sbuf", [128, 32, 8], f32)
-for _t in range(RO):
-    SCRATCH["MN%d" % _t] = ("sbuf", [128, 1024], bf)
-    SCRATCH["Fin%d" % _t] = ("sbuf", [128, 32, 8], f32)
-    SCRATCH["ms%d" % _t] = ("sbuf", [128, 512], bf)
-DMAS = ["lp", "lc", "ln", "lw", "lt", "lx0", "lx1", "sp", "sc", "sn"] + ["sx%d" % h for h in range(2 if NH == 2 else 4)]
-SEMAPHORES = ["v", "a", "t", "p", "sent"] + DMAS + ["r%s%d%d" % (k, t, h) for k in "cn" for t in range(RO) for h in range(NH)]
+SCALED = (("In", -1.0, bf), ("Ih", 0.5, bf), ("IL", -1.0 * L, bf), ("I2", -2.0, bf), ("IK", 4096.0, bf), ("IKn", -4096.0, bf), ("Jp", 1.0, f32), ("Jn", -1.0, f32))
+SCRATCH = {n: ("sbuf", [128, NP * s[0]] + s[1:], d) for n, (s, d) in PIPE.items()}
+SCRATCH.update({n: ("sbuf", [128, 128], d) for n, c, d in SCALED})
+SCRATCH.update({
+    "cM": ("sbuf", [128, 2 * GC], bf), "cR": ("sbuf", [128, 1152], bf), "cC": ("sbuf", [128, 9 * VB], bf), "th9": ("sbuf", [128, K8], bf),
+    "pin": ("sbuf", [128, 256], i32), "cin": ("sbuf", [128, 256], i32), "pf": ("sbuf", [128, 8, 32], f32), "cf": ("sbuf", [128, 8, 32], f32),
+    "nin": ("sbuf", [128, 512], bf), "win": ("sbuf", [128, 1], i32), "tin": ("sbuf", [128, 8], i32), "tbc": ("sbuf", [128, 8], i32), "G": ("sbuf", [128, 8], f32), "G0": ("sbuf", [128, 8], f32), "G4": ("sbuf", [128, 8], f32),
+    "col": ("sbuf", [128, 16], f32), "coli": ("sbuf", [128, 8], i32), "wb": ("sbuf", [128, 2 * NP], bf), "cnt": ("sbuf", [128, 2 * NP], f32),
+    "b16": ("sbuf", [128, NB], bf), "bL": ("sbuf", [128, NB], bf), "b144": ("sbuf", [128, NB], bf), "r9": ("sbuf", [128, NB], bf), "c9": ("sbuf", [128, NB], bf), "cK": ("sbuf", [128, K8], bf),
+    "base": ("sbuf", [128, NB], f32), "lane8": ("sbuf", [128, NB], f32), "d2": ("sbuf", [128, K8], f32), "m8": ("sbuf", [128, K8], f32),
+    "ones": ("sbuf", [128, 128], bf), "BO": ("sbuf", [128, 128], bf), "I": ("sbuf", [128, 128], bf),
+    "Fm": ("sbuf", [128, 1024], bf), "Z": ("sbuf", [128, 144], bf), "Zh": ("sbuf", [128, 144], bf),
+    "pD": ("psum", [128, 32, 16], f32), "pC": ("psum", [128, 64, 8], f32), "pV": ("psum", [128, 512], f32),
+    "pN": ("psum", [128, 32, 16], f32), "pe0": ("psum", [128, 8, 8, 16], f32), "pX": ("psum", [128, 64, 8], f32), "pY": ("psum", [128, 32, 16], f32),
+})
+SEMAPHORES = ["v", "a", "t", "p", "sent"] + ["d%d" % i for i in range(64)] + ["r%s%d%d" % (k, t, h) for k in "cn" for t in range(RO) for h in range(NP)]
+
+
+def sweep(ops, cost, wake, delta, pre, succ, rank, first):
+    n = len(ops)
+    todo = [len(p) for p in pre]
+    est = list(first)
+    start, end = [0.0] * n, [0.0] * n
+    ready = {q: [] for q in "vatps"}
+    free = {q: 0.0 for q in ready}
+    for i, o in enumerate(ops):
+        if not todo[i]:
+            ready[o["q"]].append(i)
+    user = {}
+
+    def at(i):
+        o = ops[i]
+        return max([est[i]] + [user[b][1] + wake for b in o["banks"] if b in user and ops[user[b][0]]["q"] != o["q"]])
+    for _ in range(n):
+        can = {q: [(at(i), i) for i in ready[q]] for q in ready}
+        q = min((q for q in can if can[q]), key=lambda q: max(free[q], min(can[q])[0]))
+        t0 = max(free[q], min(can[q])[0])
+        now = max((c for c in can[q] if c[0] <= t0), key=lambda c: (rank[c[1]], -c[1]))
+        d = delta * min(1.0, cost[now[1]])
+        e, i = max((c for c in can[q] if c[0] <= t0 + d), key=lambda c: (rank[c[1]], -c[1]))
+        ready[q].remove(i)
+        o = ops[i]
+        start[i] = max(t0, e)
+        end[i] = free[q] = start[i] + cost[i]
+        for b in o["banks"]:
+            user[b] = (i, free[q])
+        for j in succ[i]:
+            est[j] = max(est[j], free[q] + pre[j][i])
+            todo[j] -= 1
+            if not todo[j]:
+                ready[ops[j]["q"]].append(j)
+    return start, end
+
+
+def price(ops, case):
+    f, ga, sc, wake, dl, bw, rl, di, ri, tf = case
+    rate = {"e": CYC * f, "g": CYC * f * ga, "s": CYC * f * sc, "t": PEC * tf}
+    return [di if o["kind"] == "d" else ri if o["kind"] == "r" else o["fix"] * f + o["n"] * rate[o["kind"]] for o in ops], [dl + o["n"] / bw if o["kind"] == "d" else rl if o["kind"] == "r" else 0.0 for o in ops], wake
+
+
+def handover(ops, out):
+    user, more = {}, {}
+    for i in out:
+        for b in ops[i]["banks"]:
+            if b in user and ops[user[b]]["q"] != ops[i]["q"]:
+                more.setdefault(i, []).append(user[b])
+            user[b] = i
+    return more
+
+
+def span(ops, out, more, cost, lat, wake):
+    free, end = {}, {}
+    for i in out:
+        o = ops[i]
+        t = max([free.get(o["q"], 0.0)] + [end[j] + lat[j] + wake for j, w in o["pre"].items() if w] + [end[j] + wake for j in more.get(i, [])])
+        end[i] = free[o["q"]] = t + cost[i]
+    return max(end[i] + lat[i] for i in out)
+
+
+def order(ops):
+    n = len(ops)
+    prices = [price(ops, c) for c in CASES]
+    found = []
+    for cost, lat, wake in prices[:PLANS]:
+        fwd = [{j: (lat[j] + wake if w else 0.0) for j, w in o["pre"].items()} for o in ops]
+        back = [{} for _ in ops]
+        for i in range(n):
+            for j, d in fwd[i].items():
+                back[j][i] = d
+        left = [0.0] * n
+        for i in range(n - 1, -1, -1):
+            left[i] = cost[i] + max([left[j] + d for j, d in back[i].items()] + [lat[i]])
+        for turn in TURNS:
+            for delta in DELTAS:
+                rank = [r - turn * o["lead"] for r, o in zip(left, ops)]
+                for _ in range(PASSES):
+                    start, end = sweep(ops, cost, wake, delta, fwd, back, rank, [0.0] * n)
+                    out = sorted(range(n), key=lambda i: (start[i], i)); more = handover(ops, out)
+                    found.append(([span(ops, out, more, *p) for p in prices], out, more))
+                    rank = sweep(ops, cost, wake, delta, back, fwd, end, lat)[1]
+    unit = [min(f[0][c] for f in found) for c in range(len(CASES))]
+    return min(found, key=lambda f: sum((a / b) ** 8 for a, b in zip(f[0], unit)))[1:]
+
+
+PLAN = []
 
 
 def rank_program(g, core, T, topo):
@@ -64,433 +150,466 @@ def rank_program(g, core, T, topo):
     N = len(T.cores)
     Q = {"v": g.vector, "a": g.scalar, "t": g.tensor, "p": g, "s": g.sync}
     V, S, PE = g.vector, g.scalar, g.tensor
-    cnt = {"v": 0, "a": 0, "t": 0, "p": 0}
+    ops, lastw, readers, lastload, ndma, lead, sent = [], {}, {}, {}, [0, 0], [0.0], [0]
+
+    def add(q, fix, n, fn, rd, wr, sig=None):
+        i = len(ops); pre = {}
+
+        def edge(j, wait):
+            pre[j] = pre.get(j, False) or ops[j]["q"] != q or ops[j]["sig"] is not None or (wait and q != "t")
+        for k in rd:
+            for j in lastw.get(k, []):
+                edge(j, True)
+        for k in wr:
+            for j in lastw.get(k, []):
+                edge(j, True)
+            for j in readers.get(k, []):
+                edge(j, True)
+        banks = sorted({k.split(":")[0] for k in list(rd) + list(wr) if k[0] == "@"})
+        for k in rd:
+            readers.setdefault(k, []).append(i)
+        for k in wr:
+            lastw[k] = [i]; readers[k] = []
+        kind, n = n if isinstance(n, tuple) else ("e", n)
+        ops.append({"q": q, "fix": fix, "kind": kind, "n": n, "fn": fn, "pre": pre, "sig": sig, "banks": banks, "lead": lead[0]})
+
+    def vop(fn, n, rd, wr):
+        add("v", VFIX, n, fn, rd, wr)
+
+    def ts(o, i, s1, s2, o0, o1, n, rd, wr):
+        vop((lambda: V.tensor_scalar(o, i, s1, None, o0)) if o1 is None else (lambda: V.tensor_scalar(o, i, s1, s2, o0, o1)), n, rd, wr)
+
+    def tt(o, a, b, f, n, rd, wr):
+        vop(lambda: V.tensor_tensor(o, a, b, f), n, rd, wr)
+
+    def cp(o, i, n, rd, wr):
+        vop(lambda: V.tensor_copy(o, i), n, rd, wr)
+
+    def fill(o, c, n, wr):
+        vop(lambda: V.memset(o, c), n, [], wr)
+
+    def scan(o, a, b, init, o0, o1, n, rd, wr):
+        vop(lambda: V.tensor_tensor_scan(o, a, b, init, o0, o1), n, rd, wr)
+
+    def act(o, i, n, rd, wr, f=F.Identity, **k):
+        add("a", SFIX, n, lambda: S.activation(o, i, f, **k), rd, wr)
+
+    def pool(fn, n, rd, wr):
+        add("p", 0.17, 2 * n, fn, rd, wr)
+
+    def mm(calls, n, rd, wr):
+        def fn():
+            for a in calls[:-1]:
+                PE.matmul(*a)
+            return PE.matmul(*calls[-1])
+        b = "group" + wr[0].split(":")[0]
+        if any(a[3] for a in calls) and calls[-1][4]:
+            rd = list(rd) + [b]
+        else:
+            wr = list(wr) + [b]
+        add("t", 0.0, ("t", n), fn, rd, wr)
+
+    def dma(q, out, in_, kb, rd, wr, inturn=False):
+        sem = "d%d" % ndma[0]; ndma[0] += 1
+        if inturn:
+            ndma[1] += kb; kb = ndma[1]
+        add(q, 0.05, ("d", kb), lambda: Q[q].dma_start(out, in_), rd, wr, (sem, 16, True))
+        if inturn:
+            if q in lastload:
+                ops[-1]["pre"][lastload[q]] = False
+            lastload[q] = len(ops) - 1
+
+    def send(dst, src, sem, t, rd, wr):
+        to = T.cores[(rank + 1 + t % 3) % N]; fr = T.cores[(rank - 1 - t % 3) % N]
+        rid, pid, _ = topo.addr(to)
+        add("p", 0.8, ("r", 0), lambda: g.remote_dma(dst, src, T.sem[sem], T.sem.sent, pid, rid, topo.mask(core, to)), rd, wr,
+            (sem, len(topo.engines(fr, core)), False))
+        sent[0] += len(topo.engines(core, to))
+
+    def view(h):
+        def b(name, *ix):
+            w = PIPE[name][0][0]
+            if not ix:
+                return T[name][:, w * h:w * h + w]
+            f = ix[0]
+            if isinstance(f, slice):
+                f = slice(w * h + (f.start or 0), w * h + (w if f.stop is None else f.stop), f.step)
+            else:
+                f = w * h + f
+            return T[name][(slice(None), f) + ix[1:]]
+        return b
+    gat = lambda n: ("g", n)
+    sl, al = slice, slice(None)
+    each = lambda k, h: ["%s%d%d" % (k, h, s) for s in range(NP)]
+
+    table = lambda h, s: dma("sa"[s % 2], T.X[PB * s:PB * s + PB, 4096 * h:4096 * h + 4096], T.lit[PB * h:PB * h + PB, :], 512, [], ["X%d%d" % (h, s)], True)
+    dma("s", T.pin[:], T.pn[:], 128, [], ["pin"], True)
+    dma("a", T.cin[:], T.cn[:], 128, [], ["cin"], True)
+    for h in range(NP):
+        for s in range(NP):
+            table(h, s)
+        if h == 0:
+            dma("s", T.nin[:], T.neg[:], 128, [], ["nin"], True)
+            dma("a", T.tin[0:1, :], T.th[:], 1, [], ["tin"], True)
+            dma("s", T.win[:], T.wt[:], 1, [], ["win"], True)
+    fill(T.ones[:], 1.0, 64, ["ones"])
+    fill(T.G0[:], 1.0, 8, ["G0"])
+    fill(T.Fm[:], -512.0, 512, ["Fm"])
+    pool(lambda: g.iota(T.coli[:, 0:1], [[0, 1]], 0, 1), 1, [], ["coli"])
+    pool(lambda: g.iota(T.b16[:], [[16, NB]], 0, 0, allow_small_or_imprecise_dtypes=True), NB, [], ["b16"])
+    pool(lambda: g.affine_select(T.I[:], T.ones[:], [[-1, 128]], A.is_equal, 0.0, 0, 1), 128, ["ones"], ["I"])
+    pool(lambda: g.affine_select(T.G[:], T.G0[:], [[-16, 8]], A.is_ge, 0.0, 0, 1), 8, ["G0"], ["G"])
+    pool(lambda: g.affine_select(T.G[:], T.G[:], [[16, 8]], A.is_ge, 0.0, 15, -1), 8, ["G"], ["G"])
+    pool(lambda: g.partition_broadcast(T.tbc[:], T.tin[0:1, :], 128), 16, ["tin"], ["tbc"])
+    pool(lambda: g.affine_select(T.Fm[:], T.Fm[:], [[-2, 8], [-16, 8], [0, 16]], A.is_ge, 0.0, 0, 1), 1024, ["Fm"], ["Fm"])
+    pool(lambda: g.affine_select(T.Fm[:], T.Fm[:], [[2, 8], [16, 8], [0, 16]], A.is_ge, 0.0, 1, -1), 1024, ["Fm"], ["Fm"])
+    pool(lambda: g.affine_select(T.BO[:], T.ones[:], [[-16, 8], [0, 16]], A.is_ge, 0.0, 0, 1), 128, ["ones"], ["BO"])
+    pool(lambda: g.affine_select(T.BO[:], T.BO[:], [[16, 8], [0, 16]], A.is_ge, 0.0, 15, -1), 128, ["BO"], ["BO"])
+    for nm, c, _ in SCALED:
+        act(T[nm][:], T.I[:], 128, ["I"], [nm], scale=c)
+    for z, c in (("Z", 1.0), ("Zh", -0.5)):
+        fill(T[z][:], 0.0, 72, [z])
+        ts(T[z][:, 15:143:16], T.G[:], c, None, A.mult, None, 8, ["G", z], [z])
+    fill(T.cM[:], BIG, GC, ["cM"])
+    fill(T.cM[:, 0::2], -BIG, GC // 2, ["cM"])
+    fill(T.cR[:], -BIG, 576, ["cR"])
+    fill(T.cR[:, 0::9], BIG, 64, ["cR"])
+    for k in range(9):
+        fill(T.cC[:, k::9], 32.0 ** (k - 8), VB // 2, ["cC%d" % k])
+    for k in range(8):
+        fill(T.th9[:, k::8], -8.5 * 32.0 ** (k - 7), 8, ["th9%d" % k])
+    CC, TH9 = ["cC%d" % k for k in range(9)], ["th9%d" % k for k in range(8)]
+    ts(T.coli[:, 1:2], T.coli[:, 0:1], 1, None, A.bitwise_and, None, 1, ["coli"], ["c1"])
+    ts(T.col[:, 6:7], T.coli[:, 1:2], -1.0, None, A.add, None, 1, ["c1"], ["par0"])
+    ts(T.col[:, 7:8], T.coli[:, 1:2], -1.0, None, A.mult, None, 1, ["c1"], ["par1"])
+    ts(T.coli[:, 2:3], T.coli[:, 0:1], 15, None, A.bitwise_and, None, 1, ["coli"], ["c2"])
+    cp(T.col[:, 0:1], T.coli[:, 2:3], 1, ["c2"], ["r"])
+    ts(T.coli[:, 3:4], T.coli[:, 0:1], 128 - PB, None, A.bitwise_and, None, 1, ["coli"], ["c3"])
+    ts(T.col[:, 1:2], T.coli[:, 3:4], 1.0 * L / PB, T.col[:, 0:1], A.mult, A.add, 1, ["c3", "r"], ["rs"])
+    ts(T.b144[:], T.b16[:], 9.0, None, A.mult, None, NB, ["b16"], ["b144"])
+    ts(T.bL[:], T.b16[:], 1.0 * L, None, A.add, None, NB, ["b16"], ["bL"])
+    ts(T.base[:], T.b16[:], T.col[:, 0:1], 9.0, A.add, A.mult, NB, ["b16", "r"], ["base"])
+    ts(T.col[:, 2:3], T.col[:, 0:1], 9.0, None, A.mult, None, 1, ["r"], ["r9c"])
+    ts(T.r9[:], T.b16[:], 0.0, T.col[:, 2:3], A.mult, A.add, NB, ["b16", "r9c"], ["r9"])
+    ts(T.lane8[:], T.b16[:], T.col[:, 1:2], 8.0, A.add, A.mult, NB, ["b16", "rs"], ["lane8"])
+    fill(T.c9[:], 9.0, NB, ["c9"])
+    fill(T.cK[:], -2.5, K8 // 2, ["cK"])
+    fill(T.d2[:], -100.0, K8, ["d2"])
+    cp(T.d2[:, 0::8], T.base[:], NB, ["base", "d2"], ["d2"])
+    fill(T.m8[:], 1.0, K8, ["m8"])
+    fill(T.m8[:, 0::8], 0.0, NB, ["m8"])
+    fill(T.d3[:], -100.0, K8 * NP, ["d3%d" % h for h in range(NP)])
+    fill(T.t3[:, 7::K8 + 8], 1, NP, ["t30"])
+    fill(T.tm[:, :, 0], 0.0, 3 * NP, ["tm0"])
+    fill(T.pN[:, 0:NB, 15], 0.0, NB, ["@pN:t"])
+    fill(T.Zw[:], 0.0, 144, ["Zw%d" % h for h in range(NP)])
+    GN = 8 // NP
+    tt(T.G4[:, 0:GN], T.G[:, 0:GN], T.G[:, GN:2 * GN], A.add, GN, ["G"], ["G4"])
+    ts(T.pf[:], T.pin[:], -2048.0, None, A.add, None, 256, ["pin"], ["pf"])
+    ts(T.cf[:], T.cin[:], -2048.0, None, A.add, None, 256, ["cin"], ["cf"])
+    cp(T.wb[:, 0:1], T.win[:], 1, ["win"], ["wb"])
+    for h in range(NP):
+        B = view(h); s_ = str(h); rows = sl(PB * h, PB * h + PB); to = lambda s: sl(PB * s, PB * s + PB)
+        for j, (src, nm, ky) in enumerate(((T.pf, "Pn", ["@pD:y"]), (T.cf, "C", ["@pD:z"]))):
+            mm([(T.pD[to(s), 16 + 8 * j:24 + 8 * j], T.Jp[:, rows], src[:, :, NB * s:NB * s + NB], True, True) for s in range(NP)], 4 * K8 * NP, ["Jp", "pf", "cf"][0:2 + j:1 + j], ky)
+            for k in range(8):
+                act(B(nm, sl(k, K8, 8)) if j else B(nm, al, k), T.pD[:, 16 + 8 * j + k], NB, ky, ["%s%d%d" % (nm, h, k)])
+            lastw[("Pn", "C0")[j] + s_] = [lastw.pop("%s%d%d" % (nm, h, k))[0] for k in range(8)]
+        ts(B("poff"), B("Pn"), 2048.0, None, A.add, None, K8, ["Pn" + s_], ["poff" + s_])
+        mm([(T.pV[to(s), 0:L], T.I[:, rows], T.nin[:, L * s:L * s + L], True, True) for s in range(NP)], L * NP, ["I", "nin"], ["@pV:v"])
+        act(B("MN", sl(L, 2 * L)), T.pV[:, 0:L], L, ["@pV:v"], ["n0" + s_], scale=-1.0, bias=256.0)
+        tt(T.G0[:, GN * h:GN * h + GN], T.tbc[:, GN * h:GN * h + GN], T.G4[:, 0:GN], A.mult, GN, ["tbc", "G4", "G0"], ["tg" + s_])
+        vop(lambda h=h, B=B: V.tensor_reduce(B("wcol", sl(6, 7)), T.G0[:, GN * h:GN * h + GN], AX.X, A.add), GN, ["tg" + s_], ["tj" + s_])
+        ts(B("wcol", sl(1, 2)), B("wcol", sl(6, 7)), 0.5, None, A.add, None, 1, ["tj" + s_], ["th" + s_])
+        ts(B("wcol", sl(4, 5)), B("wcol", sl(1, 2)), 0.5, None, A.mult, None, 1, ["th" + s_], ["thr" + s_])
+        mm([(T.pX[to(s), 2 * h + j, 0:1], T[m][:, rows], T.wb[:, 0:1], True, True) for j, m in enumerate(("I", "BO")) for s in range(NP)], 128 * NP, ["I", "BO", "wb"], ["@pX:w" + s_])
+        ts(B("Zw", sl(15, 143, 16)), T.G[:], T.pX[:, 2 * h, 0:1], None, A.mult, None, 8, ["G", "@pX:w" + s_, "Zw" + s_], ["Zw" + s_])
+        act(B("wcol", sl(3, 4)), T.pX[:, 1 + 2 * h, 0:1], 1, ["@pX:w" + s_], ["c0" + s_], scale=255.0)
+
+    def head(t, h):
+        B = view(h); s_ = str(h); XK = each("X", h); kC = "C%d%d" % (t, h); kn = "n%d%d" % (t, h)
+        if MERGE and t:
+            act(B("MN", sl(2 * L * t + L, 2 * L * t + 2 * L)), B("C", sl(MW * t + K8, MW * t + MW)), L, [kC], [kn])
+        X = B("X"); C = B("C", sl(MW * t, MW * t + K8)); npr = lambda a, n: B("MN", sl(2 * L * t + L + a, 2 * L * t + L + a + n))
+        pA, pB, kA = T.pY[:, 8 * h:8 * h + 8], T.pY[:, 16:24], "@pY:A" + s_; how = FOLD if t + h else FOLD0
+        act(pA, B("Pn"), K8, ["Pn" + s_], [kA], bias=3232.0)
+        act(B("rp"), B("Pn"), K8, ["Pn" + s_], ["rp" + s_], scale=2080.0, bias=-3801088.0)
+        ts(B("coff"), C, 2048.0, None, A.add, None, K8, [kC], ["coff" + s_])
+        tt(pA, pA, C, A.mult, K8, [kA, kC], [kA])
+        tt(B("hs"), pA, B("rp"), A.add, K8, [kA, "rp" + s_], ["hs" + s_])
+        ts(B("hi"), B("hs"), 5, 4095, A.arith_shift_right, A.bitwise_and, K8, ["hs" + s_], ["hi" + s_])
+        cp(B("hoff"), B("hi"), K8, ["hi" + s_], ["hoff" + s_])
+        if EZ == "a":
+            act(B("es", sl(0, 9 * L, 9)), npr(0, L), L, [kn], ["ez" + s_])
+        else:
+            pool(lambda: g.affine_select(B("es", sl(0, 9 * L, 9)), npr(0, L), [[0, L]], A.is_ge, 0.0, 0, 0), L, [kn], ["ez" + s_])
+        for c in range(L // 128):
+            ks = lambda nm, a, n: ["%s%d%d" % (nm, h, u) for u in range(a // 256, (a + n) // 256)]
+            e0 = 1024 * c
+            for a in range(e0, e0 + 1024, GC):
+                e = sl(a, a + GC); o = sl(a // 16, (a + GC) // 16)
+                if how[c] == "s":
+                    e2 = sl(2 * a, 2 * (a + GC)); odd = sl(2 * a + 1, 2 * (a + GC), 2)
+                    act(B("xy", sl(2 * a, 2 * (a + GC), 2)), X.indirect(B("poff", o)), gat(GC), XK + ["poff" + s_], ks("x", a, GC))
+                    act(B("xy", odd), X.indirect(B("coff", o)), gat(GC), XK + ["coff" + s_], ks("y", a, GC))
+                    scan(B("xm", e2), T.cM[:], B("xy", e2), 0.0, A.min, A.max, GC, ["cM"] + ks("x", a, GC) + ks("y", a, GC), ks("m", a, GC))
+                    tt(B("lr", e), X.indirect(B("hoff", o)), B("xm", odd), A.min, gat(GC), XK + ["hoff" + s_] + ks("m", a, GC), ks("l", a, GC))
+                    continue
+                act(B("xg", e), X.indirect(B("poff", o)), gat(GC), XK + ["poff" + s_], ks("x", a, GC))
+                act(B("yg", e), X.indirect(B("coff", o)), gat(GC), XK + ["coff" + s_], ks("y", a, GC))
+                tt(B("mx", e), X.indirect(B("coff", o)), B("xg", e), A.max, gat(GC), XK + ["coff" + s_] + ks("x", a, GC), ks("m", a, GC))
+                tt(B("lr", e), X.indirect(B("hoff", o)), B("mx", e), A.min, gat(GC), XK + ["hoff" + s_] + ks("m", a, GC), ks("l", a, GC))
+            if how[c] == "s":
+                row = lambda src, r: B("xm" if src == "mx" else "xy", sl(2 * (e0 + r) + (src != "xg"), 2 * (e0 + 1024), 32))
+            else:
+                row = lambda src, r: B(src, sl(e0 + r, e0 + 1024, 16))
+            pD = T.pD[:, 8 * h + 4 * c:8 * h + 4 * c + 4]; kD = "@pD:%d%d" % (h, c)
+            part = lambda z, src, first, last: [(pD, T[z][:, 15 - r:143 - r], row(src, r), first and r == 0, last and r == 15) for r in range(16)]
+            mm(part("Zh", "xg", True, False), 1024, ["Zh"] + ks("x", e0, 1024) + ks("y", e0, 1024), [kD])
+            mm(part("Zh", "yg", False, False), 1024, ["Zh"] + ks("y", e0, 1024), [kD])
+            mm(part("Z", "mx", False, True), 1024, ["Z"] + ks("m", e0, 1024), [kD])
+            for u in range(2):
+                act(B("ok2", sl(64 * c, 64 * c + 64), u), pD, 64, [kD, "thr" + s_, "par%d" % u], ["ok%d%d%d" % (h, c, u)], F.Sign, scale=T.col[:, 6 + u:7 + u], bias=B("wcol", sl(4, 5)))
+            pe = T.pe0; kb = ["@pe0%d" % u for u in range(2)]; sc = "%d%d" % (h, c)
+            for u in range(2):
+                bk = sl(4 * u, 4 * u + 4); b0 = 8 * c + 4 * u; l0 = 16 * b0
+                mm([(pe[:, bk, k, :], T.I[:], npr(l0, 64), k == 0, False) for k in range(8)], 512, ["I", kn], [kb[u]])
+                mm([(pe[:, bk, :, 2 * r:2 * r + 2], T.Fm[:, 128 * r:128 * r + 128], B("ok2", sl(8 * b0, 8 * b0 + 32)), False, False) for r in range(8)], 512, ["Fm", "ok%s0" % sc, "ok%s1" % sc], [kb[u]])
+                mm([(pe[:, bk], T.I[:], B("lr", sl(8 * l0, 8 * l0 + 512)), False, True)], 512, ks("l", 8 * l0, 512), [kb[u]])
+            for k in range(8):
+                act(B("es", sl(1152 * c + 1 + k, 1152 * c + 1152, 9)), pe[:, :, k, :], 128, kb, ["es%s%d" % (sc, k)], bias=769.0)
+            ln = sl(1152 * c, 1152 * c + 1152)
+            scan(B("E", ln), T.cR[:], B("es", ln), 0.0, A.max, A.min, 576, ["cR", "ez" + s_] + ["es%s%d" % (sc, k) for k in range(8)], ["E" + sc])
+            for b in range(128 * c // VB, (128 * c + 128) // VB):
+                scan(B("V", b), B("E", sl(9 * VB * b, 9 * VB * (b + 1))), T.cC[:], 1.0, A.max, A.min, 4.5 * VB, CC + ["E" + sc], ["V%d%d" % (h, b)])
+        if V1 == "a":
+            act(B("v1"), B("V", al, sl(6, 9 * VB, 9)), L, ["V%d%d" % (h, b) for b in range(L // VB)], ["v1" + s_])
+        else:
+            pool(lambda: g.affine_select(B("v1"), B("V", al, sl(6, 9 * VB, 9)), [[0, L]], A.is_ge, 0.0, 0, 0), L, ["V%d%d" % (h, b) for b in range(L // VB)], ["v1" + s_])
+        OK = ["ok%d%d%d" % (h, c, u) for c in range(L // 128) for u in range(2)]
+        pO = T.pY[:, 24:32]
+        if "2" in OPT:
+            act(pB, B("Pn"), K8, ["Pn" + s_], ["@pY:B"], bias=2048.0)
+            tt(B("hp"), B("hi"), pB, A.subtract, K8, ["hi" + s_, "@pY:B"], ["hp" + s_])
+            mm([(pO, T.Ih[:], B("ok2", al, u), u == 0, u == 1) for u in range(2)], 2 * K8, OK + ["Ih"], ["@pY:o"])
+            tt(pO, pO, B("hp"), A.mult, K8, ["@pY:o", "hp" + s_], ["@pY:o"])
+            tt(B("Nn"), B("Pn"), pO, A.add, K8, ["@pY:o", "Pn" + s_], ["Nn" + s_])
+            return
+        mm([(pO, T.IK[:], B("ok2", al, u), u == 0, False) for u in range(2)] + [(pO, T.IK[:], T.cK[:], False, True)], 3 * K8, OK + ["IK", "cK"], ["@pY:o"])
+        mm([(pB, T.Jp[:], B("Pn"), True, False)] + [(pB, T.IKn[:], B("ok2", al, u), False, u == 1) for u in range(2)], 6 * K8, OK + ["IKn", "Jp", "Pn" + s_], ["@pY:B"])
+        tt(B("hp"), B("hi"), pO, A.add, K8, ["@pY:o", "hi" + s_], ["hp" + s_])
+        tt(B("Nn"), B("hp"), pB, A.max, K8, ["@pY:B", "hp" + s_], ["Nn" + s_])
+
+    def tail(t, h):
+        B = view(h); s_ = str(h); XK = each("X", h); kC = "C%d%d" % (t, h); kn = "n%d%d" % (t, h); last = t == RO - 1
+        k_ = lambda *n: [x + s_ for x in n]
+        ES = ["es%d%d%d" % (h, c, k) for c in range(L // 128) for k in range(8)] + ["ez" + s_]
+        EK, VK = ["E%d%d" % (h, c) for c in range(L // 128)], ["V%d%d" % (h, b) for b in range(L // VB)]
+        C = B("C", sl(MW * t, MW * t + K8)); Fin = B("Fin", sl(MW * t, MW * t + K8)); npr = B("MN", sl(2 * L * t + L, 2 * L * t + 2 * L))
+        pC, pN = T.pC, T.pN
+        nb = sl(0, NB)
+        pX = T.pX; pP = pX[:, 8 + 2 * h:10 + 2 * h]
+        pQ, pS, pF, pF0, pG = pC[:, 16 + 2 * h:18 + 2 * h], pX[:, 24:26], pN[:, 16:24], pN[:, 16:24, 0::8], pN[:, 24:32]
+        if "3" in OPT:
+            act(pX[:, 32:48, 0:7], B("Nn", al, sl(0, 7)), 7 * NB, k_("Nn"), ["@pX:d"])
+            tt(B("dr"), pX[:, 32:48, 0:7], B("Nn", al, sl(1, 8)), A.subtract, 7 * NB, ["@pX:d"] + k_("Nn"), k_("dr"))
+        else:
+            mm([(pX[:, 32:48, 0:7], T.Jp[:], B("Nn", al, sl(0, 7)), True, False), (pX[:, 32:48, 0:7], T.Jn[:], B("Nn", al, sl(1, 8)), False, True)], 8 * 112, ["Jp", "Jn"] + k_("Nn"), ["@pX:d"])
+            act(B("dr"), pX[:, 32:48, 0:7], 7 * NB, ["@pX:d"], k_("dr"))
+        if "4" not in OPT:
+            mm([(pP, B("Zw", sl(15 - r, 143 - r)), B("MN", sl(2 * L * t + L + r, 2 * L * t + 2 * L, 16)), r == 0, r == 15) for r in range(16)], 1024, k_("Zw") + [kn], k_("@pX:p"))
+            act(B("pre"), pP, NB, k_("@pX:p", "c0"), k_("pre"), scale=-1.0, bias=B("wcol", sl(3, 4)))
+        m = VB // 16
+        mm([(pC[:, nb], T.I[:], T.th9[:], True, False)] +
+           [(pC[:, u:NB:m], T.Z[:, 15 - r:143 - r], B("V", al, sl(144 * u + 9 * r + 1, 144 * u + 9 * r + 9)), False, r == 15 and u == m - 1) for u in range(m) for r in range(16)],
+           K8 + 16 * m * max(64, K8 // m), ["Z"] + TH9 + VK, ["@pC:c"])
+        act(B("s1"), pC[:, nb], K8, ["@pC:c"], k_("s1"), F.Sign)
+        S1 = k_("s1")
+        mm([(pQ, T.I[:], T.b144[:], True, False), (pQ, T.I[:], T.r9[:], False, False), (pQ, T.Ih[:], T.c9[:], False, False)] +
+           [(pQ, T.Ih[:], B("s1", al, k), False, k == 6) for k in range(7)], 640, S1 + ["b144", "r9", "c9"], k_("@pC:q"))
+        cp(B("oa"), pQ, NB, k_("@pC:q"), k_("oa"))
+        tt(B("v2"), B("es").indirect(B("oa")), B("v1"), A.min, gat(L), ES + k_("oa", "v1"), k_("v2"))
+        act(B("ne"), B("s1", al, 7), NB, S1, k_("ne"), scale=-0.5, bias=0.5)
+        act(B("t1"), B("s1"), K8, S1, k_("t1"), F.Relu)
+        mm([(pX[:, 48:64, j], T.I[:], B("ne"), True, True) for j in range(7)], 7 * 64, k_("ne"), ["@pX:m"])
+        mm([(pX[:, 26:28], T.ones[:], B("ne"), True, True),
+            (pX[:, 28:30], T.I[:], T.bL[:], True, False), (pX[:, 28:30], T.IL[:], B("ne"), False, True),
+            (pX[:, 30:32], T.I[:], T.b144[:], True, False), (pX[:, 30:32], T.I[:], T.r9[:], False, False), (pX[:, 30:32], T.I2[:], B("ne"), False, True)],
+           6 * 64, k_("ne") + ["IL", "I2", "bL"], ["@pX:e"])
+        tt(pN[:, nb, 8:15], pX[:, 48:64, 0:7], B("dr"), A.mult, 7 * NB, ["@pX:m"] + k_("dr"), ["@pN:t"])
+        ts(B("eo"), pX[:, 28:30], T.col[:, 0:1], None, A.add, None, NB, ["@pX:e", "r"], k_("eo"))
+        act(B("d3", sl(1, K8, 8)), pX[:, 30:32], NB, ["@pX:e"] + k_("d3"), k_("d3"), bias=2.0)
+        if not last:
+            act(B("junk"), pX[:, 26:28], NB, ["@pX:e"], k_("cnt"), scale=-1.0, bias=128.0, accum_out=T.cnt[:, h:h + 1])
+
+        def turn(n, tk, keys):
+            tm, fr = "tm%d" % n, "fr%d" % n; front = B("fr", n - 1, sl(7, K8, 8))
+            tt(B("tm", n - 1, sl(1, K8 + 1)), tk, pN[:, nb, 9 - n:17 - n], A.mult, K8, keys + ["@pN:t"], k_(tm))
+            scan(B("fr", n - 1), T.m8[:], B("tm", n - 1, sl(1, K8 + 1)), 0.0, A.mult, A.subtract, K8, ["m8"] + k_(tm), k_(fr))
+            if n < 3:
+                act(pN[:, nb, 8 - n], front, NB, k_(fr), ["@pN:t"])
+            if n == 1:
+                mm([(pF, T.Jp[:], B("Nn"), True, False)], 4 * K8, k_("Nn", tm), ["@pN:f"])
+            if "5" in OPT and n < 3:
+                act(B("tm", n - 1, sl(0, K8, 8)), front, NB, k_(fr, tm), k_(tm))
+            mm([(pF, T.Jp[:], B("tm", n - 1, sl(0, K8)), False, False)], 4 * K8, k_(tm) + ["tm0"], ["@pN:f"])
+            if "5" not in OPT or n == 3:
+                mm([(pF0, T.Jp[:], front, False, n == 3)], 256, k_(fr), ["@pN:f"])
+
+        def count(n, v, out):
+            u = 32.0 ** (-7 - n)
+            ts(B("LH", al, 0), B(v), u, u * 2.0 ** 20, A.max, A.min, L // 2, k_(v), k_("LHa"))
+            act(B("LH", al, 1), B(v), L, k_(v), k_("LHb"), F.Relu, scale=2.0 ** -20)
+            w = pC[:, 20:24]
+            mm([(w, T.Z[:, 15 - r:143 - r], B("LH", al, al, r), r == 0, r == 15) for r in range(16)], 1024, k_("LHa", "LHb"), ["@pC:n"])
+            ts(B("Ti"), w, 1.0 / u / 31, 7 * 33825 - 8.0 / 31, A.mult, A.add, 2 * NB, ["@pC:n"], k_("Ti"))
+            for j in range(4):
+                ts(out(j), B("Ti"), 4 + 5 * j, 1, A.logical_shift_right, A.bitwise_and, 2 * NB, k_("Ti"), k_("t%d%d" % (n, j)))
+            return k_(*["t%d%d" % (n, j) for j in range(4)])
+
+        turn(1, B("t1"), k_("t1"))
+        ts(B("v2c"), B("v2"), 32.0 ** -9, None, A.max, None, L // 2, k_("v2"), k_("v2c"))
+        T2 = count(2, "v2", lambda j: B("t2", sl(j, K8, 4)))
+        scan(B("q2"), T.d2[:], B("t2"), -8.0, A.max, A.add, K8, ["d2"] + T2, k_("q2"))
+        cp(B("ob"), B("q2", sl(7, K8, 8)), NB, k_("q2"), k_("ob"))
+        tt(B("v3"), B("es").indirect(B("ob")), B("v2c"), A.min, gat(L), ES + k_("ob", "v2c"), k_("v3"))
+        act(B("g1"), B("es").indirect(B("ob")), gat(L), ES + k_("ob"), k_("g1"))
+        turn(2, B("t2"), T2)
+        T3 = count(3, "v3", lambda j: B("t3", sl(8 + j, K8 + 8, 4)))
+        t3, t30 = B("t3", sl(8, K8 + 8)), B("t3", sl(8, K8 + 8, 8))
+        scan(B("Q3", sl(0, K8)), B("d3"), t3, -8.0, A.max, A.add, K8, k_("d3") + T3, k_("q3"))
+        tt(B("o2f"), pQ, t30, A.mult, NB, k_("@pC:q") + T3[:1], k_("o2f"))
+        tt(B("Q3", sl(K8 + 6, 2 * K8, 8)), B("o2f"), T.base[:], A.max, 2 * NB, k_("o2f") + ["base"], k_("o2g"))
+        cp(B("oo"), B("Q3", sl(6, 2 * K8, 8)), 2 * NB, k_("q3", "o2g"), k_("oo"))
+        turn(3, t3, T3)
+        tt(t30, t30, B("t2", sl(0, K8, 8)), A.mult, 2 * NB, T3[:1] + T2[:1], T3[:1])
+        act(Fin, pF, K8, ["@pN:f"], k_("Fin%d" % t))
+        if not MERGE:
+            send(B("C", sl(MW * t + MW, MW * t + MW + K8)), Fin, "rc%d%d" % (t, h), t, k_("Fin%d" % t), ["C%d%d" % (t + 1, h)])
+        tt(B("g2"), B("E").indirect(B("oo", nb)), B("g1"), A.min, gat(L), EK + k_("oo", "g1"), k_("g2"))
+        tt(B("g3"), B("es").indirect(B("oo", sl(NB, 2 * NB))), B("g2"), A.min, gat(L), ES + k_("oo", "g2"), k_("g3"))
+        pv, pm = T.pV[:, 0:L], T.pV[:, L:2 * L]
+        if "4" in OPT:
+            pm = T.pC[:, 32:64]
+            mm([(pm, T.I[:], npr, True, False), (pm, T.In[:], B("g3"), False, True)], 2 * L, [kn] + k_("g3"), ["@pC:m"])
+            act(B("MN", sl(2 * L * t, 2 * L * t + L)), pm, L, ["@pC:m"], k_("Mp"), bias=1.0)
+            mm([(pS, B("Zw", sl(15 - r, 143 - r)), B("MN", sl(2 * L * t + r, 2 * L * t + L, 16)), r == 0, r == 15) for r in range(16)], 1024, k_("Zw", "Mp"), ["@pX:s"])
+        else:
+            mm([(pS, B("Zw", sl(15 - r, 143 - r)), B("g3", sl(r, L, 16)), r == 0, r == 15) for r in range(16)], 1024, k_("Zw", "g3"), ["@pX:s"])
+        mm([(pv, T.In[:], npr, True, False)], L, ["In", kn], ["@pV:v"])
+        mm([(pv, T.Ih[:], B("g3"), False, True)], L, ["Ih"] + k_("g3"), ["@pV:v"])
+        act(B("vf"), pv, L, ["@pV:v"], k_("vf"), scale=1.0 - 2.0 ** -10, bias=MAGIC + 255.0)
+        if "4" not in OPT:
+            mm([(pm, T.I[:], npr, True, False), (pm, T.In[:], B("g3"), False, True)], 2 * L, [kn] + k_("g3"), ["@pV:m"])
+            act(B("MN", sl(2 * L * t, 2 * L * t + L)), pm, L, ["@pV:m"], k_("Mp"), bias=1.0)
+        act(B("val"), B("vf"), L, k_("vf"), k_("val"), bias=-MAGIC)
+        ms = B("ms", sl(L * t, L * t + L)); mw = B("MN", sl(2 * L * t, 2 * L * t + 2 * L)).indirect(B("eo"))
+        if MERGE:
+            act(B("Fin", sl(MW * t + K8, MW * t + MW)), mw, gat(L), k_("Mp", "eo") + [kn], k_("ms%d" % t))
+            send(B("C", sl(MW * t + MW, MW * t + 2 * MW)), B("Fin", sl(MW * t, MW * t + MW)), "rc%d%d" % (t, h), t, k_("Fin%d" % t, "ms%d" % t), ["C%d%d" % (t + 1, h)])
+        else:
+            act(ms, mw, gat(L), k_("Mp", "eo") + [kn], k_("ms%d" % t), **({"scale": -1.0, "bias": 256.0} if last else {}))
+            send(B("N4") if last else B("MN", sl(2 * L * t + 3 * L, 2 * L * t + 4 * L)), ms, "rn%d%d" % (t, h), t, k_("ms%d" % t), ["n%d%d" % (t + 1, h)])
+        if "4" in OPT:
+            ts(B("si"), pS, -1.0, 262144.0, A.mult, A.add, NB, ["@pX:s"], k_("si"))
+        else:
+            tt(B("si"), pS, B("pre"), A.add, NB, ["@pX:s"] + k_("pre"), k_("si"))
+        ts(B("sj"), B("si"), 7, None, A.bitwise_and, None, NB, k_("si"), k_("sj"))
+        tt(B("sk"), B("sj"), T.lane8[:], A.add, 2 * NB, k_("sj") + ["lane8"], k_("sk"))
+        cp(B("po"), B("sk"), NB, k_("sk"), k_("po"))
+        cp(B("X").indirect(B("po")), B("val"), ("s", L), k_("po", "val"), XK + k_("Xw"))
+        W = 4096 // NP
+        if last:
+            for s in range(NP):
+                dma("sa"[s * h], T.yx[PB * h:PB * h + PB, W * s:W * s + W], T.X[PB * s:PB * s + PB, 4096 * h + W * s:4096 * h + W * s + W], 512, k_("Xw"), [])
+        else:
+            for s in range(NP):
+                cols = sl(4096 * h + W * s, 4096 * h + W * s + W); s2 = 1 - s
+                dma("s", T.X[PB * s2:PB * s2 + PB, cols], T.X[PB * s:PB * s + PB, cols], 512, k_("Xw"), [XK[s2]])
+        if "1" in OPT:
+            tt(pG, pF, C, A.subtract, K8, ["@pN:f", kC], ["@pN:g"])
+            tt(pG, pG, B("t3", sl(7, K8 + 7)), A.mult, K8, ["@pN:g", "t30"] + T3, ["@pN:g"])
+            tt(B("Pn"), pG, C, A.add, K8, ["@pN:g", kC], k_("Pn"))
+            act(B("Pn", al, 0), B("Fin", sl(MW * t, MW * t + K8, 8)), NB, k_("Fin%d" % t, "Pn"), k_("Pn"))
+            if not last:
+                ts(B("poff"), B("Pn"), 2048.0, None, A.add, None, K8, k_("Pn"), k_("poff"))
+            return
+        if "7" in OPT:
+            tt(B("kx"), pF, C, A.subtract, K8, ["@pN:f", kC], k_("kx"))
+            tt(B("kw"), B("kx"), B("t3", sl(7, K8 + 7)), A.mult, 2 * K8, ["t30"] + k_("kx") + T3, k_("kw"))
+            act(B("kw", al, 0), B("kx", al, 0), NB, k_("kw", "kx"), k_("kw"))
+        else:
+            mm([(pG, T.Jp[:], Fin, True, False), (pG, T.Jn[:], C, False, True)], 8 * K8, k_("Fin%d" % t) + [kC], ["@pN:g"])
+            tt(B("kw"), pG, B("t3", sl(7, K8 + 7)), A.mult, K8, ["@pN:g", "t30"] + T3, k_("kw"))
+            act(B("kw", al, 0), pN[:, 24:32, 0::8], NB, ["@pN:g"] + k_("kw"), k_("kw"))
+        mm([(pG, T.Jp[:], B("kw"), True, False), (pG, T.Jp[:], C, False, True)], 8 * K8, k_("kw") + [kC], ["@pN:g"])
+        if not last:
+            ts(B("poff"), pG, 2048.0, None, A.add, None, K8, ["@pN:g"], k_("poff"))
+        act(B("Pn"), pG, K8, ["@pN:g"], k_("Pn"))
+
+    def limit():
+        ts(T.coli[:, 4:5], T.cnt[:, 0:1], T.cnt[:, 1:2], None, A.add, None, 1, ["cnt0", "cnt1"], ["ai"])
+        ts(T.coli[:, 5:6], T.coli[:, 4:5], 63, None, A.bitwise_and, None, 1, ["ai"], ["aj"])
+        for h in range(NP):
+            B = view(h)
+            ts(B("wcol", sl(4, 5)), T.coli[:, 5:6], B("wcol", sl(1, 2)), 0.5, A.add, A.mult, 1, ["aj", "th%d" % h], ["thr%d" % h])
+
+    def names_out(h, j, src, key, out):
+        B = view(h); s_ = "%d%d" % (h, j); ky = ["@pD:y", "@pD:z"] if j else ["@pD:00", "@pD:01", "@pD:10", "@pD:11"]
+        for k in range(8):
+            act(B("Yk", 8 * j + k), src(k), NB, [key], ["Yk%s%d" % (s_, k)], bias=2048.0)
+        mm([(T.pD[0:PB, 16 * j + s:16 * j + 16:2, :], T.Jp[:, PB * s:PB * s + PB], B("Yk", sl(8 * j, 8 * j + 8)), True, True) for s in range(NP)],
+           4 * 128 * NP, ["Yk%s%d" % (s_, k) for k in range(8)], ky)
+        o = T.Yo[0:PB, 512 * h + 256 * j:512 * h + 256 * j + 256]
+        act(o, T.pD[0:PB, 16 * j:16 * j + 16, :], 256, ky, ["Yo" + s_])
+        dma("sa"[j * h], out[PB * h:PB * h + PB, :], o, 64, ["Yo" + s_], [])
+
+    for t in range(RO):
+        for part in (head, tail):
+            for h in range(NP):
+                lead[0] = NP * t + h
+                part(t, h)
+        if t < RO - 1:
+            limit()
+    for h in range(NP):
+        B = view(h)
+        names_out(h, 0, lambda k: B("Pn", al, k), "Pn%d" % h, T.yp)
+        names_out(h, 1, lambda k: B("C", sl(MW * RO + k, MW * RO + K8, 8)), "C%d%d" % (RO, h), T.yc)
+        if MERGE:
+            act(B("N4"), B("C", sl(MW * RO + K8, MW * RO + MW)), L, ["C%d%d" % (RO, h)], ["n%d%d" % (RO, h)], scale=-1.0, bias=256.0)
+        for s in range(NP):
+            dma("sa"[s * h], T.yn[PB * h:PB * h + PB, L * s:L * s + L], T.N4[PB * s:PB * s + PB, L * h:L * h + L], 32, ["n%d%d" % (RO, h)], [])
+
+    cnt = {q: 0 for q in "vatp"}
     seen = {q: {} for q in Q}
-    lastw, readers, total = {}, {}, {}
+    total = {"sent": sent[0]}
 
     def need(q, sem, n):
         if seen[q].get(sem, 0) < n:
             Q[q].wait_ge(T.sem[sem], n)
             seen[q][sem] = n
-
-    def deps(q, rd, wr):
-        want = {}
-        for k in rd:
-            if k in lastw and not (q == "t" and lastw[k][0] == "t"):
-                s, n = lastw[k]; want[s] = max(want.get(s, 0), n)
-        for k in list(wr) + [k for k in rd if k[0] == "@"]:
-            for s, n in list(readers.get(k, {}).items()) + ([lastw[k]] if k in lastw else []):
-                if s != q:
-                    want[s] = max(want.get(s, 0), n)
-        for k in wr:
-            if q != "t" and q in readers.get(k, {}):
-                want[q] = max(want.get(q, 0), readers[k][q])
+    if not PLAN:
+        PLAN.extend(order(ops))
+    for i in PLAN[0]:
+        o = ops[i]; q = o["q"]; want = {}
+        o["pre"].update({j: True for j in PLAN[1].get(i, [])})
+        for j, w in o["pre"].items():
+            if w:
+                s, n = ops[j]["at"]
+                want[s] = max(want.get(s, 0), n)
         for s, n in want.items():
             need(q, s, n)
-
-    def done(sem, n, rd, wr):
-        for k in rd:
-            readers.setdefault(k, {})[sem] = n
-        for k in wr:
-            lastw[k] = (sem, n); readers[k] = {}
-        total[sem] = n
-
-    def op(q, fn, rd, wr):
-        deps(q, rd, wr)
-        cnt[q] += 1
-        fn().then_inc(T.sem[q], 1)
-        done(q, cnt[q], rd, wr)
-
-    def mm(calls, rd, wr):
-        deps("t", rd, wr)
-        for a in calls[:-1]:
-            PE.matmul(*a)
-        cnt["t"] += 1
-        PE.matmul(*calls[-1]).then_inc(T.sem.t, 1)
-        done("t", cnt["t"], rd, wr)
-
-    def dma(q, sem, out, in_, rd, wr):
-        deps(q, rd, wr)
-        Q[q].dma_start(out, in_).then_inc(T.sem[sem], 16)
-        done(sem, 16, rd, wr)
-
-    def ts(o, i, s1, s2, o0, o1, rd, wr):
-        if o1 is None:
-            op("v", lambda: V.tensor_scalar(o, i, s1, None, o0), rd, wr)
+        if o["sig"] is None:
+            calls = o["fn"]()
+            for call in calls if isinstance(calls, list) else [calls]:
+                cnt[q] += 1
+                call.then_inc(T.sem[q], 1)
+            o["at"] = (q, cnt[q])
         else:
-            op("v", lambda: V.tensor_scalar(o, i, s1, s2, o0, o1), rd, wr)
-
-    def tt(o, a, b, f, rd, wr):
-        op("v", lambda: V.tensor_tensor(o, a, b, f), rd, wr)
-
-    def cp(o, i, rd, wr):
-        op("v", lambda: V.tensor_copy(o, i), rd, wr)
-
-    def fill(o, c, wr, rd=()):
-        op("v", lambda: V.memset(o, c), rd, wr)
-
-    def act(o, i, rd, wr, f=F.Identity, **k):
-        op("a", lambda: S.activation(o, i, f, **k), rd, wr)
-
-    def send(dst_ap, src_ap, sem, t, rd):
-        to = T.cores[(rank + 1 + t % 3) % N]
-        rid, pid, _ = topo.addr(to)
-        deps("p", rd, [])
-        g.remote_dma(dst_ap, src_ap, T.sem[sem], T.sem.sent, pid, rid, topo.mask(core, to))
-        total["sent"] = total.get("sent", 0) + len(topo.engines(core, to))
-
-    def arrival(sem, t, key):
-        fr = T.cores[(rank - 1 - t % 3) % N]
-        lastw[key] = (sem, len(topo.engines(fr, core))); total[sem] = lastw[key][1]
-
-    H = range(NH)
-    PNK = ["Pn%d" % h for h in H]
-    dma("s", "lp", T.pin[:], T.pn[:], [], ["pin"])
-    dma("a", "lx0", T.X[:, 0:2048], T.lit[:, 0:2048], [], ["Xa"])
-    dma("s", "lx1", T.X[:, 2048:4096], T.lit[:, 2048:4096], [], ["Xb"])
-    dma("a", "lc", T.cin[:], T.cn[:], [], ["cin"])
-    dma("s", "ln", T.nin[:], T.neg[:], [], ["nin"])
-    dma("a", "lw", T.win[:], T.wt[:], [], ["win"])
-    dma("s", "lt", T.tin[0:1, :], T.th[:], [], ["tin"])
-    XK = ["Xa", "Xb"]
-    fill(T.ones[:], 1.0, ["ones"])
-    fill(T.G0[:], 1.0, ["G0"])
-    fill(T.Fm[:], -1024.0, ["Fm"])
-    op("p", lambda: g.iota(T.coli[:, 0:1], [[0, 1]], 0, 1), [], ["coli"])
-    op("p", lambda: g.iota(T.b16[:], [[16, 32]], 0, 0, allow_small_or_imprecise_dtypes=True), [], ["b16"])
-    op("p", lambda: g.affine_select(T.I[:], T.ones[:], [[-1, 128]], A.is_equal, 0.0, 0, 1), ["ones"], ["I"])
-    op("p", lambda: g.affine_select(T.G[:], T.G0[:], [[-16, 8]], A.is_ge, 0.0, 0, 1), ["G0"], ["G"])
-    op("p", lambda: g.affine_select(T.G[:], T.G[:], [[16, 8]], A.is_ge, 0.0, 15, -1), ["G"], ["G"])
-    op("p", lambda: g.partition_broadcast(T.tbc[:], T.tin[0:1, :], 128), ["tin"], ["tbc"])
-    op("p", lambda: g.affine_select(T.Fm[:], T.Fm[:], [[-2, 8], [-16, 8], [0, 16]], A.is_ge, 0.0, 0, 1), ["Fm"], ["Fm"])
-    op("p", lambda: g.affine_select(T.Fm[:], T.Fm[:], [[2, 8], [16, 8], [0, 16]], A.is_ge, 0.0, 1, -1), ["Fm"], ["Fm"])
-    op("p", lambda: g.affine_select(T.BO0[:], T.ones[:], [[-16, 8], [0, 16]], A.is_ge, 0.0, 0, 1), ["ones"], ["BO0"])
-    op("p", lambda: g.affine_select(T.BO[:], T.BO0[:], [[16, 8], [0, 16]], A.is_ge, 0.0, 15, -1), ["BO0"], ["BO"])
-    for z in ("Z", "Zh", "Zw", "Zs"):
-        fill(T[z][:], 0.0, [z])
-    fill(T.cR[:], -BIG, ["cR"])
-    fill(T.c25[:], 0.25, ["c25"])
-    for k in range(8):
-        ts(T.Pn[:, :, k], T.pin[:, 32 * k:32 * k + 32], -2048.0, None, A.add, None, ["pin"], PNK)
-    for h in H:
-        ts(T.poff[:, 8 * NB * h:8 * NB * (h + 1)], T.Pn[:, NB * h:NB * (h + 1), :], 2048.0, None, A.add, None, PNK, ["poff%d" % h])
-    for k in range(8):
-        ts(T.C0[:, :, k], T.cin[:, 32 * k:32 * k + 32], -2048.0, None, A.add, None, ["cin"], ["C0%d" % h for h in H])
-    for nm, sc in (("Isc", 1.0 / SC), ("In", -1.0), ("Ih", 0.5 / SC), ("Ip", 0.5), ("Im", -1.0 * NL)):
-        act(T[nm][:], T.I[:], ["I"], [nm], scale=sc)
-    act(T.Jp[:], T.I[:], ["I"], ["J"])
-    act(T.Jn[:], T.I[:], ["I"], ["J"], scale=-1.0)
-    for h in H:
-        act(T.MN0[:, 2 * NL * h + NL:2 * NL * (h + 1)], T.nin[:, NL * h:NL * (h + 1)], ["nin"], ["n0%d" % h], scale=-1.0, bias=255.0)
-
-    def consts_head():
-        ts(T.coli[:, 3:4], T.coli[:, 0:1], 1, None, A.bitwise_and, None, ["coli"], ["aj"])
-        ts(T.col[:, 4:5], T.coli[:, 3:4], -1.0, 1.0, A.mult, A.add, ["aj"], ["par"])
-        cp(T.col[:, 5:6], T.coli[:, 3:4], ["aj"], ["par"])
-        cp(T.Z[:, 15:143:16], T.G[:], ["G", "Z"], ["Z"])
-        ts(T.Zh[:, 15:143:16], T.G[:], -0.5, None, A.mult, None, ["G", "Zh"], ["Zh"])
-        tt(T.G0[:], T.tbc[:], T.G[:], A.mult, ["tbc", "G"], ["G0"])
-        fill(T.es[:, 4608:4624], BIG, ["ez"])
-        op("v", lambda: V.tensor_reduce(T.col[:, 3:4], T.G0[:], AX.X, A.add), ["G0"], ["th"])
-        fill(T.cR[:, 0::9], BIG, ["cR"], ["cR"])
-        ts(T.thr[:], T.col[:, 3:4], 0.5, None, A.mult, None, ["th"], ["thr"])
-        for k in range(9):
-            fill(T.cC[:, k::9], 32.0 ** k, ["cC"])
-
-    def consts_tail():
-        ts(T.coli[:, 1:2], T.coli[:, 0:1], 15, None, A.bitwise_and, None, ["coli"], ["coli"])
-        cp(T.col[:, 0:1], T.coli[:, 1:2], ["coli"], ["r"])
-        for s in (1, 2, 3):
-            fill(T["d%d" % s][:], -100.0, ["d%d" % s])
-        for s in (1, 2, 3):
-            fill(T["tm%d" % s][:, 0:1], 0.0, ["tm%d" % s])
-        fill(T.pn2[:, :, 10], 0.0, ["@pn2"])
-        ts(T.lb[:], T.b16[:], 1.0 * NL, None, A.add, None, ["b16"], ["lb"])
-        ts(T.lane8[:], T.b16[:], T.col[:, 0:1], 8.0, A.add, A.mult, ["b16", "r"], ["lane8"])
-        ts(T.base[:], T.b16[:], T.col[:, 0:1], 9.0, A.add, A.mult, ["b16", "r"], ["base"])
-        ts(T.col[:, 1:2], T.win[:], -1.0, None, A.mult, None, ["win"], ["nw"])
-        cp(T.wb[:, 0:1], T.win[:], ["win"], ["wb"])
-        ts(T.d1[:, 0::8], T.base[:, 0:NB], 1.0, None, A.add, None, ["base", "d1"], ["d1"])
-        mm([(T.pn2[:, 0, 15:16], T.BO[:], T.wb[:, 0:1], True, True)], ["BO", "wb"], ["@pn2"])
-        cp(T.d2[:, 0::8], T.base[:, 0:NB], ["base", "d2"], ["d2"])
-        cp(T.d3[:, 1::8], T.base[:, 0:NB], ["base", "d3"], ["d3"])
-        ts(T.Zw[:, 15:143:16], T.G[:], T.col[:, 1:2], None, A.mult, None, ["G", "nw", "Zw"], ["Zw"])
-        ts(T.Zs[:, 15:143:16], T.G[:], T.col[:, 1:2], -1.0 / SC, A.mult, A.mult, ["G", "nw", "Zs"], ["Zs"])
-        ts(T.col[:, 2:3], T.pn2[:, 0, 15:16], 254.0, None, A.mult, None, ["@pn2"], ["c0"])
-
-    def pside(h):
-        b = slice(NB * h, NB * (h + 1)); k = "Pn%d" % h
-        act(T.pn1[:, 0:256], T.Pn[:, b, :], [k], ["@pn1"], bias=3232.0)
-        act(T.pn1[:, 256:512], T.Pn[:, b, :], [k], ["@pn1"], bias=2048.0)
-        act(T.rp[:, b, :], T.Pn[:, b, :], [k], ["rp%d" % h], scale=2080.0, bias=-3801088.0)
-
-    def coffs(t, h):
-        ts(T.coff[:, 8 * NB * h:8 * NB * (h + 1)], T["C%d" % t][:, NB * h:NB * (h + 1), :], 2048.0, None, A.add, None, ["C%d%d" % (t, h)], ["coff%d" % h])
-
-    def joined(t, h):
-        b = slice(NB * h, NB * (h + 1)); b2 = slice(32 + NB * h, 32 + NB * (h + 1)); s = str(h)
-        tt(T.pn1[:, 0:256], T.pn1[:, 0:256], T["C%d" % t][:, b, :], A.mult, ["@pn1", "C%d%d" % (t, h)], ["@pn1"])
-        tt(T.hs[:, b, :], T.pn1[:, 0:256], T.rp[:, b, :], A.add, ["@pn1", "rp" + s], ["hs" + s])
-        ts(T.hi[:, b, :], T.hs[:, b, :], 5, 4095, A.arith_shift_right, A.bitwise_and, ["hs" + s], ["hi" + s])
-        cp(T.hoff[:, 8 * NB * h:8 * NB * (h + 1)], T.hi[:, b, :], ["hi" + s], ["hoff" + s])
-
-    def apart(c):
-        tt(T.hp[:], T.hi[:], T.pn1[:, 256:512], A.subtract, ["hi0", "@pn1"], ["hp"])
-
-    def limit(t):
-        if t > 0:
-            ts(T.coli[:, 2:3], T.cnt[:, 0:1], 4096.0, None, A.add, None, ["cnt0"], ["ai"])
-            ts(T.coli[:, 3:4], T.coli[:, 2:3], 63, None, A.bitwise_and, None, ["ai"], ["aj"])
-            ts(T.thr[:], T.coli[:, 3:4], T.col[:, 3:4], 0.5, A.add, A.mult, ["aj", "th"], ["thr"])
-
-    def nap(t, l0, n):
-        h = l0 // NL; o = 2 * NL * h + NL + l0 - NL * h
-        return T["MN%d" % t][:, o:o + n]
-
-    def gx(c):
-        e = slice(1024 * c, 1024 * c + 1024); o = slice(64 * c, 64 * c + 64); h = str(8 * c // NB); s = str(c)
-        act(T.xg[:, e], T.X[:].indirect(T.poff[:, o]), XK + ["poff" + h], ["x" + s])
-
-    def gy(c):
-        e = slice(1024 * c, 1024 * c + 1024); o = slice(64 * c, 64 * c + 64); h = str(8 * c // NB); s = str(c)
-        act(T.yg[:, e], T.X[:].indirect(T.coff[:, o]), XK + ["coff" + h], ["y" + s])
-
-    def gmx(c, early=False):
-        if early and c in ROUTE:
-            return
-        e = slice(1024 * c, 1024 * c + 1024); o = slice(64 * c, 64 * c + 64); h = str(8 * c // NB); s = str(c)
-        pD = T["pD%d" % (c % 2)]; k = "@pD%d" % (c % 2)
-        part = lambda z, src, first, last: [(pD[:, 0:8, :], T[z][:, 15 - r:143 - r], src[:, 1024 * c + r:1024 * c + 1024:16], first and r == 0, last and r == 15) for r in range(16)]
-        if c in ROUTE:
-            pe = T["pe%d" % (c % 2)]; ks = ["@pe%d0" % (c % 2), "@pe%d1" % (c % 2)]
-            hv = lambda src, u: src[:, 1024 * c + 512 * u:1024 * c + 512 * u + 512]
-            for u in range(2):
-                mm([(pe[:, 4 * u:4 * u + 4], T.I[:], hv(T.xg, u), True, False), (pe[:, 4 * u:4 * u + 4], T.In[:], hv(T.yg, u), False, True)], ["I", "In", "x" + s, "y" + s], [ks[u]])
-                act(hv(T.ad, u), pe[:, 4 * u:4 * u + 4], [ks[u]], ["ad%s%d" % (s, u)], F.Abs, scale=0.5)
-            for u in range(2):
-                mm([(pe[:, 4 * u:4 * u + 4], T.Ip[:], hv(T.xg, u), True, False), (pe[:, 4 * u:4 * u + 4], T.Ip[:], hv(T.yg, u), False, False),
-                    (pe[:, 4 * u:4 * u + 4], T.I[:], hv(T.ad, u), False, True)], ["Ip", "ad%s%d" % (s, u)], [ks[u]])
-                act(hv(T.mx, u), pe[:, 4 * u:4 * u + 4], [ks[u]], ["mx" + s])
-            mm(part("Z", T.ad, True, True), ["Z", "ad%s0" % s, "ad%s1" % s], [k])
-            return
-        ylast = c in LATE
-        if early:
-            mm(part("Zh", T.xg, True, False), ["Zh", "x" + s], [k])
-            if not ylast:
-                mm(part("Zh", T.yg, False, False), ["y" + s], [k])
-            return
-        tt(T.mx[:, e], T.X[:].indirect(T.coff[:, o]), T.xg[:, e], A.max, XK + ["coff" + h, "x" + s], ["mx" + s])
-        if ylast:
-            mm(part("Zh", T.yg, False, False), ["y" + s], [k])
-        mm(part("Z", T.mx, False, True), ["Z", "mx" + s], [k])
-
-    def glr(t, c):
-        e = slice(1024 * c, 1024 * c + 1024); o = slice(64 * c, 64 * c + 64); h = str(8 * c // NB); s = str(c)
-        late = c in LATE
-        pe = T["pe%d" % (c % 2)]
-        gather = lambda: tt(T.lr[:, e], T.X[:].indirect(T.hoff[:, o]), T.mx[:, e], A.min, XK + ["hoff" + h, "mx" + s], ["lr" + s])
-        if not late:
-            gather()
-        for u in range(2):
-            ts(T.ok2[:, o, u], T["pD%d" % (c % 2)][:, 0:8, :], T.thr[:], T.col[:, 4 + u:5 + u], A.is_le, A.mult, ["@pD%d" % (c % 2), "thr", "par"], ["ok2" + s])
-        if late:
-            gather()
-
-    def esum(t, c):
-        h = str(8 * c // NB); s = str(c); late = c in LATE
-        pe = T["pe%d" % (c % 2)]
-        lit = lambda u, first: [(pe[:, 4 * u:4 * u + 4], T.I[:], T.lr[:, 1024 * c + 512 * u:1024 * c + 512 * u + 512], first, not first)]
-        for u in range(2):
-            bk = slice(4 * u, 4 * u + 4); k = "@pe%d%d" % (c % 2, u)
-            mm(([(pe[:, bk], T.I[:], T.c25[:], True, False)] if late else lit(u, True)) +
-               [(pe[:, bk, j, :], T.I[:], nap(t, 128 * c + 64 * u, 64), False, False) for j in range(8)], ["I", "c25" if late else "lr" + s, "n%d%s" % (t, h)], [k])
-        for u in range(2):
-            bk = slice(4 * u, 4 * u + 4); k = "@pe%d%d" % (c % 2, u)
-            mm([(pe[:, bk, :, 2 * r:2 * r + 2], T.Fm[:, 128 * r:128 * r + 128], T.ok2[:, 64 * c + 32 * u:64 * c + 32 * u + 32, :], False, r == 7 and not late) for r in range(8)], ["Fm", "ok2" + s], [k])
-        for u in range(2 if late else 0):
-            mm(lit(u, False), ["lr" + s], ["@pe%d%d" % (c % 2, u)])
-
-    def evac(c):
-        pe = T["pe%d" % (c % 2)]
-        for j in range(8):
-            act(T.es[:, 1152 * c + 1 + j:1152 * c + 1152:9], pe[:, :, j, :], ["@pe%d0" % (c % 2), "@pe%d1" % (c % 2)], ["es%d" % c], scale=SC, bias=(769.75 if c in LATE else 770.0) * SC)
-
-    def scans(c):
-        e = slice(1152 * c, 1152 * c + 1152); s = str(c)
-        op("v", lambda: V.tensor_tensor_scan(T.E[:, e], T.cR[:], T.es[:, e], 0.0, A.max, A.min), ["cR", "ez", "es" + s], ["E" + s])
-        op("v", lambda: V.tensor_tensor_scan(T.V[:, e], T.E[:, e], T.cC[:], 1.0, A.max, A.min), ["cC", "E" + s], ["V" + s])
-
-    def tail(t, h):
-        s = str(h); b = slice(NB * h, NB * (h + 1)); b2 = slice(32 + NB * h, 32 + NB * (h + 1)); L = slice(NL * h, NL * (h + 1))
-        cs = range(4 * h // NH, 4 * (h + 1) // NH)
-        ES, EK, VK, OK = (["%s%d" % (k, c) for c in cs] for k in ("es", "E", "V", "ok2"))
-        ES = ES + ["ez"]
-        esw = T.es[:, 9 * NL * h:9 * NL * (h + 1) + 1]; Ew = T.E[:, 9 * NL * h:9 * NL * (h + 1)]; v1 = T.V[:, 9 * NL * h + 8:9 * NL * (h + 1):9]
-        pD = T["pD%d" % h]; kD = "@pD%d" % h; pe = T["pe%d" % h]; kM, kV = "@pe%d0" % h, "@pe%d1" % h
-        Ti = T.Ti[:, 2 * NB * h:2 * NB * (h + 1)]; w = NB // 8
-        C = T["C%d" % t]; Fin = T["Fin%d" % t]; MN = T["MN%d" % t]; kn = "n%d%d" % (t, h); kC = "C%d%d" % (t, h)
-        Mp = MN[:, 2 * NL * h:2 * NL * h + NL]; npr = nap(t, NL * h, NL)
-
-        def count(n, v, keys):
-            u = 32.0 ** (1 - n)
-            ts(T.LH[:, b, 0, :], v, u, u * 2.0 ** 20, A.max, A.min, keys, ["LHa" + s])
-            act(T.LH[:, b, 1, :], v, keys, ["LHb" + s], F.Relu, scale=2.0 ** -20, bias=-u)
-            mm([(pD[:, 0:2 * w, :], T.Z[:, 15 - r:143 - r], T.LH[:, b, :, r], r == 0, r == 15) for r in range(16)], ["LHa" + s, "LHb" + s, "Z"], [kD])
-
-        def decode(n):
-            tn = T["t%d" % n]; k = "t%d%s" % (n, s)
-            ts(Ti, pD[:, 0:2 * w, :], 32.0 ** (n - 1) / 31, 7 * 33825 - 8.0 / 31, A.mult, A.add, [kD], ["Ti" + s])
-            for j in range(4):
-                if n == 3 and j == 3:
-                    ts(tn[:, 3::8], T.Ti[:, 0:64:2], 19, 1, A.logical_shift_right, A.bitwise_and, ["Ti" + s], [k])
-                else:
-                    ts(tn[:, j::4], Ti, 4 + 5 * j, 1, A.logical_shift_right, A.bitwise_and, ["Ti" + s], [k])
-            if n < 3:
-                place(n)
-
-        def place(n):
-            op("v", lambda: V.tensor_tensor_scan(T["q%d" % n][:], T["d%d" % n][:], T["t%d" % n][:], -8.0, A.max, A.add), ["t%d%s" % (n, s), "d%d" % n], ["q%d%s" % (n, s)])
-
-        def turn(n, out, src, ko, ks):
-            tm = T["tm%d" % n]; k = "tm%d" % n
-            tt(tm[:, 1:257], T["t%d" % n][:], T.pn2[:, b, 4 - n:12 - n], A.mult, ["t%d%s" % (n, s), "@pn2", k], [k])
-            if n < 3:
-                mm([(T.pn2[:, b, 3 - n], T.Jn[:], tm[:, m:256:8], m == 1, m == 7) for m in range(1, 8)], ["J", k], ["@pn2"])
-                act(T.pat[:, 32 * n - 32:32 * n], T.pn2[:, b, 3 - n], ["@pn2"], ["pat%d" % n])
-                mm(([(T.pn1[:, 0:256], T.Jp[:], T.Nn[:], True, False)] if n == 1 else [(T.pn1[:, 0:256:8], T.Jp[:], T.pat[:, 0:32], False, False)]) +
-                   [(T.pn1[:, 0:256], T.Jp[:], tm[:, 0:256], False, False)], [k, "Nn0"] + (["pat1"] if n == 2 else []), ["@pn1"])
-            else:
-                mm([(T.pn1[:, 0:256:8], T.Jp[:], T.pat[:, 32:64], False, False)], ["pat2"], ["@pn1"])
-                mm([(T.pn1[:, 0:256:8], T.Jn[:], tm[:, m:256:8], False, False) for m in range(1, 8)] + [(T.pn1[:, 0:256], T.Jp[:], tm[:, 0:256], False, True)], [k], ["@pn1"])
-                act(out, T.pn1[:, 0:256], ["@pn1"], [ko])
-
-        mm([(T.pD0[:, 32:64, :], T.I[:], T.ok2[:, :, u], u == 0, u == 1) for u in range(2)], OK, ["@pD0"])
-        tt(T.pn1[:, 256:512], T.pD0[:, 32:64, :], T.hp[:], A.mult, ["@pD0", "hp"], ["@pn1"])
-        tt(T.Nn[:, b, :], T.Pn[:, b, :], T.pn1[:, 256:512], A.add, ["Pn" + s, "@pn1"], ["Nn" + s])
-        yield
-        count(1, v1, VK)
-        ts(T.v3c[:, L], v1, 2.0 ** 30, None, A.min, None, VK, ["v1c" + s])
-        tt(T.dr[:, b, 0:7], T.Nn[:, b, 0:7], T.Nn[:, b, 1:8], A.subtract, ["Nn" + s], ["dr" + s])
-        act(T.pn1[:, 256:512], C[:, b, :], [kC], ["@pn1"])
-        mm([(pe[:, 4:4 + w], T.I[:], T.c25[:, 0:NL], True, False), (pe[:, 4:4 + w], T.In[:], npr, False, False)], ["In", "c25", kn], [kV])
-        mm([(pe[:, 0:w], T.In[:], npr, True, False)], [kn], [kM])
-        yield
-        decode(1)
-        cp(T.oa[:, b], T.q1[:, 7::8], ["q1" + s], ["oa" + s])
-        ts(T.ne[:, b], T.t1[:, 7::8], -1.0, 1.0, A.mult, A.add, ["t1" + s], ["ne" + s])
-        tt(T.v2[:, L], esw.indirect(T.oa[:, b]), T.v3c[:, L], A.min, ES + ["v1c" + s, "oa" + s], ["v2" + s])
-        pX, kX = (T.pD1, "@pD1") if NH == 1 else (pD, kD)
-        mm([(pX[:, 32:32 + NB, j], T.I[:], T.ne[:, b], True, True) for j in range(7)] +
-           [(pX[:, 8:8 + w, :], T.ones[:], T.ne[:, b], True, True),
-            (pX[:, 12:12 + w, :], T.Im[:], T.ne[:, b], True, False), (pX[:, 12:12 + w, :], T.I[:], T.lb[:, 0:NB], False, True)], ["ne" + s, "I", "Im", "lb", "ones"], [kX])
-        n0 = 2 * NL * h + NL
-        mm([(pX[:, 16:16 + w, :], T.Zw[:, 15 - r:143 - r], MN[:, n0 + r:n0 + NL:16], r == 0, False) for r in range(16)], ["Zw", kn], [kX])
-        count(2, T.v2[:, L], ["v2" + s])
-        ts(T.v2c[:, L], T.v2[:, L], 2.0 ** -5, None, A.max, None, ["v2" + s], ["v2c" + s])
-        tt(T.pn2[:, b, 3:10], pX[:, 32:32 + NB, 0:7], T.dr[:, b, 0:7], A.mult, [kX, "dr" + s], ["@pn2"])
-        if t < RO - 1:
-            act(T.junk[:, b], pX[:, 8:8 + w, :], [kX], ["cnt" + s], scale=-1.0, accum_out=T.cnt[:, h:h + 1])
-        turn(1, None, None, None, None)
-        yield
-        decode(2)
-        cp(T.ob[:, b], T.q2[:, 7::8], ["q2" + s], ["ob" + s])
-        tt(T.v3[:, L], esw.indirect(T.ob[:, b]), T.v2c[:, L], A.min, ES + ["v2c" + s, "ob" + s], ["v3" + s])
-        act(T.g1[:, L], esw.indirect(T.ob[:, b]), ES + ["ob" + s], ["g1" + s])
-        count(3, T.v3[:, L], ["v3" + s])
-        turn(2, None, None, None, None)
-        tt(T.oan[:, b], T.q1[:, 7::8], T.ne[:, b], A.mult, ["q1" + s, "ne" + s], ["oan" + s])
-        ts(T.eo[:, b], pX[:, 12:12 + w, :], T.col[:, 0:1], None, A.add, None, [kX, "r"], ["eo" + s])
-        ts(T.t3[:, 7::8], T.t1[:, 7::8], 2.0, None, A.mult, None, ["t1" + s], ["t3" + s])
-        if t < RO - 1:
-            limit(t + 1)
-        yield
-        decode(3)
-        tt(T.o2f[:, b], T.oan[:, b], T.t3[:, 0::8], A.mult, ["oan" + s, "t3" + s], ["o2f" + s])
-        tt(T.t3[:, 0::8], T.t3[:, 0::8], T.t2[:, 0::8], A.mult, ["t3" + s, "t2" + s], ["t3" + s])
-        tt(T.o2g[:, b], T.o2f[:, b], T.base[:, 0:NB], A.max, ["o2f" + s, "base"], ["o2g" + s])
-        turn(3, Fin[:, b, :], None, "Fin" + s, None)
-        send(T["C%d" % (t + 1)][:, b, :], Fin[:, b, :], "rc%d%d" % (t, h), t, ["Fin" + s])
-        arrival("rc%d%d" % (t, h), t, "C%d%d" % (t + 1, h))
-        place(3)
-        cp(T.o2[:, b], T.o2g[:, b], ["o2g" + s], ["o2" + s])
-        cp(T.o3[:, b], T.q3[:, 7::8], ["q3" + s], ["o3" + s])
-        tt(T.g2[:, L], Ew.indirect(T.o3[:, b]), T.g1[:, L], A.min, EK + ["o3" + s, "g1" + s], ["g2" + s])
-        tt(T.g3[:, L], esw.indirect(T.o2[:, b]), T.g2[:, L], A.min, ES + ["o2" + s, "g2" + s], ["g3" + s])
-        mm([(pe[:, 4:4 + w], T.Ih[:], T.g3[:, L], False, True)], ["Ih", "g3" + s], [kV])
-        mm([(pX[:, 16:16 + w, :], T.Zs[:, 15 - r:143 - r], T.g3[:, NL * h + r:NL * (h + 1):16], False, r == 15) for r in range(16)], ["Zs", "g3" + s], [kX])
-        mm([(pe[:, 0:w], T.Isc[:], T.g3[:, L], False, True)], ["Isc", "g3" + s], [kM])
-        def values():
-            act(T.vf[:, L], pe[:, 4:4 + w], [kV], ["vf" + s], bias=MAGIC + 254.0)
-            act(T.val[:, L], T.vf[:, L], ["vf" + s], ["val" + s], bias=-MAGIC)
-        if t < RO - 1:
-            values()
-        act(Mp, pe[:, 0:w], [kM], ["Mp" + s], scale=-1.0, bias=1.0)
-        mw = MN[:, 2 * NL * h:2 * NL * (h + 1)].indirect(T.eo[:, b])
-        if t < RO - 1:
-            act(T["ms%d" % t][:, L], mw, ["Mp" + s, kn, "eo" + s], ["ms" + s])
-            send(nap(t + 1, NL * h, NL), T["ms%d" % t][:, L], "rn%d%d" % (t, h), t, ["ms" + s])
-        else:
-            act(T["ms%d" % t][:, L], mw, ["Mp" + s, kn, "eo" + s], ["ms" + s], scale=-1.0, bias=255.0)
-            send(T.N4[:, L], T["ms%d" % t][:, L], "rn%d%d" % (t, h), t, ["ms" + s])
-            values()
-        arrival("rn%d%d" % (t, h), t, "n%d%d" % (t + 1, h))
-        yield
-        tt(T.pn1[:, 256:512], Fin[:, b, :], T.pn1[:, 256:512], A.subtract, ["Fin" + s, "@pn1"], ["@pn1"])
-        tt(T.pn1[:, 257:512], T.t3[:, 0:255], T.pn1[:, 257:512], A.mult, ["t3" + s, "@pn1"], ["@pn1"])
-        tt(T.Pn[:, b, :], C[:, b, :], T.pn1[:, 256:512], A.add, [kC, "@pn1"], ["Pn" + s])
-        ts(T.si[:, b], pX[:, 16:16 + w, :], T.col[:, 2:3], None, A.add, None, [kX, "c0"], ["si" + s])
-        cp(T.Pn[:, b, 0], Fin[:, b, 0], ["Fin" + s, "Pn" + s], ["Pn" + s])
-        ts(T.sj[:, b], T.si[:, b], 7, None, A.bitwise_and, None, ["si" + s], ["sj" + s])
-        tt(T.sk[:, b], T.sj[:, b], T.lane8[:, 0:NB], A.add, ["sj" + s, "lane8"], ["sk" + s])
-        if t < RO - 1 or NH == 2:
-            xk = XK if NH == 1 else [XK[h]]
-            cp(T.po[:, b], T.sk[:, b], ["sk" + s], ["po" + s])
-            if t < RO - 1:
-                ts(T.poff[:, 8 * NB * h:8 * NB * (h + 1)], T.Pn[:, b, :], 2048.0, None, A.add, None, ["Pn" + s], ["poff" + s])
-            cp(T.X[:, 8 * NL * h:8 * NL * (h + 1)].indirect(T.po[:, b]), T.val[:, L], ["po" + s, "val" + s], xk)
-            if t == RO - 1:
-                dma("s", "sx" + s, T.yx[:, 8 * NL * h:8 * NL * (h + 1)], T.X[:, 8 * NL * h:8 * NL * (h + 1)], xk, [])
-        else:
-            for u in range(4):
-                ts(T.po[:, 8 * u:8 * u + 8], T.sk[:, 8 * u:8 * u + 8], -1024.0 * u, None, A.add, None, ["sk0"], ["po%d" % u])
-            for u in range(4):
-                e = slice(1024 * u, 1024 * u + 1024)
-                cp(T.X[:, e].indirect(T.po[:, 8 * u:8 * u + 8]), T.val[:, 128 * u:128 * u + 128], ["po%d" % u, "val0"], ["Xq%d" % u] + (XK if u == 0 else []))
-                dma("s", "sx%d" % u, T.yx[:, e], T.X[:, e], ["Xq%d" % u], [])
-        if t < RO - 1:
-            pside(h)
-        yield
-
-    for h in H:
-        pside(h)
-    for t in range(RO):
-        gx(0)
-        coffs(t, 0)
-        gy(0)
-        joined(t, 0)
-        if t == 0:
-            consts_head()
-        rest = tail(t, 0)
-
-        def slot0(c):
-            act(T.es[:, 0:9 * NL:9], nap(t, 0, NL), ["n%d0" % t, "ez"], ["ez"], scale=SC, bias=SC)
-
-        def names(c):
-            next(rest)
-            if t == 0:
-                consts_tail()
-        step = {"x": gx, "y": gy, "d": lambda c: gmx(c, True), "m": gmx, "l": lambda c: glr(t, c), "e": lambda c: esum(t, c),
-                "v": evac, "s": scans, "z": slot0, "n": names, "h": apart}
-        for w in ORDER.split():
-            step[w[0]](int(w[1]))
-        for _ in rest:
-            pass
-    for k in range(8):
-        act(T.Yp[:, 32 * k:32 * k + 32], T.Pn[:, :, k], PNK, ["Yp"], bias=2048.0)
-    dma("a", "sp", T.yp[:], T.Yp[:], ["Yp"], [])
-    dma("s", "sn", T.yn[:], T.N4[:], ["n%d%d" % (RO, h) for h in H], [])
-    for k in range(8):
-        act(T.Yc[:, 32 * k:32 * k + 32], T["C%d" % RO][:, :, k], ["C%d%d" % (RO, h) for h in H], ["Yc"], bias=2048.0)
-    dma("a", "sc", T.yc[:], T.Yc[:], ["Yc"], [])
+            call = o["fn"]()
+            if o["sig"][2]:
+                call.then_inc(T.sem[o["sig"][0]], 16)
+            o["at"] = o["sig"][:2]
+        total[o["at"][0]] = o["at"][1]
     for sem, n in total.items():
         need("p", sem, n)

from concourse.mybir import dt, AluOpType as A, ActivationFunctionType as F, AxisListType as AX

NP = 2
PB = 128 // NP
L = 512 // NP
NB = L // 16
K8 = 8 * NB
RO = 4
GC = 512
VB = 32
FOLD, FOLD0 = "ss", "--"
V1, EZ, MERGE = "p", "p", False
OPT = "1235"
MW = K8 + L
TURNS, DELTAS, PASSES, PLANS = (7.0, 8.0, 9.0, 10.0, 11.0, 12.0, 14.0), (0.15, 0.22, 0.3), 3, 3
CYC, PEC, VFIX, SFIX = 0.83e-3, 0.417e-3, 0.05, 0.065
CASES = ((1.2, 1.56, 3.8, 0.11, 1.6, 250.0, 5.0, 0.3, 0.8, 1.6), (1.0, 1.56, 3.8, 0.1, 1.5, 220.0, 5.0, 0.05, 0.8, 1.4), (1.0, 1.4, 3.8, 0.1, 1.5, 220.0, 4.0, 0.05, 0.8, 2.0),
         (1.0, 1.56, 3.8, 0.1, 1.5, 220.0, 2.5, 0.05, 0.8, 1.0), (1.4, 2.0, 3.0, 0.1, 1.5, 220.0, 3.5, 0.3, 0.8, 1.4), (1.25, 1.1, 2.0, 0.1, 1.5, 220.0, 2.5, 0.05, 0.8, 1.6),
         (1.4, 1.1, 5.5, 0.08, 1.5, 220.0, 4.0, 0.5, 0.8, 1.4), (1.1, 1.56, 3.8, 0.1, 2.0, 180.0, 8.0, 0.05, 1.5, 1.1), (1.2, 1.3, 3.8, 0.1, 1.5, 220.0, 3.0, 0.05, 0.8, 2.2))
BIG = 1024.0
MAGIC = 12582912.0
bf, f32, i32, u16 = "bfloat16", "float32", "int32", "uint16"
PIPE = {
    "X": ([4096], bf), "xg": ([8 * L], bf), "yg": ([8 * L], bf), "mx": ([8 * L], bf), "lr": ([8 * L], bf), "xy": ([16 * L], bf), "xm": ([16 * L], bf),
    "es": ([L * 9], bf), "E": ([L * 9], bf), "V": ([L // VB, 9 * VB], bf), "v1": ([L], bf), "v2c": ([L], bf),
    "wcol": ([8], f32), "Zw": ([144], bf),
    "Pn": ([NB, 8], f32), "Nn": ([NB, 8], f32), "rp": ([K8], f32), "hs": ([K8], i32), "hi": ([K8], i32), "hp": ([K8], f32),
    "dr": ([NB, 7], f32), "tm": ([3, K8 + 8], f32), "fr": ([3, K8], f32),
    "poff": ([K8], u16), "coff": ([K8], u16), "hoff": ([K8], u16), "ok2": ([K8, 2], bf),
    "s1": ([NB, 8], bf), "t1": ([K8], bf), "t2": ([K8], i32), "t3": ([K8 + 8], i32), "Ti": ([2 * NB], i32),
    "LH": ([NB, 2, 16], bf), "v2": ([L], bf), "v3": ([L], bf), "g1": ([L], bf), "g2": ([L], bf), "g3": ([L], bf),
    "val": ([L], bf), "vf": ([L], f32), "N4": ([L], bf), "ne": ([NB], bf), "o2f": ([NB], f32),
    "q2": ([K8], f32), "Q3": ([2 * K8], f32), "d3": ([K8], f32), "pre": ([NB], f32), "kw": ([NB, 8], f32), "kx": ([NB, 8], f32), "q1": ([K8], f32),
    "si": ([NB], i32), "sj": ([NB], i32), "sk": ([NB], f32), "junk": ([NB], f32),
    "oa": ([NB], u16), "ob": ([NB], u16), "oo": ([2 * NB], u16), "eo": ([NB], u16), "po": ([NB], u16),
    "C": ([(RO + 1) * MW], f32), "Fin": ([RO * MW], f32), "MN": ([RO * 2 * L], bf), "ms": ([RO * L], bf),
    "Yk": ([16, NB], f32), "Yo": ([512], f32),
}
SCALED = (("In", -1.0, bf), ("Ih", 0.5, bf), ("IL", -1.0 * L, bf), ("I2", -2.0, bf), ("IK", 4096.0, bf), ("IKn", -4096.0, bf), ("Jp", 1.0, f32), ("Jn", -1.0, f32))
SCRATCH = {n: ("sbuf", [128, NP * s[0]] + s[1:], d) for n, (s, d) in PIPE.items()}
SCRATCH.update({n: ("sbuf", [128, 128], d) for n, c, d in SCALED})
SCRATCH.update({
    "cM": ("sbuf", [128, 2 * GC], bf), "cR": ("sbuf", [128, 1152], bf), "cC": ("sbuf", [128, 9 * VB], bf), "th9": ("sbuf", [128, K8], bf),
    "pin": ("sbuf", [128, 256], i32), "cin": ("sbuf", [128, 256], i32), "pf": ("sbuf", [128, 8, 32], f32), "cf": ("sbuf", [128, 8, 32], f32),
    "nin": ("sbuf", [128, 512], bf), "win": ("sbuf", [128, 1], i32), "tin": ("sbuf", [128, 8], i32), "tbc": ("sbuf", [128, 8], i32), "G": ("sbuf", [128, 8], f32), "G0": ("sbuf", [128, 8], f32), "G4": ("sbuf", [128, 8], f32),
    "col": ("sbuf", [128, 16], f32), "coli": ("sbuf", [128, 8], i32), "wb": ("sbuf", [128, 2 * NP], bf), "cnt": ("sbuf", [128, 2 * NP], f32),
    "b16": ("sbuf", [128, NB], bf), "bL": ("sbuf", [128, NB], bf), "b144": ("sbuf", [128, NB], bf), "r9": ("sbuf", [128, NB], bf), "c9": ("sbuf", [128, NB], bf), "cK": ("sbuf", [128, K8], bf),
    "base": ("sbuf", [128, NB], f32), "lane8": ("sbuf", [128, NB], f32), "d2": ("sbuf", [128, K8], f32), "m8": ("sbuf", [128, K8], f32),
    "ones": ("sbuf", [128, 128], bf), "BO": ("sbuf", [128, 128], bf), "I": ("sbuf", [128, 128], bf),
    "Fm": ("sbuf", [128, 1024], bf), "Z": ("sbuf", [128, 144], bf), "Zh": ("sbuf", [128, 144], bf),
    "pD": ("psum", [128, 32, 16], f32), "pC": ("psum", [128, 64, 8], f32), "pV": ("psum", [128, 512], f32),
    "pN": ("psum", [128, 32, 16], f32), "pe0": ("psum", [128, 8, 8, 16], f32), "pX": ("psum", [128, 64, 8], f32), "pY": ("psum", [128, 32, 16], f32),
})
SEMAPHORES = ["v", "a", "t", "p", "sent"] + ["d%d" % i for i in range(64)] + ["r%s%d%d" % (k, t, h) for k in "cn" for t in range(RO) for h in range(NP)]


def sweep(ops, cost, wake, delta, pre, succ, rank, first):
    n = len(ops)
    todo = [len(p) for p in pre]
    est = list(first)
    start, end = [0.0] * n, [0.0] * n
    ready = {q: [] for q in "vatps"}
    free = {q: 0.0 for q in ready}
    for i, o in enumerate(ops):
        if not todo[i]:
            ready[o["q"]].append(i)
    user = {}

    def at(i):
        o = ops[i]
        return max([est[i]] + [user[b][1] + wake for b in o["banks"] if b in user and ops[user[b][0]]["q"] != o["q"]])
    for _ in range(n):
        can = {q: [(at(i), i) for i in ready[q]] for q in ready}
        q = min((q for q in can if can[q]), key=lambda q: max(free[q], min(can[q])[0]))
        t0 = max(free[q], min(can[q])[0])
        now = max((c for c in can[q] if c[0] <= t0), key=lambda c: (rank[c[1]], -c[1]))
        d = delta * min(1.0, cost[now[1]])
        e, i = max((c for c in can[q] if c[0] <= t0 + d), key=lambda c: (rank[c[1]], -c[1]))
        ready[q].remove(i)
        o = ops[i]
        start[i] = max(t0, e)
        end[i] = free[q] = start[i] + cost[i]
        for b in o["banks"]:
            user[b] = (i, free[q])
        for j in succ[i]:
            est[j] = max(est[j], free[q] + pre[j][i])
            todo[j] -= 1
            if not todo[j]:
                ready[ops[j]["q"]].append(j)
    return start, end


def price(ops, case):
    f, ga, sc, wake, dl, bw, rl, di, ri, tf = case
    rate = {"e": CYC * f, "g": CYC * f * ga, "s": CYC * f * sc, "t": PEC * tf}
    return [di if o["kind"] == "d" else ri if o["kind"] == "r" else o["fix"] * f + o["n"] * rate[o["kind"]] for o in ops], [dl + o["n"] / bw if o["kind"] == "d" else rl if o["kind"] == "r" else 0.0 for o in ops], wake


def handover(ops, out):
    user, more = {}, {}
    for i in out:
        for b in ops[i]["banks"]:
            if b in user and ops[user[b]]["q"] != ops[i]["q"]:
                more.setdefault(i, []).append(user[b])
            user[b] = i
    return more


def span(ops, out, more, cost, lat, wake):
    free, end = {}, {}
    for i in out:
        o = ops[i]
        t = max([free.get(o["q"], 0.0)] + [end[j] + lat[j] + wake for j, w in o["pre"].items() if w] + [end[j] + wake for j in more.get(i, [])])
        end[i] = free[o["q"]] = t + cost[i]
    return max(end[i] + lat[i] for i in out)


def order(ops):
    n = len(ops)
    prices = [price(ops, c) for c in CASES]
    found = []
    for cost, lat, wake in prices[:PLANS]:
        fwd = [{j: (lat[j] + wake if w else 0.0) for j, w in o["pre"].items()} for o in ops]
        back = [{} for _ in ops]
        for i in range(n):
            for j, d in fwd[i].items():
                back[j][i] = d
        left = [0.0] * n
        for i in range(n - 1, -1, -1):
            left[i] = cost[i] + max([left[j] + d for j, d in back[i].items()] + [lat[i]])
        for turn in TURNS:
            for delta in DELTAS:
                rank = [r - turn * o["lead"] for r, o in zip(left, ops)]
                for _ in range(PASSES):
                    start, end = sweep(ops, cost, wake, delta, fwd, back, rank, [0.0] * n)
                    out = sorted(range(n), key=lambda i: (start[i], i)); more = handover(ops, out)
                    found.append(([span(ops, out, more, *p) for p in prices], out, more))
                    rank = sweep(ops, cost, wake, delta, back, fwd, end, lat)[1]
    unit = [min(f[0][c] for f in found) for c in range(len(CASES))]
    return min(found, key=lambda f: sum((a / b) ** 8 for a, b in zip(f[0], unit)))[1:]


PLAN = []


def rank_program(g, core, T, topo):
    rank = T.rank_of(core)
    if rank is None:
        return
    N = len(T.cores)
    Q = {"v": g.vector, "a": g.scalar, "t": g.tensor, "p": g, "s": g.sync}
    V, S, PE = g.vector, g.scalar, g.tensor
    ops, lastw, readers, lastload, ndma, lead, sent = [], {}, {}, {}, [0, 0], [0.0], [0]

    def add(q, fix, n, fn, rd, wr, sig=None):
        i = len(ops); pre = {}

        def edge(j, wait):
            pre[j] = pre.get(j, False) or ops[j]["q"] != q or ops[j]["sig"] is not None or (wait and q != "t")
        for k in rd:
            for j in lastw.get(k, []):
                edge(j, True)
        for k in wr:
            for j in lastw.get(k, []):
                edge(j, True)
            for j in readers.get(k, []):
                edge(j, True)
        banks = sorted({k.split(":")[0] for k in list(rd) + list(wr) if k[0] == "@"})
        for k in rd:
            readers.setdefault(k, []).append(i)
        for k in wr:
            lastw[k] = [i]; readers[k] = []
        kind, n = n if isinstance(n, tuple) else ("e", n)
        ops.append({"q": q, "fix": fix, "kind": kind, "n": n, "fn": fn, "pre": pre, "sig": sig, "banks": banks, "lead": lead[0]})

    def vop(fn, n, rd, wr):
        add("v", VFIX, n, fn, rd, wr)

    def ts(o, i, s1, s2, o0, o1, n, rd, wr):
        vop((lambda: V.tensor_scalar(o, i, s1, None, o0)) if o1 is None else (lambda: V.tensor_scalar(o, i, s1, s2, o0, o1)), n, rd, wr)

    def tt(o, a, b, f, n, rd, wr):
        vop(lambda: V.tensor_tensor(o, a, b, f), n, rd, wr)

    def cp(o, i, n, rd, wr):
        vop(lambda: V.tensor_copy(o, i), n, rd, wr)

    def fill(o, c, n, wr):
        vop(lambda: V.memset(o, c), n, [], wr)

    def scan(o, a, b, init, o0, o1, n, rd, wr):
        vop(lambda: V.tensor_tensor_scan(o, a, b, init, o0, o1), n, rd, wr)

    def act(o, i, n, rd, wr, f=F.Identity, **k):
        add("a", SFIX, n, lambda: S.activation(o, i, f, **k), rd, wr)

    def pool(fn, n, rd, wr):
        add("p", 0.17, 2 * n, fn, rd, wr)

    def mm(calls, n, rd, wr):
        def fn():
            for a in calls[:-1]:
                PE.matmul(*a)
            return PE.matmul(*calls[-1])
        b = "group" + wr[0].split(":")[0]
        if any(a[3] for a in calls) and calls[-1][4]:
            rd = list(rd) + [b]
        else:
            wr = list(wr) + [b]
        add("t", 0.0, ("t", n), fn, rd, wr)

    def dma(q, out, in_, kb, rd, wr, inturn=False):
        sem = "d%d" % ndma[0]; ndma[0] += 1
        if inturn:
            ndma[1] += kb; kb = ndma[1]
        add(q, 0.05, ("d", kb), lambda: Q[q].dma_start(out, in_), rd, wr, (sem, 16, True))
        if inturn:
            if q in lastload:
                ops[-1]["pre"][lastload[q]] = False
            lastload[q] = len(ops) - 1

    def send(dst, src, sem, t, rd, wr):
        to = T.cores[(rank + 1 + t % 3) % N]; fr = T.cores[(rank - 1 - t % 3) % N]
        rid, pid, _ = topo.addr(to)
        add("p", 0.8, ("r", 0), lambda: g.remote_dma(dst, src, T.sem[sem], T.sem.sent, pid, rid, topo.mask(core, to)), rd, wr,
            (sem, len(topo.engines(fr, core)), False))
        sent[0] += len(topo.engines(core, to))

    def view(h):
        def b(name, *ix):
            w = PIPE[name][0][0]
            if not ix:
                return T[name][:, w * h:w * h + w]
            f = ix[0]
            if isinstance(f, slice):
                f = slice(w * h + (f.start or 0), w * h + (w if f.stop is None else f.stop), f.step)
            else:
                f = w * h + f
            return T[name][(slice(None), f) + ix[1:]]
        return b
    gat = lambda n: ("g", n)
    sl, al = slice, slice(None)
    each = lambda k, h: ["%s%d%d" % (k, h, s) for s in range(NP)]

    table = lambda h, s: dma("sa"[s % 2], T.X[PB * s:PB * s + PB, 4096 * h:4096 * h + 4096], T.lit[PB * h:PB * h + PB, :], 512, [], ["X%d%d" % (h, s)], True)
    dma("s", T.pin[:], T.pn[:], 128, [], ["pin"], True)
    dma("a", T.cin[:], T.cn[:], 128, [], ["cin"], True)
    for h in range(NP):
        for s in range(NP):
            table(h, s)
        if h == 0:
            dma("s", T.nin[:], T.neg[:], 128, [], ["nin"], True)
            dma("a", T.tin[0:1, :], T.th[:], 1, [], ["tin"], True)
            dma("s", T.win[:], T.wt[:], 1, [], ["win"], True)
    fill(T.ones[:], 1.0, 64, ["ones"])
    fill(T.G0[:], 1.0, 8, ["G0"])
    fill(T.Fm[:], -512.0, 512, ["Fm"])
    pool(lambda: g.iota(T.coli[:, 0:1], [[0, 1]], 0, 1), 1, [], ["coli"])
    pool(lambda: g.iota(T.b16[:], [[16, NB]], 0, 0, allow_small_or_imprecise_dtypes=True), NB, [], ["b16"])
    pool(lambda: g.affine_select(T.I[:], T.ones[:], [[-1, 128]], A.is_equal, 0.0, 0, 1), 128, ["ones"], ["I"])
    pool(lambda: g.affine_select(T.G[:], T.G0[:], [[-16, 8]], A.is_ge, 0.0, 0, 1), 8, ["G0"], ["G"])
    pool(lambda: g.affine_select(T.G[:], T.G[:], [[16, 8]], A.is_ge, 0.0, 15, -1), 8, ["G"], ["G"])
    pool(lambda: g.partition_broadcast(T.tbc[:], T.tin[0:1, :], 128), 16, ["tin"], ["tbc"])
    pool(lambda: g.affine_select(T.Fm[:], T.Fm[:], [[-2, 8], [-16, 8], [0, 16]], A.is_ge, 0.0, 0, 1), 1024, ["Fm"], ["Fm"])
    pool(lambda: g.affine_select(T.Fm[:], T.Fm[:], [[2, 8], [16, 8], [0, 16]], A.is_ge, 0.0, 1, -1), 1024, ["Fm"], ["Fm"])
    pool(lambda: g.affine_select(T.BO[:], T.ones[:], [[-16, 8], [0, 16]], A.is_ge, 0.0, 0, 1), 128, ["ones"], ["BO"])
    pool(lambda: g.affine_select(T.BO[:], T.BO[:], [[16, 8], [0, 16]], A.is_ge, 0.0, 15, -1), 128, ["BO"], ["BO"])
    for nm, c, _ in SCALED:
        act(T[nm][:], T.I[:], 128, ["I"], [nm], scale=c)
    for z, c in (("Z", 1.0), ("Zh", -0.5)):
        fill(T[z][:], 0.0, 72, [z])
        ts(T[z][:, 15:143:16], T.G[:], c, None, A.mult, None, 8, ["G", z], [z])
    fill(T.cM[:], BIG, GC, ["cM"])
    fill(T.cM[:, 0::2], -BIG, GC // 2, ["cM"])
    fill(T.cR[:], -BIG, 576, ["cR"])
    fill(T.cR[:, 0::9], BIG, 64, ["cR"])
    for k in range(9):
        fill(T.cC[:, k::9], 32.0 ** (k - 8), VB // 2, ["cC%d" % k])
    for k in range(8):
        fill(T.th9[:, k::8], -8.5 * 32.0 ** (k - 7), 8, ["th9%d" % k])
    CC, TH9 = ["cC%d" % k for k in range(9)], ["th9%d" % k for k in range(8)]
    ts(T.coli[:, 1:2], T.coli[:, 0:1], 1, None, A.bitwise_and, None, 1, ["coli"], ["c1"])
    ts(T.col[:, 6:7], T.coli[:, 1:2], -1.0, None, A.add, None, 1, ["c1"], ["par0"])
    ts(T.col[:, 7:8], T.coli[:, 1:2], -1.0, None, A.mult, None, 1, ["c1"], ["par1"])
    ts(T.coli[:, 2:3], T.coli[:, 0:1], 15, None, A.bitwise_and, None, 1, ["coli"], ["c2"])
    cp(T.col[:, 0:1], T.coli[:, 2:3], 1, ["c2"], ["r"])
    ts(T.coli[:, 3:4], T.coli[:, 0:1], 128 - PB, None, A.bitwise_and, None, 1, ["coli"], ["c3"])
    ts(T.col[:, 1:2], T.coli[:, 3:4], 1.0 * L / PB, T.col[:, 0:1], A.mult, A.add, 1, ["c3", "r"], ["rs"])
    ts(T.b144[:], T.b16[:], 9.0, None, A.mult, None, NB, ["b16"], ["b144"])
    ts(T.bL[:], T.b16[:], 1.0 * L, None, A.add, None, NB, ["b16"], ["bL"])
    ts(T.base[:], T.b16[:], T.col[:, 0:1], 9.0, A.add, A.mult, NB, ["b16", "r"], ["base"])
    ts(T.col[:, 2:3], T.col[:, 0:1], 9.0, None, A.mult, None, 1, ["r"], ["r9c"])
    ts(T.r9[:], T.b16[:], 0.0, T.col[:, 2:3], A.mult, A.add, NB, ["b16", "r9c"], ["r9"])
    ts(T.lane8[:], T.b16[:], T.col[:, 1:2], 8.0, A.add, A.mult, NB, ["b16", "rs"], ["lane8"])
    fill(T.c9[:], 9.0, NB, ["c9"])
    fill(T.cK[:], -2.5, K8 // 2, ["cK"])
    fill(T.d2[:], -100.0, K8, ["d2"])
    cp(T.d2[:, 0::8], T.base[:], NB, ["base", "d2"], ["d2"])
    fill(T.m8[:], 1.0, K8, ["m8"])
    fill(T.m8[:, 0::8], 0.0, NB, ["m8"])
    fill(T.d3[:], -100.0, K8 * NP, ["d3%d" % h for h in range(NP)])
    fill(T.t3[:, 7::K8 + 8], 1, NP, ["t30"])
    fill(T.tm[:, :, 0], 0.0, 3 * NP, ["tm0"])
    fill(T.pN[:, 0:NB, 15], 0.0, NB, ["@pN:t"])
    fill(T.Zw[:], 0.0, 144, ["Zw%d" % h for h in range(NP)])
    GN = 8 // NP
    tt(T.G4[:, 0:GN], T.G[:, 0:GN], T.G[:, GN:2 * GN], A.add, GN, ["G"], ["G4"])
    ts(T.pf[:], T.pin[:], -2048.0, None, A.add, None, 256, ["pin"], ["pf"])
    ts(T.cf[:], T.cin[:], -2048.0, None, A.add, None, 256, ["cin"], ["cf"])
    cp(T.wb[:, 0:1], T.win[:], 1, ["win"], ["wb"])
    for h in range(NP):
        B = view(h); s_ = str(h); rows = sl(PB * h, PB * h + PB); to = lambda s: sl(PB * s, PB * s + PB)
        for j, (src, nm, ky) in enumerate(((T.pf, "Pn", ["@pD:y"]), (T.cf, "C", ["@pD:z"]))):
            mm([(T.pD[to(s), 16 + 8 * j:24 + 8 * j], T.Jp[:, rows], src[:, :, NB * s:NB * s + NB], True, True) for s in range(NP)], 4 * K8 * NP, ["Jp", "pf", "cf"][0:2 + j:1 + j], ky)
            for k in range(8):
                act(B(nm, sl(k, K8, 8)) if j else B(nm, al, k), T.pD[:, 16 + 8 * j + k], NB, ky, ["%s%d%d" % (nm, h, k)])
            lastw[("Pn", "C0")[j] + s_] = [lastw.pop("%s%d%d" % (nm, h, k))[0] for k in range(8)]
        ts(B("poff"), B("Pn"), 2048.0, None, A.add, None, K8, ["Pn" + s_], ["poff" + s_])
        mm([(T.pV[to(s), 0:L], T.I[:, rows], T.nin[:, L * s:L * s + L], True, True) for s in range(NP)], L * NP, ["I", "nin"], ["@pV:v"])
        act(B("MN", sl(L, 2 * L)), T.pV[:, 0:L], L, ["@pV:v"], ["n0" + s_], scale=-1.0, bias=256.0)
        tt(T.G0[:, GN * h:GN * h + GN], T.tbc[:, GN * h:GN * h + GN], T.G4[:, 0:GN], A.mult, GN, ["tbc", "G4", "G0"], ["tg" + s_])
        vop(lambda h=h, B=B: V.tensor_reduce(B("wcol", sl(6, 7)), T.G0[:, GN * h:GN * h + GN], AX.X, A.add), GN, ["tg" + s_], ["tj" + s_])
        ts(B("wcol", sl(1, 2)), B("wcol", sl(6, 7)), 0.5, None, A.add, None, 1, ["tj" + s_], ["th" + s_])
        ts(B("wcol", sl(4, 5)), B("wcol", sl(1, 2)), 0.5, None, A.mult, None, 1, ["th" + s_], ["thr" + s_])
        mm([(T.pX[to(s), 2 * h + j, 0:1], T[m][:, rows], T.wb[:, 0:1], True, True) for j, m in enumerate(("I", "BO")) for s in range(NP)], 128 * NP, ["I", "BO", "wb"], ["@pX:w" + s_])
        ts(B("Zw", sl(15, 143, 16)), T.G[:], T.pX[:, 2 * h, 0:1], None, A.mult, None, 8, ["G", "@pX:w" + s_, "Zw" + s_], ["Zw" + s_])
        act(B("wcol", sl(3, 4)), T.pX[:, 1 + 2 * h, 0:1], 1, ["@pX:w" + s_], ["c0" + s_], scale=255.0)

    def head(t, h):
        B = view(h); s_ = str(h); XK = each("X", h); kC = "C%d%d" % (t, h); kn = "n%d%d" % (t, h)
        if MERGE and t:
            act(B("MN", sl(2 * L * t + L, 2 * L * t + 2 * L)), B("C", sl(MW * t + K8, MW * t + MW)), L, [kC], [kn])
        X = B("X"); C = B("C", sl(MW * t, MW * t + K8)); npr = lambda a, n: B("MN", sl(2 * L * t + L + a, 2 * L * t + L + a + n))
        pA, pB, kA = T.pY[:, 8 * h:8 * h + 8], T.pY[:, 16:24], "@pY:A" + s_; how = FOLD if t + h else FOLD0
        act(pA, B("Pn"), K8, ["Pn" + s_], [kA], bias=3232.0)
        act(B("rp"), B("Pn"), K8, ["Pn" + s_], ["rp" + s_], scale=2080.0, bias=-3801088.0)
        ts(B("coff"), C, 2048.0, None, A.add, None, K8, [kC], ["coff" + s_])
        tt(pA, pA, C, A.mult, K8, [kA, kC], [kA])
        tt(B("hs"), pA, B("rp"), A.add, K8, [kA, "rp" + s_], ["hs" + s_])
        ts(B("hi"), B("hs"), 5, 4095, A.arith_shift_right, A.bitwise_and, K8, ["hs" + s_], ["hi" + s_])
        cp(B("hoff"), B("hi"), K8, ["hi" + s_], ["hoff" + s_])
        if EZ == "a":
            act(B("es", sl(0, 9 * L, 9)), npr(0, L), L, [kn], ["ez" + s_])
        else:
            pool(lambda: g.affine_select(B("es", sl(0, 9 * L, 9)), npr(0, L), [[0, L]], A.is_ge, 0.0, 0, 0), L, [kn], ["ez" + s_])
        for c in range(L // 128):
            ks = lambda nm, a, n: ["%s%d%d" % (nm, h, u) for u in range(a // 256, (a + n) // 256)]
            e0 = 1024 * c
            for a in range(e0, e0 + 1024, GC):
                e = sl(a, a + GC); o = sl(a // 16, (a + GC) // 16)
                if how[c] == "s":
                    e2 = sl(2 * a, 2 * (a + GC)); odd = sl(2 * a + 1, 2 * (a + GC), 2)
                    act(B("xy", sl(2 * a, 2 * (a + GC), 2)), X.indirect(B("poff", o)), gat(GC), XK + ["poff" + s_], ks("x", a, GC))
                    act(B("xy", odd), X.indirect(B("coff", o)), gat(GC), XK + ["coff" + s_], ks("y", a, GC))
                    scan(B("xm", e2), T.cM[:], B("xy", e2), 0.0, A.min, A.max, GC, ["cM"] + ks("x", a, GC) + ks("y", a, GC), ks("m", a, GC))
                    tt(B("lr", e), X.indirect(B("hoff", o)), B("xm", odd), A.min, gat(GC), XK + ["hoff" + s_] + ks("m", a, GC), ks("l", a, GC))
                    continue
                act(B("xg", e), X.indirect(B("poff", o)), gat(GC), XK + ["poff" + s_], ks("x", a, GC))
                act(B("yg", e), X.indirect(B("coff", o)), gat(GC), XK + ["coff" + s_], ks("y", a, GC))
                tt(B("mx", e), X.indirect(B("coff", o)), B("xg", e), A.max, gat(GC), XK + ["coff" + s_] + ks("x", a, GC), ks("m", a, GC))
                tt(B("lr", e), X.indirect(B("hoff", o)), B("mx", e), A.min, gat(GC), XK + ["hoff" + s_] + ks("m", a, GC), ks("l", a, GC))
            if how[c] == "s":
                row = lambda src, r: B("xm" if src == "mx" else "xy", sl(2 * (e0 + r) + (src != "xg"), 2 * (e0 + 1024), 32))
            else:
                row = lambda src, r: B(src, sl(e0 + r, e0 + 1024, 16))
            pD = T.pD[:, 8 * h + 4 * c:8 * h + 4 * c + 4]; kD = "@pD:%d%d" % (h, c)
            part = lambda z, src, first, last: [(pD, T[z][:, 15 - r:143 - r], row(src, r), first and r == 0, last and r == 15) for r in range(16)]
            mm(part("Zh", "xg", True, False), 1024, ["Zh"] + ks("x", e0, 1024) + ks("y", e0, 1024), [kD])
            mm(part("Zh", "yg", False, False), 1024, ["Zh"] + ks("y", e0, 1024), [kD])
            mm(part("Z", "mx", False, True), 1024, ["Z"] + ks("m", e0, 1024), [kD])
            for u in range(2):
                act(B("ok2", sl(64 * c, 64 * c + 64), u), pD, 64, [kD, "thr" + s_, "par%d" % u], ["ok%d%d%d" % (h, c, u)], F.Sign, scale=T.col[:, 6 + u:7 + u], bias=B("wcol", sl(4, 5)))
            pe = T.pe0; kb = ["@pe0%d" % u for u in range(2)]; sc = "%d%d" % (h, c)
            for u in range(2):
                bk = sl(4 * u, 4 * u + 4); b0 = 8 * c + 4 * u; l0 = 16 * b0
                mm([(pe[:, bk, k, :], T.I[:], npr(l0, 64), k == 0, False) for k in range(8)], 512, ["I", kn], [kb[u]])
                mm([(pe[:, bk, :, 2 * r:2 * r + 2], T.Fm[:, 128 * r:128 * r + 128], B("ok2", sl(8 * b0, 8 * b0 + 32)), False, False) for r in range(8)], 512, ["Fm", "ok%s0" % sc, "ok%s1" % sc], [kb[u]])
                mm([(pe[:, bk], T.I[:], B("lr", sl(8 * l0, 8 * l0 + 512)), False, True)], 512, ks("l", 8 * l0, 512), [kb[u]])
            for k in range(8):
                act(B("es", sl(1152 * c + 1 + k, 1152 * c + 1152, 9)), pe[:, :, k, :], 128, kb, ["es%s%d" % (sc, k)], bias=769.0)
            ln = sl(1152 * c, 1152 * c + 1152)
            scan(B("E", ln), T.cR[:], B("es", ln), 0.0, A.max, A.min, 576, ["cR", "ez" + s_] + ["es%s%d" % (sc, k) for k in range(8)], ["E" + sc])
            for b in range(128 * c // VB, (128 * c + 128) // VB):
                scan(B("V", b), B("E", sl(9 * VB * b, 9 * VB * (b + 1))), T.cC[:], 1.0, A.max, A.min, 4.5 * VB, CC + ["E" + sc], ["V%d%d" % (h, b)])
        if V1 == "a":
            act(B("v1"), B("V", al, sl(6, 9 * VB, 9)), L, ["V%d%d" % (h, b) for b in range(L // VB)], ["v1" + s_])
        else:
            pool(lambda: g.affine_select(B("v1"), B("V", al, sl(6, 9 * VB, 9)), [[0, L]], A.is_ge, 0.0, 0, 0), L, ["V%d%d" % (h, b) for b in range(L // VB)], ["v1" + s_])
        OK = ["ok%d%d%d" % (h, c, u) for c in range(L // 128) for u in range(2)]
        pO = T.pY[:, 24:32]
        if "2" in OPT:
            act(pB, B("Pn"), K8, ["Pn" + s_], ["@pY:B"], bias=2048.0)
            tt(B("hp"), B("hi"), pB, A.subtract, K8, ["hi" + s_, "@pY:B"], ["hp" + s_])
            mm([(pO, T.Ih[:], B("ok2", al, u), u == 0, u == 1) for u in range(2)], 2 * K8, OK + ["Ih"], ["@pY:o"])
            tt(pO, pO, B("hp"), A.mult, K8, ["@pY:o", "hp" + s_], ["@pY:o"])
            tt(B("Nn"), B("Pn"), pO, A.add, K8, ["@pY:o", "Pn" + s_], ["Nn" + s_])
            return
        mm([(pO, T.IK[:], B("ok2", al, u), u == 0, False) for u in range(2)] + [(pO, T.IK[:], T.cK[:], False, True)], 3 * K8, OK + ["IK", "cK"], ["@pY:o"])
        mm([(pB, T.Jp[:], B("Pn"), True, False)] + [(pB, T.IKn[:], B("ok2", al, u), False, u == 1) for u in range(2)], 6 * K8, OK + ["IKn", "Jp", "Pn" + s_], ["@pY:B"])
        tt(B("hp"), B("hi"), pO, A.add, K8, ["@pY:o", "hi" + s_], ["hp" + s_])
        tt(B("Nn"), B("hp"), pB, A.max, K8, ["@pY:B", "hp" + s_], ["Nn" + s_])

    def tail(t, h):
        B = view(h); s_ = str(h); XK = each("X", h); kC = "C%d%d" % (t, h); kn = "n%d%d" % (t, h); last = t == RO - 1
        k_ = lambda *n: [x + s_ for x in n]
        ES = ["es%d%d%d" % (h, c, k) for c in range(L // 128) for k in range(8)] + ["ez" + s_]
        EK, VK = ["E%d%d" % (h, c) for c in range(L // 128)], ["V%d%d" % (h, b) for b in range(L // VB)]
        C = B("C", sl(MW * t, MW * t + K8)); Fin = B("Fin", sl(MW * t, MW * t + K8)); npr = B("MN", sl(2 * L * t + L, 2 * L * t + 2 * L))
        pC, pN = T.pC, T.pN
        nb = sl(0, NB)
        pX = T.pX; pP = pX[:, 8 + 2 * h:10 + 2 * h]
        pQ, pS, pF, pF0, pG = pC[:, 16 + 2 * h:18 + 2 * h], pX[:, 24:26], pN[:, 16:24], pN[:, 16:24, 0::8], pN[:, 24:32]
        if "3" in OPT:
            act(pX[:, 32:48, 0:7], B("Nn", al, sl(0, 7)), 7 * NB, k_("Nn"), ["@pX:d"])
            tt(B("dr"), pX[:, 32:48, 0:7], B("Nn", al, sl(1, 8)), A.subtract, 7 * NB, ["@pX:d"] + k_("Nn"), k_("dr"))
        else:
            mm([(pX[:, 32:48, 0:7], T.Jp[:], B("Nn", al, sl(0, 7)), True, False), (pX[:, 32:48, 0:7], T.Jn[:], B("Nn", al, sl(1, 8)), False, True)], 8 * 112, ["Jp", "Jn"] + k_("Nn"), ["@pX:d"])
            act(B("dr"), pX[:, 32:48, 0:7], 7 * NB, ["@pX:d"], k_("dr"))
        if "4" not in OPT:
            mm([(pP, B("Zw", sl(15 - r, 143 - r)), B("MN", sl(2 * L * t + L + r, 2 * L * t + 2 * L, 16)), r == 0, r == 15) for r in range(16)], 1024, k_("Zw") + [kn], k_("@pX:p"))
            act(B("pre"), pP, NB, k_("@pX:p", "c0"), k_("pre"), scale=-1.0, bias=B("wcol", sl(3, 4)))
        m = VB // 16
        mm([(pC[:, nb], T.I[:], T.th9[:], True, False)] +
           [(pC[:, u:NB:m], T.Z[:, 15 - r:143 - r], B("V", al, sl(144 * u + 9 * r + 1, 144 * u + 9 * r + 9)), False, r == 15 and u == m - 1) for u in range(m) for r in range(16)],
           K8 + 16 * m * max(64, K8 // m), ["Z"] + TH9 + VK, ["@pC:c"])
        act(B("s1"), pC[:, nb], K8, ["@pC:c"], k_("s1"), F.Sign)
        S1 = k_("s1")
        mm([(pQ, T.I[:], T.b144[:], True, False), (pQ, T.I[:], T.r9[:], False, False), (pQ, T.Ih[:], T.c9[:], False, False)] +
           [(pQ, T.Ih[:], B("s1", al, k), False, k == 6) for k in range(7)], 640, S1 + ["b144", "r9", "c9"], k_("@pC:q"))
        cp(B("oa"), pQ, NB, k_("@pC:q"), k_("oa"))
        tt(B("v2"), B("es").indirect(B("oa")), B("v1"), A.min, gat(L), ES + k_("oa", "v1"), k_("v2"))
        act(B("ne"), B("s1", al, 7), NB, S1, k_("ne"), scale=-0.5, bias=0.5)
        act(B("t1"), B("s1"), K8, S1, k_("t1"), F.Relu)
        mm([(pX[:, 48:64, j], T.I[:], B("ne"), True, True) for j in range(7)], 7 * 64, k_("ne"), ["@pX:m"])
        mm([(pX[:, 26:28], T.ones[:], B("ne"), True, True),
            (pX[:, 28:30], T.I[:], T.bL[:], True, False), (pX[:, 28:30], T.IL[:], B("ne"), False, True),
            (pX[:, 30:32], T.I[:], T.b144[:], True, False), (pX[:, 30:32], T.I[:], T.r9[:], False, False), (pX[:, 30:32], T.I2[:], B("ne"), False, True)],
           6 * 64, k_("ne") + ["IL", "I2", "bL"], ["@pX:e"])
        tt(pN[:, nb, 8:15], pX[:, 48:64, 0:7], B("dr"), A.mult, 7 * NB, ["@pX:m"] + k_("dr"), ["@pN:t"])
        ts(B("eo"), pX[:, 28:30], T.col[:, 0:1], None, A.add, None, NB, ["@pX:e", "r"], k_("eo"))
        act(B("d3", sl(1, K8, 8)), pX[:, 30:32], NB, ["@pX:e"] + k_("d3"), k_("d3"), bias=2.0)
        if not last:
            act(B("junk"), pX[:, 26:28], NB, ["@pX:e"], k_("cnt"), scale=-1.0, bias=128.0, accum_out=T.cnt[:, h:h + 1])

        def turn(n, tk, keys):
            tm, fr = "tm%d" % n, "fr%d" % n; front = B("fr", n - 1, sl(7, K8, 8))
            tt(B("tm", n - 1, sl(1, K8 + 1)), tk, pN[:, nb, 9 - n:17 - n], A.mult, K8, keys + ["@pN:t"], k_(tm))
            scan(B("fr", n - 1), T.m8[:], B("tm", n - 1, sl(1, K8 + 1)), 0.0, A.mult, A.subtract, K8, ["m8"] + k_(tm), k_(fr))
            if n < 3:
                act(pN[:, nb, 8 - n], front, NB, k_(fr), ["@pN:t"])
            if n == 1:
                mm([(pF, T.Jp[:], B("Nn"), True, False)], 4 * K8, k_("Nn", tm), ["@pN:f"])
            if "5" in OPT and n < 3:
                act(B("tm", n - 1, sl(0, K8, 8)), front, NB, k_(fr, tm), k_(tm))
            mm([(pF, T.Jp[:], B("tm", n - 1, sl(0, K8)), False, False)], 4 * K8, k_(tm) + ["tm0"], ["@pN:f"])
            if "5" not in OPT or n == 3:
                mm([(pF0, T.Jp[:], front, False, n == 3)], 256, k_(fr), ["@pN:f"])

        def count(n, v, out):
            u = 32.0 ** (-7 - n)
            ts(B("LH", al, 0), B(v), u, u * 2.0 ** 20, A.max, A.min, L // 2, k_(v), k_("LHa"))
            act(B("LH", al, 1), B(v), L, k_(v), k_("LHb"), F.Relu, scale=2.0 ** -20)
            w = pC[:, 20:24]
            mm([(w, T.Z[:, 15 - r:143 - r], B("LH", al, al, r), r == 0, r == 15) for r in range(16)], 1024, k_("LHa", "LHb"), ["@pC:n"])
            ts(B("Ti"), w, 1.0 / u / 31, 7 * 33825 - 8.0 / 31, A.mult, A.add, 2 * NB, ["@pC:n"], k_("Ti"))
            for j in range(4):
                ts(out(j), B("Ti"), 4 + 5 * j, 1, A.logical_shift_right, A.bitwise_and, 2 * NB, k_("Ti"), k_("t%d%d" % (n, j)))
            return k_(*["t%d%d" % (n, j) for j in range(4)])

        turn(1, B("t1"), k_("t1"))
        ts(B("v2c"), B("v2"), 32.0 ** -9, None, A.max, None, L // 2, k_("v2"), k_("v2c"))
        T2 = count(2, "v2", lambda j: B("t2", sl(j, K8, 4)))
        scan(B("q2"), T.d2[:], B("t2"), -8.0, A.max, A.add, K8, ["d2"] + T2, k_("q2"))
        cp(B("ob"), B("q2", sl(7, K8, 8)), NB, k_("q2"), k_("ob"))
        tt(B("v3"), B("es").indirect(B("ob")), B("v2c"), A.min, gat(L), ES + k_("ob", "v2c"), k_("v3"))
        act(B("g1"), B("es").indirect(B("ob")), gat(L), ES + k_("ob"), k_("g1"))
        turn(2, B("t2"), T2)
        T3 = count(3, "v3", lambda j: B("t3", sl(8 + j, K8 + 8, 4)))
        t3, t30 = B("t3", sl(8, K8 + 8)), B("t3", sl(8, K8 + 8, 8))
        scan(B("Q3", sl(0, K8)), B("d3"), t3, -8.0, A.max, A.add, K8, k_("d3") + T3, k_("q3"))
        tt(B("o2f"), pQ, t30, A.mult, NB, k_("@pC:q") + T3[:1], k_("o2f"))
        tt(B("Q3", sl(K8 + 6, 2 * K8, 8)), B("o2f"), T.base[:], A.max, 2 * NB, k_("o2f") + ["base"], k_("o2g"))
        cp(B("oo"), B("Q3", sl(6, 2 * K8, 8)), 2 * NB, k_("q3", "o2g"), k_("oo"))
        turn(3, t3, T3)
        tt(t30, t30, B("t2", sl(0, K8, 8)), A.mult, 2 * NB, T3[:1] + T2[:1], T3[:1])
        act(Fin, pF, K8, ["@pN:f"], k_("Fin%d" % t))
        if not MERGE:
            send(B("C", sl(MW * t + MW, MW * t + MW + K8)), Fin, "rc%d%d" % (t, h), t, k_("Fin%d" % t), ["C%d%d" % (t + 1, h)])
        tt(B("g2"), B("E").indirect(B("oo", nb)), B("g1"), A.min, gat(L), EK + k_("oo", "g1"), k_("g2"))
        tt(B("g3"), B("es").indirect(B("oo", sl(NB, 2 * NB))), B("g2"), A.min, gat(L), ES + k_("oo", "g2"), k_("g3"))
        pv, pm = T.pV[:, 0:L], T.pV[:, L:2 * L]
        if "4" in OPT:
            pm = T.pC[:, 32:64]
            mm([(pm, T.I[:], npr, True, False), (pm, T.In[:], B("g3"), False, True)], 2 * L, [kn] + k_("g3"), ["@pC:m"])
            act(B("MN", sl(2 * L * t, 2 * L * t + L)), pm, L, ["@pC:m"], k_("Mp"), bias=1.0)
            mm([(pS, B("Zw", sl(15 - r, 143 - r)), B("MN", sl(2 * L * t + r, 2 * L * t + L, 16)), r == 0, r == 15) for r in range(16)], 1024, k_("Zw", "Mp"), ["@pX:s"])
        else:
            mm([(pS, B("Zw", sl(15 - r, 143 - r)), B("g3", sl(r, L, 16)), r == 0, r == 15) for r in range(16)], 1024, k_("Zw", "g3"), ["@pX:s"])
        mm([(pv, T.In[:], npr, True, False)], L, ["In", kn], ["@pV:v"])
        mm([(pv, T.Ih[:], B("g3"), False, True)], L, ["Ih"] + k_("g3"), ["@pV:v"])
        act(B("vf"), pv, L, ["@pV:v"], k_("vf"), scale=1.0 - 2.0 ** -10, bias=MAGIC + 255.0)
        if "4" not in OPT:
            mm([(pm, T.I[:], npr, True, False), (pm, T.In[:], B("g3"), False, True)], 2 * L, [kn] + k_("g3"), ["@pV:m"])
            act(B("MN", sl(2 * L * t, 2 * L * t + L)), pm, L, ["@pV:m"], k_("Mp"), bias=1.0)
        act(B("val"), B("vf"), L, k_("vf"), k_("val"), bias=-MAGIC)
        ms = B("ms", sl(L * t, L * t + L)); mw = B("MN", sl(2 * L * t, 2 * L * t + 2 * L)).indirect(B("eo"))
        if MERGE:
            act(B("Fin", sl(MW * t + K8, MW * t + MW)), mw, gat(L), k_("Mp", "eo") + [kn], k_("ms%d" % t))
            send(B("C", sl(MW * t + MW, MW * t + 2 * MW)), B("Fin", sl(MW * t, MW * t + MW)), "rc%d%d" % (t, h), t, k_("Fin%d" % t, "ms%d" % t), ["C%d%d" % (t + 1, h)])
        else:
            act(ms, mw, gat(L), k_("Mp", "eo") + [kn], k_("ms%d" % t), **({"scale": -1.0, "bias": 256.0} if last else {}))
            send(B("N4") if last else B("MN", sl(2 * L * t + 3 * L, 2 * L * t + 4 * L)), ms, "rn%d%d" % (t, h), t, k_("ms%d" % t), ["n%d%d" % (t + 1, h)])
        if "4" in OPT:
            ts(B("si"), pS, -1.0, 262144.0, A.mult, A.add, NB, ["@pX:s"], k_("si"))
        else:
            tt(B("si"), pS, B("pre"), A.add, NB, ["@pX:s"] + k_("pre"), k_("si"))
        ts(B("sj"), B("si"), 7, None, A.bitwise_and, None, NB, k_("si"), k_("sj"))
        tt(B("sk"), B("sj"), T.lane8[:], A.add, 2 * NB, k_("sj") + ["lane8"], k_("sk"))
        cp(B("po"), B("sk"), NB, k_("sk"), k_("po"))
        cp(B("X").indirect(B("po")), B("val"), ("s", L), k_("po", "val"), XK + k_("Xw"))
        W = 4096 // NP
        if last:
            for s in range(NP):
                dma("sa"[s * h], T.yx[PB * h:PB * h + PB, W * s:W * s + W], T.X[PB * s:PB * s + PB, 4096 * h + W * s:4096 * h + W * s + W], 512, k_("Xw"), [])
        else:
            for s in range(NP):
                cols = sl(4096 * h + W * s, 4096 * h + W * s + W); s2 = 1 - s
                dma("s", T.X[PB * s2:PB * s2 + PB, cols], T.X[PB * s:PB * s + PB, cols], 512, k_("Xw"), [XK[s2]])
        if "1" in OPT:
            tt(pG, pF, C, A.subtract, K8, ["@pN:f", kC], ["@pN:g"])
            tt(pG, pG, B("t3", sl(7, K8 + 7)), A.mult, K8, ["@pN:g", "t30"] + T3, ["@pN:g"])
            tt(B("Pn"), pG, C, A.add, K8, ["@pN:g", kC], k_("Pn"))
            act(B("Pn", al, 0), B("Fin", sl(MW * t, MW * t + K8, 8)), NB, k_("Fin%d" % t, "Pn"), k_("Pn"))
            if not last:
                ts(B("poff"), B("Pn"), 2048.0, None, A.add, None, K8, k_("Pn"), k_("poff"))
            return
        if "7" in OPT:
            tt(B("kx"), pF, C, A.subtract, K8, ["@pN:f", kC], k_("kx"))
            tt(B("kw"), B("kx"), B("t3", sl(7, K8 + 7)), A.mult, 2 * K8, ["t30"] + k_("kx") + T3, k_("kw"))
            act(B("kw", al, 0), B("kx", al, 0), NB, k_("kw", "kx"), k_("kw"))
        else:
            mm([(pG, T.Jp[:], Fin, True, False), (pG, T.Jn[:], C, False, True)], 8 * K8, k_("Fin%d" % t) + [kC], ["@pN:g"])
            tt(B("kw"), pG, B("t3", sl(7, K8 + 7)), A.mult, K8, ["@pN:g", "t30"] + T3, k_("kw"))
            act(B("kw", al, 0), pN[:, 24:32, 0::8], NB, ["@pN:g"] + k_("kw"), k_("kw"))
        mm([(pG, T.Jp[:], B("kw"), True, False), (pG, T.Jp[:], C, False, True)], 8 * K8, k_("kw") + [kC], ["@pN:g"])
        if not last:
            ts(B("poff"), pG, 2048.0, None, A.add, None, K8, ["@pN:g"], k_("poff"))
        act(B("Pn"), pG, K8, ["@pN:g"], k_("Pn"))

    def limit():
        ts(T.coli[:, 4:5], T.cnt[:, 0:1], T.cnt[:, 1:2], None, A.add, None, 1, ["cnt0", "cnt1"], ["ai"])
        ts(T.coli[:, 5:6], T.coli[:, 4:5], 63, None, A.bitwise_and, None, 1, ["ai"], ["aj"])
        for h in range(NP):
            B = view(h)
            ts(B("wcol", sl(4, 5)), T.coli[:, 5:6], B("wcol", sl(1, 2)), 0.5, A.add, A.mult, 1, ["aj", "th%d" % h], ["thr%d" % h])

    def names_out(h, j, src, key, out):
        B = view(h); s_ = "%d%d" % (h, j); ky = ["@pD:y", "@pD:z"] if j else ["@pD:00", "@pD:01", "@pD:10", "@pD:11"]
        for k in range(8):
            act(B("Yk", 8 * j + k), src(k), NB, [key], ["Yk%s%d" % (s_, k)], bias=2048.0)
        mm([(T.pD[0:PB, 16 * j + s:16 * j + 16:2, :], T.Jp[:, PB * s:PB * s + PB], B("Yk", sl(8 * j, 8 * j + 8)), True, True) for s in range(NP)],
           4 * 128 * NP, ["Yk%s%d" % (s_, k) for k in range(8)], ky)
        o = T.Yo[0:PB, 512 * h + 256 * j:512 * h + 256 * j + 256]
        act(o, T.pD[0:PB, 16 * j:16 * j + 16, :], 256, ky, ["Yo" + s_])
        dma("sa"[j * h], out[PB * h:PB * h + PB, :], o, 64, ["Yo" + s_], [])

    for t in range(RO):
        for part in (head, tail):
            for h in range(NP):
                lead[0] = NP * t + h
                part(t, h)
        if t < RO - 1:
            limit()
    for h in range(NP):
        B = view(h)
        names_out(h, 0, lambda k: B("Pn", al, k), "Pn%d" % h, T.yp)
        names_out(h, 1, lambda k: B("C", sl(MW * RO + k, MW * RO + K8, 8)), "C%d%d" % (RO, h), T.yc)
        if MERGE:
            act(B("N4"), B("C", sl(MW * RO + K8, MW * RO + MW)), L, ["C%d%d" % (RO, h)], ["n%d%d" % (RO, h)], scale=-1.0, bias=256.0)
        for s in range(NP):
            dma("sa"[s * h], T.yn[PB * h:PB * h + PB, L * s:L * s + L], T.N4[PB * s:PB * s + PB, L * h:L * h + L], 32, ["n%d%d" % (RO, h)], [])

    cnt = {q: 0 for q in "vatp"}
    seen = {q: {} for q in Q}
    total = {"sent": sent[0]}

    def need(q, sem, n):
        if seen[q].get(sem, 0) < n:
            Q[q].wait_ge(T.sem[sem], n)
            seen[q][sem] = n
    if not PLAN:
        PLAN.extend(order(ops))
    for i in PLAN[0]:
        o = ops[i]; q = o["q"]; want = {}
        o["pre"].update({j: True for j in PLAN[1].get(i, [])})
        for j, w in o["pre"].items():
            if w:
                s, n = ops[j]["at"]
                want[s] = max(want.get(s, 0), n)
        for s, n in want.items():
            need(q, s, n)
        if o["sig"] is None:
            calls = o["fn"]()
            for call in calls if isinstance(calls, list) else [calls]:
                cnt[q] += 1
                call.then_inc(T.sem[q], 1)
            o["at"] = (q, cnt[q])
        else:
            call = o["fn"]()
            if o["sig"][2]:
                call.then_inc(T.sem[o["sig"][0]], 16)
            o["at"] = o["sig"][:2]
        total[o["at"][0]] = o["at"][1]
    for sem, n in total.items():
        need("p", sem, n)
